import numpy as np
import ml_dtypes


def mxq(x, axis, fmt="e4m3"):
    dtype, down = {"e4m3": (ml_dtypes.float8_e4m3fn, 7), "e5m2": (ml_dtypes.float8_e5m2, 14)}[fmt]
    v = np.moveaxis(np.asarray(x, np.float32).astype(ml_dtypes.bfloat16).astype(np.float64), axis, -1)
    blocks = v.reshape(v.shape[:-1] + (-1, 32))
    amax = np.abs(blocks).max(-1, keepdims=True)
    byte = np.maximum(np.where(amax > 0, np.frexp(amax)[1] - 1 + 127, 0) - down, 1)
    scale = np.exp2(byte - 127.0)
    codes = (blocks / scale).astype(np.float32).astype(dtype).astype(np.float64)
    return np.moveaxis((codes * scale).reshape(v.shape), -1, axis)


WIDE = False


def mx_kscale(k):
    if not WIDE:
        return np.ones(k)
    levels = np.array([24, -24, 12, -12, 0])
    if k % 512:
        return np.exp2(np.random.permutation(np.resize(levels, k // 32))).repeat(32)
    a = np.empty((k // 512, 16))
    for p in range(k // 512):
        a[p, :8] = np.random.permutation(np.resize(levels, 8))
        for g in range(8):
            far = levels[np.abs(levels - a[p, g]) >= 10]
            a[p, g + 8] = far[np.random.randint(len(far))]
    return np.exp2(a.ravel()).repeat(32)


def f64(x):
    return np.asarray(x).astype(np.float64)


def striped(idx):
    return np.tile(idx.reshape(-1, 16).T, (8, 1)).astype(np.uint16)


def unstriped(offs):
    return offs[:16].T.reshape(-1).astype(np.int64)


E2M1 = np.array([0.0, 0.5, 1.0, 1.5, 2.0, 3.0, 4.0, 6.0, -0.0, -0.5, -1.0, -1.5, -2.0, -3.0, -4.0, -6.0])


def pack_weight(w, fmt):
    k, n = w.shape
    w = f64(np.asarray(w, np.float32).astype(ml_dtypes.bfloat16)).reshape(k // 32, 32, n)
    amax = np.abs(w).max(1)
    if fmt == "e4m3":
        byte = np.frexp(amax)[1] - 1 + 127 - 7
    else:
        mant, ex = np.frexp(amax / 6.0)
        byte = np.where(mant > 0.5, ex, ex - 1) + 127
    byte = np.clip(np.where(amax > 0, byte, 1), 1, 254)
    scaled = (w * np.exp2(127.0 - byte)[:, None, :]).reshape(k, n).astype(np.float32)
    by_word = np.ascontiguousarray(scaled.reshape(k // 512, 128, 4, n).transpose(0, 1, 3, 2))
    if fmt == "e4m3":
        words = by_word.astype(ml_dtypes.float8_e4m3fn).view(np.uint8)
    else:
        c = by_word.astype(ml_dtypes.float4_e2m1fn).view(np.uint8) & 0xF
        words = (c[..., 0::2] | (c[..., 1::2] << 4)).reshape(k // 512, 128, 2 * n)
    return np.ascontiguousarray(words), np.ascontiguousarray(byte.astype(np.uint8).reshape(k // 512, 16, n))


def unpack_weight(words, scales, fmt):
    g, _, n = scales.shape
    words = np.ascontiguousarray(words).reshape(g, 128, n, -1)
    if fmt == "e4m3":
        vals = words.view(ml_dtypes.float8_e4m3fn).astype(np.float64)
    else:
        nib = np.empty((g, 128, n, 4), np.uint8)
        nib[..., 0::2] = words & 0xF
        nib[..., 1::2] = words >> 4
        vals = E2M1[nib]
    vals = vals * np.repeat(np.exp2(scales.astype(np.float64) - 127.0), 8, axis=1)[..., None]
    return vals.transpose(0, 1, 3, 2).reshape(g * 512, n)


def pack_table4(v):
    words, scales = pack_weight(v, "e2m1")
    g, t = words.shape[0] // 2, v.shape[1]
    return np.ascontiguousarray(words.reshape(g, 2, 128, t, 2).transpose(0, 2, 3, 1, 4).reshape(g, 128, t, 4)), scales


def unpack_table4(words, scales):
    g, _, t, _ = words.shape
    return unpack_weight(words.reshape(g, 128, t, 2, 2).transpose(0, 3, 1, 2, 4).reshape(2 * g, 128, 2 * t), scales, "e2m1")


K, R, N, T, J = 1024, 1024, 512, 2048, 1024


def setup_inputs():
    n = np.random.standard_normal
    s = mx_kscale(K)[:, None]
    u = mx_kscale(R)[:, None]
    p_tab = pack_table4(n((K, T)) * s)
    p_ws = pack_weight(n((K, R)) / np.sqrt(2 * K) / s * u.T, "e2m1")
    p_wt = pack_weight(n((K, R)) / np.sqrt(2 * K) / s * u.T, "e4m3")
    return {
        "tab_words": p_tab[0],
        "tab_scales": p_tab[1],
        "ws_words": p_ws[0],
        "ws_scales": p_ws[1],
        "wt_words": p_wt[0],
        "wt_scales": p_wt[1],
        "wd": (n((R, N)) / np.sqrt(R) / u).astype(np.float32),
        "b": (0.3 * n(N)).astype(np.float32),
        "wgo": np.tile(np.random.uniform(0.5, 2.0, J), (128, 1)).astype(np.float32),
        "offs": striped(np.random.permutation(T)[:J]),
        "offs2": striped(np.random.permutation(T)[:J]),
    }


def reference(tab_words, tab_scales, ws_words, ws_scales, wt_words, wt_scales, wd, b, wgo, offs, offs2):
    idx = unstriped(offs)
    idx2 = unstriped(offs2)
    tab_ = unpack_table4(tab_words, tab_scales)[:, idx]
    tabb_ = unpack_table4(tab_words, tab_scales)[:, idx2]
    ws_ = unpack_weight(ws_words, ws_scales, "e2m1")
    wt_ = unpack_weight(wt_words, wt_scales, "e4m3")
    a = ws_.T @ tab_ + wt_.T @ tabb_
    h = np.maximum(a, 0.0)
    h_ = mxq(h, 0, "e4m3")
    wd_ = mxq(f64(wd), 0, "e4m3")
    y = wd_.T @ h_
    out = np.zeros((N, T))
    out[:, idx2] = f64(wgo)[0] * (y + f64(b)[:, None])
    return out

@@ -1,0 +1,229 @@
+from contextlib import ExitStack
+
+import concourse.mybir as mybir
+from concourse.masks import make_identity
+
+K, R, N, T, J = 1024, 1024, 512, 2048, 1024
+FLOPS = 2 * 2 * K * R * J + 2 * R * N * J
+
+F32 = mybir.dt.float32
+BF16 = mybir.dt.bfloat16
+I32 = mybir.dt.int32
+U32 = mybir.dt.uint32
+U16 = mybir.dt.uint16
+U8 = mybir.dt.uint8
+FP8X4 = mybir.dt.float8_e4m3fn_x4
+FP4X4 = mybir.dt.float4_e2m1fn_x4
+ACT = mybir.ActivationFunctionType
+MULT = mybir.AluOpType.mult
+
+P = 128
+PASSES = 2
+BANK = 512
+CHUNK = 256
+HALF = 512
+N_TILES = N // P
+
+
+def tile_list_msg_relu_bias_kernel(
+    tc, tab_words, tab_scales, ws_words, ws_scales, wt_words, wt_scales, wd, b, wgo, offs, offs2, out
+):
+    nc = tc.nc
+    with ExitStack() as ctx:
+        keep = ctx.enter_context(tc.tile_pool(name="keep", bufs=1))
+        ring = ctx.enter_context(tc.tile_pool(name="ring", bufs=2))
+        single = ctx.enter_context(tc.psum_pool(name="single", bufs=1))
+        psum = ctx.enter_context(tc.psum_pool(name="psum", bufs=2))
+
+        lists = [keep.tile([P, J // 16], U16, name=f"list{i}") for i in range(2)]
+        tab_s = keep.tile([P, T], U8, name="tab_s", align_bytes=64)
+        tab_w = keep.tile([P, T], U32, name="tab_w", align_bytes=64)
+        w_s = keep.tile([P, 2, PASSES, R], U8, name="w_s", align_bytes=64)
+        ws_w = keep.tile([P, PASSES, 2 * R], U8, name="ws_w", align_bytes=64)
+        wt_w = [keep.tile([P, 4 * R], U8, name=f"wt_w{a}", align_bytes=64) for a in range(PASSES)]
+        wd_codes = keep.tile([P, PASSES, N], U32, name="wd_codes", align_bytes=64)
+        wd_scales = keep.tile([P, PASSES, N], U8, name="wd_scales", align_bytes=64)
+        bias = keep.tile([P, N_TILES], F32, name="bias")
+        ident = keep.tile([P, P], F32, name="ident")
+        pages = [keep.tile([P, T], F32, name=f"page{c}") for c in range(N_TILES)]
+
+        for q in range(4):
+            nc.vector.memset(tab_s[32 * q : 32 * q + 24, :].bitcast(I32), 0)
+
+        nc.sync.dma_start(lists[0][:], offs)
+        nc.sync.dma_start(lists[1][:], offs2)
+        for q in range(4):
+            nc.sync.dma_start(
+                out=tab_s[32 * q + 24 : 32 * q + 32, :].bitcast(I32),
+                in_=tab_scales[:, 4 * q : 4 * q + 4, :].bitcast(I32),
+            )
+        nc.sync.dma_start(out=tab_w[:].bitcast(I32), in_=tab_words[0].rearrange("p t b -> p (t b)").bitcast(I32))
+        nc.sync.dma_start(out=ws_w[:].bitcast(I32), in_=ws_words.rearrange("a p c -> p a c").bitcast(I32))
+        for i, scales in enumerate((ws_scales, wt_scales)):
+            for q in range(4):
+                nc.sync.dma_start(
+                    out=w_s[32 * q : 32 * q + 4, i, :, :].bitcast(I32),
+                    in_=scales[:, 4 * q : 4 * q + 4, :].rearrange("a r c -> r a c").bitcast(I32),
+                )
+        for a in range(PASSES):
+            nc.sync.dma_start(out=wt_w[a][:].bitcast(I32), in_=wt_words[a].rearrange("p r i -> p (r i)").bitcast(I32))
+        with nc.allow_non_contiguous_dma(reason="one bias value a partition"):
+            nc.sync.dma_start(out=bias[:], in_=b.rearrange("(c p) -> p c", p=P))
+
+        make_identity(nc, ident[:])
+        for c in range(N_TILES):
+            for s in range(2):
+                nc.gpsimd.memset(pages[c][:, 1024 * s : 1024 * (s + 1)], 0.0)
+
+        def pick_scales(j0, width, queue):
+            cols = slice(j0 // 16, (j0 + width) // 16)
+            picked = keep.tile([P, 2, width], U8, name=f"picked_s{j0}", tag=f"stage{j0}", align_bytes=64)
+            for l in range(2):
+                nc.vector.tensor_copy(picked[:, l, :], tab_s[:].indirect(lists[l][:, cols]))
+            planes = []
+            for a in range(PASSES):
+                plane = keep.tile([P, 2, width], U8, name=f"plane{a}_{j0}", align_bytes=64)
+                queue.dma_start(
+                    out=plane[0:100].rearrange("p l j -> p (l j)").bitcast(I32),
+                    in_=picked[24 + 4 * a : 124 + 4 * a].rearrange("p l j -> p (l j)").bitcast(I32),
+                )
+                planes.append(plane)
+            return planes
+
+        def pick_words(j0, width):
+            cols = slice(j0 // 16, (j0 + width) // 16)
+            both = keep.tile([P, 2, width], U32, name=f"both{j0}", tag=f"pairs{j0}", align_bytes=64)
+            for l in range(2):
+                nc.vector.tensor_copy(both[:, l, :], tab_w[:].indirect(lists[l][:, cols]))
+            parted = keep.tile([P, 2, PASSES, 2 * width], U8, name=f"parted{j0}", align_bytes=64)
+            nc.vector.tensor_copy(
+                out=parted[:].bitcast(U16),
+                in_=both[:].bitcast(U16).rearrange("p l (j d) -> p l d j", d=2),
+            )
+            return parted
+
+        def quantise_wd(g):
+            raw = keep.tile([P, 4, N], F32, name=f"wd_raw{g}", tag=f"stage{g * CHUNK}", align_bytes=64)
+            nc.sync.dma_start(out=raw[:], in_=wd[512 * g : 512 * (g + 1), :].rearrange("(p i) n -> p i n", i=4))
+            grouped = ring.tile([P, N, 4], BF16, name="wd_grouped", align_bytes=64)
+            nc.scalar.copy(out=grouped[:], in_=raw[:].rearrange("p i n -> p n i"))
+            nc.vector.quantize_mx(
+                out=wd_codes[:, g, :].bitcast(FP8X4),
+                scales=wd_scales[:, g, :],
+                in_=grouped[:].rearrange("p n i -> p (n i)"),
+            )
+
+        def first_product(parted, planes, p0):
+            banks = [psum.tile([P, BANK], F32, name=f"acc{g}") for g in range(PASSES)]
+            order = [(l, a) for a in range(PASSES) for l in range(2)]
+            for n, (l, a) in enumerate(order):
+                for g in range(PASSES):
+                    if l == 0:
+                        rhs = ws_w[:, a, 2 * BANK * g : 2 * BANK * (g + 1)].bitcast(FP4X4)
+                    else:
+                        rhs = wt_w[a][:, 4 * BANK * g : 4 * BANK * (g + 1)].bitcast(FP8X4)
+                    nc.tensor.matmul_mx(
+                        out=banks[g][:],
+                        lhsT=parted[:, l, a, 2 * p0 : 2 * (p0 + P)].bitcast(FP4X4),
+                        lhsT_scale=planes[a][:, l, p0 : p0 + P],
+                        rhs=rhs,
+                        rhs_scale=w_s[:, l, a, BANK * g : BANK * (g + 1)],
+                        start=(n == 0),
+                        stop=(n == len(order) - 1),
+                    )
+            rows = ring.tile([P, PASSES, 2, P, 2], BF16, name="h_rows")
+            for g in range(PASSES):
+                nc.scalar.activation(
+                    out=rows[:, g], in_=banks[g][:].rearrange("p (m u e) -> p u m e", u=2, e=2), func=ACT.Relu
+                )
+            return rows
+
+        def turn(rows, grouped, c0, tag):
+            words = rows[:].rearrange("p g u m e -> p (g u m e)").bitcast(F32)
+            turned = single.tile([P, PASSES, 2, P], F32, name=tag)
+            for g in range(PASSES):
+                for u in range(2):
+                    w0 = (2 * g + u) * P
+                    nc.tensor.transpose(turned[:, g, u, :], words[:, w0 : w0 + P], ident[:])
+            nc.scalar.copy(
+                out=grouped[:].bitcast(F32)[:, :, c0 : c0 + P, :],
+                in_=turned[:].rearrange("p g u j -> p g j u"),
+            )
+
+        def hidden(parted, planes, p0, j0):
+            grouped = ring.tile([P, PASSES, CHUNK, 4], BF16, name="h_grouped", align_bytes=64)
+            rows = [first_product(parted, planes, p0 + s * P) for s in range(CHUNK // P)]
+            for s in range(CHUNK // P):
+                turn(rows[s], grouped, s * P, ("early", "late")[s])
+            codes = keep.tile([P, PASSES, CHUNK], U32, name=f"h_codes{j0}", align_bytes=64)
+            scales = keep.tile([P, PASSES, CHUNK], U8, name=f"h_scales{j0}", align_bytes=64)
+            nc.vector.quantize_mx(
+                out=codes[:].rearrange("p g j -> p (g j)").bitcast(FP8X4),
+                scales=scales[:].rearrange("p g j -> p (g j)"),
+                in_=grouped[:].rearrange("p g j i -> p (g j i)"),
+            )
+            return codes, scales
+
+        def message(c, j0, chunks, acc=None):
+            width = CHUNK * len(chunks)
+            if acc is None:
+                bank = psum.tile([P, width], F32, name="y")
+                acc = bank[:]
+            for s, (codes, scales) in enumerate(chunks):
+                for g in range(PASSES):
+                    nc.tensor.matmul_mx(
+                        out=acc[:, s * CHUNK : (s + 1) * CHUNK],
+                        lhsT=wd_codes[:, g, c * P : (c + 1) * P].bitcast(FP8X4),
+                        lhsT_scale=wd_scales[:, g, c * P : (c + 1) * P],
+                        rhs=codes[:, g, :].bitcast(FP8X4),
+                        rhs_scale=scales[:, g, :],
+                        start=(g == 0),
+                        stop=(g == PASSES - 1),
+                    )
+            biased = keep.tile([P, width], F32, name=f"biased{c}_{j0}")
+            nc.scalar.activation(out=biased[:], in_=acc, func=ACT.Identity, bias=bias[:, c : c + 1], scale=1.0)
+            nc.vector.tensor_tensor(
+                pages[c][:].indirect(lists[1][:, j0 // 16 : (j0 + width) // 16]),
+                biased[:],
+                weight[:, j0 : j0 + width],
+                MULT,
+            )
+
+        def held(tiles, j0, h):
+            bank = single.tile([P, 2, CHUNK], F32, name="late")
+            for i, c in enumerate(tiles):
+                message(c, j0, [h], bank[:, i, :])
+
+        def store(c):
+            nc.sync.dma_start(out=out[c * P : (c + 1) * P, :], in_=pages[c][:])
+
+        scales_a = pick_scales(0, CHUNK, nc.scalar)
+        scales_b = pick_scales(CHUNK, CHUNK, nc.scalar)
+        words_a = pick_words(0, CHUNK)
+        words_b = pick_words(CHUNK, CHUNK)
+        scales_cd = pick_scales(HALF, HALF, nc.sync)
+        words_cd = pick_words(HALF, HALF)
+        for g in range(PASSES):
+            quantise_wd(g)
+
+        weight = keep.tile([P, J], F32, name="weight", tag="pairs0", align_bytes=64)
+        nc.sync.dma_start(out=weight[:], in_=wgo)
+
+        h_a = hidden(words_a, scales_a, 0, 0)
+        message(0, 0, [h_a])
+        message(1, 0, [h_a])
+        h_b = hidden(words_b, scales_b, 0, CHUNK)
+        held((2, 3), 0, h_a)
+        message(0, CHUNK, [h_b])
+        message(1, CHUNK, [h_b])
+        h_c = hidden(words_cd, scales_cd, 0, HALF)
+        held((2, 3), CHUNK, h_b)
+        message(0, HALF, [h_c])
+        message(1, HALF, [h_c])
+        h_d = hidden(words_cd, scales_cd, CHUNK, HALF + CHUNK)
+        held((2,), HALF, h_c)
+        for c in range(3):
+            message(c, HALF + CHUNK, [h_d])
+            store(c)
+        message(3, HALF, [h_c, h_d])
+        store(3)

@@ -22,6 +22,7 @@ PASSES = 2
 BANK = 512
 CHUNK = 256
 HALF = 512
+WD_COLS = 256
 N_TILES = N // P
 
 
@@ -41,43 +42,50 @@ def tile_list_msg_relu_bias_kernel(
         w_s = keep.tile([P, 2, PASSES, R], U8, name="w_s", align_bytes=64)
         ws_w = keep.tile([P, PASSES, 2 * R], U8, name="ws_w", align_bytes=64)
         wt_w = [keep.tile([P, 4 * R], U8, name=f"wt_w{a}", align_bytes=64) for a in range(PASSES)]
-        wd_codes = keep.tile([P, PASSES, N], U32, name="wd_codes", align_bytes=64)
-        wd_scales = keep.tile([P, PASSES, N], U8, name="wd_scales", align_bytes=64)
-        bias = keep.tile([P, N_TILES], F32, name="bias")
+        wd_codes = [keep.tile([P, PASSES, WD_COLS], U32, name=f"wd_codes{h}", align_bytes=64) for h in range(2)]
+        wd_scales = [keep.tile([P, PASSES, WD_COLS], U8, name=f"wd_scales{h}", align_bytes=64) for h in range(2)]
         ident = keep.tile([P, P], F32, name="ident")
-        pages = [keep.tile([P, T], F32, name=f"page{c}") for c in range(N_TILES)]
+        pages = [keep.tile([P, T], F32, name=f"page{c}") for c in range(2)]
 
         for q in range(4):
             nc.vector.memset(tab_s[32 * q : 32 * q + 24, :].bitcast(I32), 0)
 
-        nc.sync.dma_start(lists[0][:], offs)
-        nc.sync.dma_start(lists[1][:], offs2)
         for q in range(4):
             nc.sync.dma_start(
                 out=tab_s[32 * q + 24 : 32 * q + 32, :].bitcast(I32),
                 in_=tab_scales[:, 4 * q : 4 * q + 4, :].bitcast(I32),
             )
+        nc.sync.dma_start(lists[0][:], offs)
+        nc.sync.dma_start(lists[1][:], offs2)
         nc.sync.dma_start(out=tab_w[:].bitcast(I32), in_=tab_words[0].rearrange("p t b -> p (t b)").bitcast(I32))
         nc.sync.dma_start(out=ws_w[:].bitcast(I32), in_=ws_words.rearrange("a p c -> p a c").bitcast(I32))
-        for i, scales in enumerate((ws_scales, wt_scales)):
-            for q in range(4):
+
+        def load_scales(i, scales, quadrants):
+            for q in quadrants:
                 nc.sync.dma_start(
                     out=w_s[32 * q : 32 * q + 4, i, :, :].bitcast(I32),
                     in_=scales[:, 4 * q : 4 * q + 4, :].rearrange("a r c -> r a c").bitcast(I32),
                 )
-        for a in range(PASSES):
+
+        def load_wt(a):
             nc.sync.dma_start(out=wt_w[a][:].bitcast(I32), in_=wt_words[a].rearrange("p r i -> p (r i)").bitcast(I32))
+
+        load_scales(0, ws_scales, range(4))
+        load_scales(1, wt_scales, range(2))
+        load_wt(0)
+        load_scales(1, wt_scales, range(2, 4))
+        load_wt(1)
+        bias = keep.tile([P, N_TILES], F32, name="bias")
         with nc.allow_non_contiguous_dma(reason="one bias value a partition"):
             nc.sync.dma_start(out=bias[:], in_=b.rearrange("(c p) -> p c", p=P))
 
         make_identity(nc, ident[:])
-        for c in range(N_TILES):
-            for s in range(2):
-                nc.gpsimd.memset(pages[c][:, 1024 * s : 1024 * (s + 1)], 0.0)
+        for page in pages:
+            nc.vector.memset(page[:], 0.0)
 
-        def pick_scales(j0, width, queue):
+        def pick_scales(j0, width, queue, tag):
             cols = slice(j0 // 16, (j0 + width) // 16)
-            picked = keep.tile([P, 2, width], U8, name=f"picked_s{j0}", tag=f"stage{j0}", align_bytes=64)
+            picked = keep.tile([P, 2, width], U8, name=f"picked_s{j0}", tag=tag, align_bytes=64)
             for l in range(2):
                 nc.vector.tensor_copy(picked[:, l, :], tab_s[:].indirect(lists[l][:, cols]))
             planes = []
@@ -90,26 +98,34 @@ def tile_list_msg_relu_bias_kernel(
                 planes.append(plane)
             return planes
 
-        def pick_words(j0, width):
+        def pick_words(j0, width, tags):
             cols = slice(j0 // 16, (j0 + width) // 16)
-            both = keep.tile([P, 2, width], U32, name=f"both{j0}", tag=f"pairs{j0}", align_bytes=64)
+            share = 2 // len(tags)
+            tiles = [keep.tile([P, share, width], U32, name=f"both{j0}_{tag}", tag=tag, align_bytes=64) for tag in tags]
             for l in range(2):
-                nc.vector.tensor_copy(both[:, l, :], tab_w[:].indirect(lists[l][:, cols]))
+                nc.vector.tensor_copy(tiles[l // share][:, l % share, :], tab_w[:].indirect(lists[l][:, cols]))
             parted = keep.tile([P, 2, PASSES, 2 * width], U8, name=f"parted{j0}", align_bytes=64)
-            nc.vector.tensor_copy(
-                out=parted[:].bitcast(U16),
-                in_=both[:].bitcast(U16).rearrange("p l (j d) -> p l d j", d=2),
-            )
+            for i, both in enumerate(tiles):
+                nc.vector.tensor_copy(
+                    out=parted[:, i * share : (i + 1) * share].bitcast(U16),
+                    in_=both[:].bitcast(U16).rearrange("p l (j d) -> p l d j", d=2),
+                )
             return parted
 
-        def quantise_wd(g):
-            raw = keep.tile([P, 4, N], F32, name=f"wd_raw{g}", tag=f"stage{g * CHUNK}", align_bytes=64)
-            nc.sync.dma_start(out=raw[:], in_=wd[512 * g : 512 * (g + 1), :].rearrange("(p i) n -> p i n", i=4))
-            grouped = ring.tile([P, N, 4], BF16, name="wd_grouped", align_bytes=64)
+        def load_wd(g, h, tag):
+            raw = keep.tile([P, 4, WD_COLS], F32, name=f"wd_raw{g}{h}", tag=tag, align_bytes=64)
+            nc.sync.dma_start(
+                out=raw[:],
+                in_=wd[512 * g : 512 * (g + 1), WD_COLS * h : WD_COLS * (h + 1)].rearrange("(p i) n -> p i n", i=4),
+            )
+            return raw
+
+        def quantise_wd(raw, g, h):
+            grouped = ring.tile([P, WD_COLS, 4], BF16, name="wd_grouped", align_bytes=64)
             nc.scalar.copy(out=grouped[:], in_=raw[:].rearrange("p i n -> p n i"))
             nc.vector.quantize_mx(
-                out=wd_codes[:, g, :].bitcast(FP8X4),
-                scales=wd_scales[:, g, :],
+                out=wd_codes[h][:, g, :].bitcast(FP8X4),
+                scales=wd_scales[h][:, g, :],
                 in_=grouped[:].rearrange("p n i -> p (n i)"),
             )
 
@@ -151,7 +167,7 @@ def tile_list_msg_relu_bias_kernel(
             )
 
         def hidden(parted, planes, p0, j0):
-            grouped = ring.tile([P, PASSES, CHUNK, 4], BF16, name="h_grouped", align_bytes=64)
+            grouped = keep.tile([P, PASSES, CHUNK, 4], BF16, name=f"h_grouped{j0}", tag=f"grouped{j0}", align_bytes=64)
             rows = [first_product(parted, planes, p0 + s * P) for s in range(CHUNK // P)]
             for s in range(CHUNK // P):
                 turn(rows[s], grouped, s * P, ("early", "late")[s])
@@ -173,14 +189,14 @@ def tile_list_msg_relu_bias_kernel(
                 for g in range(PASSES):
                     nc.tensor.matmul_mx(
                         out=acc[:, s * CHUNK : (s + 1) * CHUNK],
-                        lhsT=wd_codes[:, g, c * P : (c + 1) * P].bitcast(FP8X4),
-                        lhsT_scale=wd_scales[:, g, c * P : (c + 1) * P],
+                        lhsT=wd_codes[c // 2][:, g, c % 2 * P : (c % 2 + 1) * P].bitcast(FP8X4),
+                        lhsT_scale=wd_scales[c // 2][:, g, c % 2 * P : (c % 2 + 1) * P],
                         rhs=codes[:, g, :].bitcast(FP8X4),
                         rhs_scale=scales[:, g, :],
                         start=(g == 0),
                         stop=(g == PASSES - 1),
                     )
-            biased = keep.tile([P, width], F32, name=f"biased{c}_{j0}")
+            biased = keep.tile([P, width], F32, name=f"biased{c}_{j0}", tag=f"biased{c}_{j0}")
             nc.scalar.activation(out=biased[:], in_=acc, func=ACT.Identity, bias=bias[:, c : c + 1], scale=1.0)
             nc.vector.tensor_tensor(
                 pages[c][:].indirect(lists[1][:, j0 // 16 : (j0 + width) // 16]),
@@ -197,21 +213,31 @@ def tile_list_msg_relu_bias_kernel(
         def store(c):
             nc.sync.dma_start(out=out[c * P : (c + 1) * P, :], in_=pages[c][:])
 
-        scales_a = pick_scales(0, CHUNK, nc.scalar)
-        scales_b = pick_scales(CHUNK, CHUNK, nc.scalar)
-        words_a = pick_words(0, CHUNK)
-        words_b = pick_words(CHUNK, CHUNK)
-        scales_cd = pick_scales(HALF, HALF, nc.sync)
-        words_cd = pick_words(HALF, HALF)
-        for g in range(PASSES):
-            quantise_wd(g)
-
-        weight = keep.tile([P, J], F32, name="weight", tag="pairs0", align_bytes=64)
+        wd_first = [load_wd(g, 0, f"wd{g}") for g in range(PASSES)]
+        scales_a = pick_scales(0, CHUNK, nc.scalar, "z")
+        words_a = pick_words(0, CHUNK, ("x", "w"))
+        scales_b = pick_scales(CHUNK, CHUNK, nc.scalar, "x")
+        words_b = pick_words(CHUNK, CHUNK, ("z",))
+        scales_cd = pick_scales(HALF, HALF, nc.sync, "z")
+        words_cd = pick_words(HALF, HALF, ("x",))
+        weight = keep.tile([P, J], F32, name="weight", tag="w", align_bytes=64)
         nc.sync.dma_start(out=weight[:], in_=wgo)
+        wd_second = [load_wd(g, 1, ("z", "x")[g]) for g in range(PASSES)]
+        for g in range(PASSES):
+            quantise_wd(wd_first[g], g, 0)
 
         h_a = hidden(words_a, scales_a, 0, 0)
+        page2 = keep.tile([P, T], F32, name="page2", tag="grouped0", align_bytes=64)
+        nc.vector.memset(page2[:], 0.0)
+        pages.append(page2)
         message(0, 0, [h_a])
+        page3 = keep.tile([P, T], F32, name="page3", tag="biased0_0")
+        for s in range(2):
+            nc.gpsimd.memset(page3[:, 1024 * s : 1024 * (s + 1)], 0.0)
+        pages.append(page3)
         message(1, 0, [h_a])
+        for g in range(PASSES):
+            quantise_wd(wd_second[g], g, 1)
         h_b = hidden(words_b, scales_b, 0, CHUNK)
         held((2, 3), 0, h_a)
         message(0, CHUNK, [h_b])

@@ -32,7 +32,8 @@ def tile_list_msg_relu_bias_kernel(
     nc = tc.nc
     with ExitStack() as ctx:
         keep = ctx.enter_context(tc.tile_pool(name="keep", bufs=1))
-        ring = ctx.enter_context(tc.tile_pool(name="ring", bufs=2))
+        stage = ctx.enter_context(tc.tile_pool(name="stage", bufs=1))
+        placed = ctx.enter_context(tc.tile_pool(name="placed", bufs=1))
         single = ctx.enter_context(tc.psum_pool(name="single", bufs=1))
         psum = ctx.enter_context(tc.psum_pool(name="psum", bufs=2))
 
@@ -45,7 +46,6 @@ def tile_list_msg_relu_bias_kernel(
         wd_codes = [keep.tile([P, PASSES, WD_COLS], U32, name=f"wd_codes{h}", align_bytes=64) for h in range(2)]
         wd_scales = [keep.tile([P, PASSES, WD_COLS], U8, name=f"wd_scales{h}", align_bytes=64) for h in range(2)]
         ident = keep.tile([P, P], F32, name="ident")
-        pages = [keep.tile([P, T], F32, name=f"page{c}") for c in range(2)]
 
         for q in range(4):
             nc.vector.memset(tab_s[32 * q : 32 * q + 24, :].bitcast(I32), 0)
@@ -75,17 +75,12 @@ def tile_list_msg_relu_bias_kernel(
         load_wt(0)
         load_scales(1, wt_scales, range(2, 4))
         load_wt(1)
-        bias = keep.tile([P, N_TILES], F32, name="bias")
-        with nc.allow_non_contiguous_dma(reason="one bias value a partition"):
-            nc.sync.dma_start(out=bias[:], in_=b.rearrange("(c p) -> p c", p=P))
 
         make_identity(nc, ident[:])
-        for page in pages:
-            nc.vector.memset(page[:], 0.0)
 
-        def pick_scales(j0, width, queue, tag):
+        def pick_scales(j0, width, queue, offset):
             cols = slice(j0 // 16, (j0 + width) // 16)
-            picked = keep.tile([P, 2, width], U8, name=f"picked_s{j0}", tag=tag, align_bytes=64)
+            picked = stage.tile([P, 2, width], U8, name=f"picked_s{j0}", offset=offset, align_bytes=64)
             for l in range(2):
                 nc.vector.tensor_copy(picked[:, l, :], tab_s[:].indirect(lists[l][:, cols]))
             planes = []
@@ -98,38 +93,37 @@ def tile_list_msg_relu_bias_kernel(
                 planes.append(plane)
             return planes
 
-        def pick_words(j0, width, tags):
+        def pick_words(j0, width, offset):
             cols = slice(j0 // 16, (j0 + width) // 16)
-            share = 2 // len(tags)
-            tiles = [keep.tile([P, share, width], U32, name=f"both{j0}_{tag}", tag=tag, align_bytes=64) for tag in tags]
+            both = stage.tile([P, 2, width], U32, name=f"both{j0}", offset=offset, align_bytes=64)
             for l in range(2):
-                nc.vector.tensor_copy(tiles[l // share][:, l % share, :], tab_w[:].indirect(lists[l][:, cols]))
+                nc.vector.tensor_copy(both[:, l, :], tab_w[:].indirect(lists[l][:, cols]))
             parted = keep.tile([P, 2, PASSES, 2 * width], U8, name=f"parted{j0}", align_bytes=64)
-            for i, both in enumerate(tiles):
-                nc.vector.tensor_copy(
-                    out=parted[:, i * share : (i + 1) * share].bitcast(U16),
-                    in_=both[:].bitcast(U16).rearrange("p l (j d) -> p l d j", d=2),
-                )
+            nc.vector.tensor_copy(
+                out=parted[:].bitcast(U16),
+                in_=both[:].bitcast(U16).rearrange("p l (j d) -> p l d j", d=2),
+            )
             return parted
 
-        def load_wd(g, h, tag):
-            raw = keep.tile([P, 4, WD_COLS], F32, name=f"wd_raw{g}{h}", tag=tag, align_bytes=64)
+        def load_wd(g, h):
+            raw = stage.tile([P, 4, WD_COLS], F32, name=f"wd_raw{g}{h}", offset=(512, 5632)[g], align_bytes=64)
             nc.sync.dma_start(
                 out=raw[:],
                 in_=wd[512 * g : 512 * (g + 1), WD_COLS * h : WD_COLS * (h + 1)].rearrange("(p i) n -> p i n", i=4),
             )
             return raw
 
-        def quantise_wd(raw, g, h):
-            grouped = ring.tile([P, WD_COLS, 4], BF16, name="wd_grouped", align_bytes=64)
-            nc.scalar.copy(out=grouped[:], in_=raw[:].rearrange("p i n -> p n i"))
+        def quantise_wd(raws, h, tag):
+            grouped = keep.tile([P, PASSES, WD_COLS, 4], BF16, name=f"wd_grouped{h}", tag=tag, align_bytes=64)
+            for g, raw in enumerate(raws):
+                nc.scalar.copy(out=grouped[:, g], in_=raw[:].rearrange("p i n -> p n i"))
             nc.vector.quantize_mx(
-                out=wd_codes[h][:, g, :].bitcast(FP8X4),
-                scales=wd_scales[h][:, g, :],
-                in_=grouped[:].rearrange("p n i -> p (n i)"),
+                out=wd_codes[h][:].rearrange("p g n -> p (g n)").bitcast(FP8X4),
+                scales=wd_scales[h][:].rearrange("p g n -> p (g n)"),
+                in_=grouped[:].rearrange("p g n i -> p (g n i)"),
             )
 
-        def first_product(parted, planes, p0):
+        def first_product(parted, planes, p0, j0):
             banks = [psum.tile([P, BANK], F32, name=f"acc{g}") for g in range(PASSES)]
             order = [(l, a) for a in range(PASSES) for l in range(2)]
             for n, (l, a) in enumerate(order):
@@ -147,7 +141,7 @@ def tile_list_msg_relu_bias_kernel(
                         start=(n == 0),
                         stop=(n == len(order) - 1),
                     )
-            rows = ring.tile([P, PASSES, 2, P, 2], BF16, name="h_rows")
+            rows = keep.tile([P, PASSES, 2, P, 2], BF16, name=f"rows{j0}", tag=f"rows{j0}", align_bytes=64)
             for g in range(PASSES):
                 nc.scalar.activation(
                     out=rows[:, g], in_=banks[g][:].rearrange("p (m u e) -> p u m e", u=2, e=2), func=ACT.Relu
@@ -167,8 +161,11 @@ def tile_list_msg_relu_bias_kernel(
             )
 
         def hidden(parted, planes, p0, j0):
-            grouped = keep.tile([P, PASSES, CHUNK, 4], BF16, name=f"h_grouped{j0}", tag=f"grouped{j0}", align_bytes=64)
-            rows = [first_product(parted, planes, p0 + s * P) for s in range(CHUNK // P)]
+            if j0 == 0:
+                grouped = placed.tile([P, PASSES, CHUNK, 4], BF16, name="h_grouped0", offset=6144, align_bytes=64)
+            else:
+                grouped = keep.tile([P, PASSES, CHUNK, 4], BF16, name=f"h_grouped{j0}", align_bytes=64)
+            rows = [first_product(parted, planes, p0 + s * P, j0 + s * P) for s in range(CHUNK // P)]
             for s in range(CHUNK // P):
                 turn(rows[s], grouped, s * P, ("early", "late")[s])
             codes = keep.tile([P, PASSES, CHUNK], U32, name=f"h_codes{j0}", align_bytes=64)
@@ -210,40 +207,48 @@ def tile_list_msg_relu_bias_kernel(
             for i, c in enumerate(tiles):
                 message(c, j0, [h], bank[:, i, :])
 
+        def clear(page):
+            for s in range(4):
+                nc.gpsimd.memset(page[:, 512 * s : 512 * (s + 1)], 0.0)
+            pages.append(page)
+
         def store(c):
             nc.sync.dma_start(out=out[c * P : (c + 1) * P, :], in_=pages[c][:])
 
-        wd_first = [load_wd(g, 0, f"wd{g}") for g in range(PASSES)]
-        scales_a = pick_scales(0, CHUNK, nc.scalar, "z")
-        words_a = pick_words(0, CHUNK, ("x", "w"))
-        scales_b = pick_scales(CHUNK, CHUNK, nc.scalar, "x")
-        words_b = pick_words(CHUNK, CHUNK, ("z",))
-        scales_cd = pick_scales(HALF, HALF, nc.sync, "z")
-        words_cd = pick_words(HALF, HALF, ("x",))
-        weight = keep.tile([P, J], F32, name="weight", tag="w", align_bytes=64)
+        scales_a = pick_scales(0, CHUNK, nc.scalar, 0)
+        scales_b = pick_scales(CHUNK, CHUNK, nc.scalar, 26624)
+        words_a = pick_words(0, CHUNK, 4096)
+        wd_first = [load_wd(g, 0) for g in range(PASSES)]
+        words_b = pick_words(CHUNK, CHUNK, 14336)
+        scales_cd = pick_scales(HALF, HALF, nc.sync, 4608)
+        weight = stage.tile([P, J], F32, name="weight", offset=10752, align_bytes=64)
         nc.sync.dma_start(out=weight[:], in_=wgo)
-        wd_second = [load_wd(g, 1, ("z", "x")[g]) for g in range(PASSES)]
-        for g in range(PASSES):
-            quantise_wd(wd_first[g], g, 0)
+        bias = stage.tile([P, N_TILES], F32, name="bias", offset=14848, align_bytes=64)
+        with nc.allow_non_contiguous_dma(reason="one bias value a partition"):
+            nc.sync.dma_start(out=bias[:], in_=b.rearrange("(c p) -> p c", p=P))
+        words_cd = pick_words(HALF, HALF, 15360)
+        page0 = keep.tile([P, T], F32, name="page0")
+        nc.vector.memset(page0[:].bitcast(I32), 0)
+        pages = [page0]
+        quantise_wd(wd_first, 0, "wd_grouped")
+        wd_second = [load_wd(g, 1) for g in range(PASSES)]
 
         h_a = hidden(words_a, scales_a, 0, 0)
-        page2 = keep.tile([P, T], F32, name="page2", tag="grouped0", align_bytes=64)
-        nc.vector.memset(page2[:], 0.0)
-        pages.append(page2)
+        for c in (1, 2):
+            page = placed.tile([P, T], F32, name=f"page{c}", offset=8192 * (c - 1))
+            clear(page)
         message(0, 0, [h_a])
         page3 = keep.tile([P, T], F32, name="page3", tag="biased0_0")
-        for s in range(2):
-            nc.gpsimd.memset(page3[:, 1024 * s : 1024 * (s + 1)], 0.0)
-        pages.append(page3)
+        clear(page3)
         message(1, 0, [h_a])
-        for g in range(PASSES):
-            quantise_wd(wd_second[g], g, 1)
+        quantise_wd(wd_second, 1, f"rows{P}")
+        message(2, 0, [h_a])
         h_b = hidden(words_b, scales_b, 0, CHUNK)
-        held((2, 3), 0, h_a)
-        message(0, CHUNK, [h_b])
-        message(1, CHUNK, [h_b])
+        held((3,), 0, h_a)
+        for c in range(3):
+            message(c, CHUNK, [h_b])
         h_c = hidden(words_cd, scales_cd, 0, HALF)
-        held((2, 3), CHUNK, h_b)
+        held((3,), CHUNK, h_b)
         message(0, HALF, [h_c])
         message(1, HALF, [h_c])
         h_d = hidden(words_cd, scales_cd, CHUNK, HALF + CHUNK)

@@ -18,12 +18,32 @@ ACT = mybir.ActivationFunctionType
 MULT = mybir.AluOpType.mult
 
 P = 128
+QUADRANTS = 4
+PASS_ROWS = 512
 PASSES = 2
+LISTS = 2
+PER_COLUMN = 16
 BANK = 512
 CHUNK = 256
-HALF = 512
 WD_COLS = 256
-N_TILES = N // P
+PAGES = N // P
+
+SCALE_ROW = 24
+MOVED_ROWS = 100
+
+OVERLAP = 512
+WD_RAW = 0
+PAIRS_A = WD_RAW + PASSES * 4 * WD_COLS * 4 - OVERLAP
+PICKED_B = PAIRS_A + OVERLAP
+PAIRS_B = PICKED_B + LISTS * CHUNK
+PICKED_CD = PAIRS_B
+BIAS = PICKED_CD + LISTS * 2 * CHUNK
+PAIRS_CD = BIAS + 64
+PAGE_1 = PAIRS_CD + LISTS * 2 * CHUNK * 4 - OVERLAP
+PICKED_A = PAGE_1 + 4 * T
+WD_GROUPED_0 = PICKED_A + 4 * J
+H_GROUPED_A = WD_GROUPED_0 + 4 * T
+H_ROWS_A1 = H_GROUPED_A + 4 * T
 
 
 def tile_list_msg_relu_bias_kernel(
@@ -33,228 +53,225 @@ def tile_list_msg_relu_bias_kernel(
     with ExitStack() as ctx:
         keep = ctx.enter_context(tc.tile_pool(name="keep", bufs=1))
         stage = ctx.enter_context(tc.tile_pool(name="stage", bufs=1))
-        placed = ctx.enter_context(tc.tile_pool(name="placed", bufs=1))
         single = ctx.enter_context(tc.psum_pool(name="single", bufs=1))
-        psum = ctx.enter_context(tc.psum_pool(name="psum", bufs=2))
+        double = ctx.enter_context(tc.psum_pool(name="double", bufs=2))
 
-        lists = [keep.tile([P, J // 16], U16, name=f"list{i}") for i in range(2)]
-        tab_s = keep.tile([P, T], U8, name="tab_s", align_bytes=64)
-        tab_w = keep.tile([P, T], U32, name="tab_w", align_bytes=64)
-        w_s = keep.tile([P, 2, PASSES, R], U8, name="w_s", align_bytes=64)
-        ws_w = keep.tile([P, PASSES, 2 * R], U8, name="ws_w", align_bytes=64)
-        wt_w = [keep.tile([P, 4 * R], U8, name=f"wt_w{a}", align_bytes=64) for a in range(PASSES)]
-        wd_codes = [keep.tile([P, PASSES, WD_COLS], U32, name=f"wd_codes{h}", align_bytes=64) for h in range(2)]
-        wd_scales = [keep.tile([P, PASSES, WD_COLS], U8, name=f"wd_scales{h}", align_bytes=64) for h in range(2)]
+        def sbuf(shape, dtype, name, offset=None):
+            if offset is None:
+                return keep.tile(shape, dtype, name=name, align_bytes=64)
+            return stage.tile(shape, dtype, name=name, offset=offset, align_bytes=64)
+
+        lists = [keep.tile([P, J // PER_COLUMN], U16, name=f"list{l}") for l in range(LISTS)]
+        tab_s = sbuf([P, T], U8, "tab_s")
+        tab_w = sbuf([P, T], U32, "tab_w")
+        w_s = sbuf([P, LISTS, PASSES, R], U8, "w_s")
+        ws_w = sbuf([P, PASSES, 2 * R], U8, "ws_w")
+        wt_w = [sbuf([P, 4 * R], U8, f"wt_w{a}") for a in range(PASSES)]
+        wd_codes = [sbuf([P, PASSES, WD_COLS], U32, f"wd_codes{half}") for half in range(N // WD_COLS)]
+        wd_scales = [sbuf([P, PASSES, WD_COLS], U8, f"wd_scales{half}") for half in range(N // WD_COLS)]
         ident = keep.tile([P, P], F32, name="ident")
 
-        for q in range(4):
-            nc.vector.memset(tab_s[32 * q : 32 * q + 24, :].bitcast(I32), 0)
+        for q in range(QUADRANTS):
+            nc.vector.memset(tab_s[32 * q : 32 * q + SCALE_ROW, :].bitcast(I32), 0)
 
-        for q in range(4):
-            nc.sync.dma_start(
-                out=tab_s[32 * q + 24 : 32 * q + 32, :].bitcast(I32),
-                in_=tab_scales[:, 4 * q : 4 * q + 4, :].bitcast(I32),
-            )
-        nc.sync.dma_start(lists[0][:], offs)
-        nc.sync.dma_start(lists[1][:], offs2)
-        nc.sync.dma_start(out=tab_w[:].bitcast(I32), in_=tab_words[0].rearrange("p t b -> p (t b)").bitcast(I32))
-        nc.sync.dma_start(out=ws_w[:].bitcast(I32), in_=ws_words.rearrange("a p c -> p a c").bitcast(I32))
-
-        def load_scales(i, scales, quadrants):
+        def load_w_scales(l, scales, quadrants):
             for q in quadrants:
                 nc.sync.dma_start(
-                    out=w_s[32 * q : 32 * q + 4, i, :, :].bitcast(I32),
-                    in_=scales[:, 4 * q : 4 * q + 4, :].rearrange("a r c -> r a c").bitcast(I32),
+                    out=w_s[32 * q : 32 * q + 4, l, :, :].bitcast(I32),
+                    in_=scales[:, 4 * q : 4 * q + 4, :].rearrange("a s r -> s a r").bitcast(I32),
                 )
 
         def load_wt(a):
             nc.sync.dma_start(out=wt_w[a][:].bitcast(I32), in_=wt_words[a].rearrange("p r i -> p (r i)").bitcast(I32))
 
-        load_scales(0, ws_scales, range(4))
-        load_scales(1, wt_scales, range(2))
+        for q in range(QUADRANTS):
+            nc.sync.dma_start(
+                out=tab_s[32 * q + SCALE_ROW : 32 * (q + 1), :].bitcast(I32),
+                in_=tab_scales[:, 4 * q : 4 * q + 4, :].bitcast(I32),
+            )
+        nc.sync.dma_start(lists[0][:], offs)
+        nc.sync.dma_start(lists[1][:], offs2)
+        load_w_scales(0, ws_scales, range(1))
+        nc.sync.dma_start(out=tab_w[:].bitcast(I32), in_=tab_words[0].rearrange("p t b -> p (t b)").bitcast(I32))
+        load_w_scales(0, ws_scales, range(1, QUADRANTS))
+        nc.sync.dma_start(out=ws_w[:].bitcast(I32), in_=ws_words.rearrange("a p c -> p a c").bitcast(I32))
+        load_w_scales(1, wt_scales, range(QUADRANTS - 1))
         load_wt(0)
-        load_scales(1, wt_scales, range(2, 4))
+        load_w_scales(1, wt_scales, range(QUADRANTS - 1, QUADRANTS))
         load_wt(1)
 
         make_identity(nc, ident[:])
 
+        def entries(l, j0, width):
+            return lists[l][:, j0 // PER_COLUMN : (j0 + width) // PER_COLUMN]
+
         def pick_scales(j0, width, queue, offset):
-            cols = slice(j0 // 16, (j0 + width) // 16)
-            picked = stage.tile([P, 2, width], U8, name=f"picked_s{j0}", offset=offset, align_bytes=64)
-            for l in range(2):
-                nc.vector.tensor_copy(picked[:, l, :], tab_s[:].indirect(lists[l][:, cols]))
+            picked = sbuf([P, LISTS, width], U8, f"picked{j0}", offset)
+            for l in range(LISTS):
+                nc.vector.tensor_copy(picked[:, l, :], tab_s[:].indirect(entries(l, j0, width)))
             planes = []
             for a in range(PASSES):
-                plane = keep.tile([P, 2, width], U8, name=f"plane{a}_{j0}", align_bytes=64)
+                plane = sbuf([P, LISTS, width], U8, f"plane{a}_{j0}")
+                first = SCALE_ROW + 4 * a
                 queue.dma_start(
-                    out=plane[0:100].rearrange("p l j -> p (l j)").bitcast(I32),
-                    in_=picked[24 + 4 * a : 124 + 4 * a].rearrange("p l j -> p (l j)").bitcast(I32),
+                    out=plane[0:MOVED_ROWS].rearrange("p l j -> p (l j)").bitcast(I32),
+                    in_=picked[first : first + MOVED_ROWS].rearrange("p l j -> p (l j)").bitcast(I32),
                 )
                 planes.append(plane)
             return planes
 
         def pick_words(j0, width, offset):
-            cols = slice(j0 // 16, (j0 + width) // 16)
-            both = stage.tile([P, 2, width], U32, name=f"both{j0}", offset=offset, align_bytes=64)
-            for l in range(2):
-                nc.vector.tensor_copy(both[:, l, :], tab_w[:].indirect(lists[l][:, cols]))
-            parted = keep.tile([P, 2, PASSES, 2 * width], U8, name=f"parted{j0}", align_bytes=64)
+            pairs = sbuf([P, LISTS, width], U32, f"pairs{j0}", offset)
+            for l in range(LISTS):
+                nc.vector.tensor_copy(pairs[:, l, :], tab_w[:].indirect(entries(l, j0, width)))
+            parted = sbuf([P, LISTS, PASSES, 2 * width], U8, f"parted{j0}")
             nc.vector.tensor_copy(
                 out=parted[:].bitcast(U16),
-                in_=both[:].bitcast(U16).rearrange("p l (j d) -> p l d j", d=2),
+                in_=pairs[:].bitcast(U16).rearrange("p l (j a) -> p l a j", a=PASSES),
             )
             return parted
 
-        def load_wd(g, h):
-            raw = stage.tile([P, 4, WD_COLS], F32, name=f"wd_raw{g}{h}", offset=(512, 5632)[g], align_bytes=64)
-            nc.sync.dma_start(
-                out=raw[:],
-                in_=wd[512 * g : 512 * (g + 1), WD_COLS * h : WD_COLS * (h + 1)].rearrange("(p i) n -> p i n", i=4),
-            )
+        def load_wd(half):
+            raw = sbuf([P, PASSES, 4, WD_COLS], F32, f"wd_raw{half}", WD_RAW)
+            for g in range(PASSES):
+                rows = wd[PASS_ROWS * g : PASS_ROWS * (g + 1), WD_COLS * half : WD_COLS * (half + 1)]
+                nc.sync.dma_start(out=raw[:, g], in_=rows.rearrange("(p t) n -> p t n", t=4))
             return raw
 
-        def quantise_wd(raws, h, tag):
-            grouped = keep.tile([P, PASSES, WD_COLS, 4], BF16, name=f"wd_grouped{h}", tag=tag, align_bytes=64)
-            for g, raw in enumerate(raws):
-                nc.scalar.copy(out=grouped[:, g], in_=raw[:].rearrange("p i n -> p n i"))
+        def quantise_wd(raw, half, offset):
+            grouped = sbuf([P, PASSES, WD_COLS, 4], BF16, f"wd_grouped{half}", offset)
+            for g in range(PASSES):
+                nc.scalar.copy(out=grouped[:, g], in_=raw[:, g].rearrange("p t n -> p n t"))
             nc.vector.quantize_mx(
-                out=wd_codes[h][:].rearrange("p g n -> p (g n)").bitcast(FP8X4),
-                scales=wd_scales[h][:].rearrange("p g n -> p (g n)"),
-                in_=grouped[:].rearrange("p g n i -> p (g n i)"),
+                out=wd_codes[half][:].rearrange("p g n -> p (g n)").bitcast(FP8X4),
+                scales=wd_scales[half][:].rearrange("p g n -> p (g n)"),
+                in_=grouped[:].rearrange("p g n t -> p (g n t)"),
             )
 
-        def first_product(parted, planes, p0, j0):
-            banks = [psum.tile([P, BANK], F32, name=f"acc{g}") for g in range(PASSES)]
-            order = [(l, a) for a in range(PASSES) for l in range(2)]
-            for n, (l, a) in enumerate(order):
+        def first_product(parted, planes, col, j0, offset):
+            banks = [double.tile([P, BANK], F32, name=f"a{g}") for g in range(PASSES)]
+            terms = [(l, a) for a in range(PASSES) for l in range(LISTS)]
+            for i, (l, a) in enumerate(terms):
                 for g in range(PASSES):
                     if l == 0:
-                        rhs = ws_w[:, a, 2 * BANK * g : 2 * BANK * (g + 1)].bitcast(FP4X4)
+                        w_words = ws_w[:, a, 2 * BANK * g : 2 * BANK * (g + 1)].bitcast(FP4X4)
                     else:
-                        rhs = wt_w[a][:, 4 * BANK * g : 4 * BANK * (g + 1)].bitcast(FP8X4)
+                        w_words = wt_w[a][:, 4 * BANK * g : 4 * BANK * (g + 1)].bitcast(FP8X4)
                     nc.tensor.matmul_mx(
                         out=banks[g][:],
-                        lhsT=parted[:, l, a, 2 * p0 : 2 * (p0 + P)].bitcast(FP4X4),
-                        lhsT_scale=planes[a][:, l, p0 : p0 + P],
-                        rhs=rhs,
+                        lhsT=parted[:, l, a, 2 * col : 2 * (col + P)].bitcast(FP4X4),
+                        lhsT_scale=planes[a][:, l, col : col + P],
+                        rhs=w_words,
                         rhs_scale=w_s[:, l, a, BANK * g : BANK * (g + 1)],
-                        start=(n == 0),
-                        stop=(n == len(order) - 1),
+                        start=(i == 0),
+                        stop=(i == len(terms) - 1),
                     )
-            rows = keep.tile([P, PASSES, 2, P, 2], BF16, name=f"rows{j0}", tag=f"rows{j0}", align_bytes=64)
+            rows = sbuf([P, PASSES, 2, P, 2], BF16, f"h_rows{j0}", offset)
             for g in range(PASSES):
                 nc.scalar.activation(
                     out=rows[:, g], in_=banks[g][:].rearrange("p (m u e) -> p u m e", u=2, e=2), func=ACT.Relu
                 )
             return rows
 
-        def turn(rows, grouped, c0, tag):
+        def turn(rows, grouped, col, bank_name):
             words = rows[:].rearrange("p g u m e -> p (g u m e)").bitcast(F32)
-            turned = single.tile([P, PASSES, 2, P], F32, name=tag)
+            turned = single.tile([P, PASSES, 2, P], F32, name=bank_name)
             for g in range(PASSES):
                 for u in range(2):
                     w0 = (2 * g + u) * P
                     nc.tensor.transpose(turned[:, g, u, :], words[:, w0 : w0 + P], ident[:])
             nc.scalar.copy(
-                out=grouped[:].bitcast(F32)[:, :, c0 : c0 + P, :],
+                out=grouped[:].bitcast(F32)[:, :, col : col + P, :],
                 in_=turned[:].rearrange("p g u j -> p g j u"),
             )
 
-        def hidden(parted, planes, p0, j0):
-            if j0 == 0:
-                grouped = placed.tile([P, PASSES, CHUNK, 4], BF16, name="h_grouped0", offset=6144, align_bytes=64)
-            else:
-                grouped = keep.tile([P, PASSES, CHUNK, 4], BF16, name=f"h_grouped{j0}", align_bytes=64)
-            rows = [first_product(parted, planes, p0 + s * P, j0 + s * P) for s in range(CHUNK // P)]
-            for s in range(CHUNK // P):
-                turn(rows[s], grouped, s * P, ("early", "late")[s])
-            codes = keep.tile([P, PASSES, CHUNK], U32, name=f"h_codes{j0}", align_bytes=64)
-            scales = keep.tile([P, PASSES, CHUNK], U8, name=f"h_scales{j0}", align_bytes=64)
+        def hidden(parted, planes, col, j0, grouped_offset=None, last_rows_offset=None):
+            grouped = sbuf([P, PASSES, CHUNK, 4], BF16, f"h_grouped{j0}", grouped_offset)
+            first_rows = first_product(parted, planes, col, j0, None)
+            last_rows = first_product(parted, planes, col + P, j0 + P, last_rows_offset)
+            turn(first_rows, grouped, 0, "early")
+            turn(last_rows, grouped, P, "late")
+            codes = sbuf([P, PASSES, CHUNK], U32, f"h_codes{j0}")
+            scales = sbuf([P, PASSES, CHUNK], U8, f"h_scales{j0}")
             nc.vector.quantize_mx(
                 out=codes[:].rearrange("p g j -> p (g j)").bitcast(FP8X4),
                 scales=scales[:].rearrange("p g j -> p (g j)"),
-                in_=grouped[:].rearrange("p g j i -> p (g j i)"),
+                in_=grouped[:].rearrange("p g j t -> p (g j t)"),
             )
             return codes, scales
 
-        def message(c, j0, chunks, acc=None):
+        def message(c, j0, chunks, held=False):
             width = CHUNK * len(chunks)
-            if acc is None:
-                bank = psum.tile([P, width], F32, name="y")
-                acc = bank[:]
+            if held:
+                bank = single.tile([P, width], F32, name="late")
+            else:
+                bank = double.tile([P, width], F32, name="y")
+            half, n0 = divmod(c * P, WD_COLS)
             for s, (codes, scales) in enumerate(chunks):
                 for g in range(PASSES):
                     nc.tensor.matmul_mx(
-                        out=acc[:, s * CHUNK : (s + 1) * CHUNK],
-                        lhsT=wd_codes[c // 2][:, g, c % 2 * P : (c % 2 + 1) * P].bitcast(FP8X4),
-                        lhsT_scale=wd_scales[c // 2][:, g, c % 2 * P : (c % 2 + 1) * P],
+                        out=bank[:, s * CHUNK : (s + 1) * CHUNK],
+                        lhsT=wd_codes[half][:, g, n0 : n0 + P].bitcast(FP8X4),
+                        lhsT_scale=wd_scales[half][:, g, n0 : n0 + P],
                         rhs=codes[:, g, :].bitcast(FP8X4),
                         rhs_scale=scales[:, g, :],
                         start=(g == 0),
                         stop=(g == PASSES - 1),
                     )
-            biased = keep.tile([P, width], F32, name=f"biased{c}_{j0}", tag=f"biased{c}_{j0}")
-            nc.scalar.activation(out=biased[:], in_=acc, func=ACT.Identity, bias=bias[:, c : c + 1], scale=1.0)
+            biased = keep.tile([P, width], F32, name=f"biased{c}_{j0}")
+            nc.scalar.activation(out=biased[:], in_=bank[:], func=ACT.Identity, bias=bias[:, c : c + 1], scale=1.0)
             nc.vector.tensor_tensor(
-                pages[c][:].indirect(lists[1][:, j0 // 16 : (j0 + width) // 16]),
-                biased[:],
-                weight[:, j0 : j0 + width],
-                MULT,
+                pages[c][:].indirect(entries(1, j0, width)), biased[:], weight[:, j0 : j0 + width], MULT
             )
 
-        def held(tiles, j0, h):
-            bank = single.tile([P, 2, CHUNK], F32, name="late")
-            for i, c in enumerate(tiles):
-                message(c, j0, [h], bank[:, i, :])
+        pages = []
 
-        def clear(page):
-            for s in range(4):
-                nc.gpsimd.memset(page[:, 512 * s : 512 * (s + 1)], 0.0)
+        def clear_page(offset):
+            page = sbuf([P, T], F32, f"page{len(pages)}", offset)
+            nc.vector.memset(page[:].bitcast(I32), 0)
             pages.append(page)
 
         def store(c):
             nc.sync.dma_start(out=out[c * P : (c + 1) * P, :], in_=pages[c][:])
 
-        scales_a = pick_scales(0, CHUNK, nc.scalar, 0)
-        scales_b = pick_scales(CHUNK, CHUNK, nc.scalar, 26624)
-        words_a = pick_words(0, CHUNK, 4096)
-        wd_first = [load_wd(g, 0) for g in range(PASSES)]
-        words_b = pick_words(CHUNK, CHUNK, 14336)
-        scales_cd = pick_scales(HALF, HALF, nc.sync, 4608)
-        weight = stage.tile([P, J], F32, name="weight", offset=10752, align_bytes=64)
-        nc.sync.dma_start(out=weight[:], in_=wgo)
-        bias = stage.tile([P, N_TILES], F32, name="bias", offset=14848, align_bytes=64)
-        with nc.allow_non_contiguous_dma(reason="one bias value a partition"):
-            nc.sync.dma_start(out=bias[:], in_=b.rearrange("(c p) -> p c", p=P))
-        words_cd = pick_words(HALF, HALF, 15360)
-        page0 = keep.tile([P, T], F32, name="page0")
-        nc.vector.memset(page0[:].bitcast(I32), 0)
-        pages = [page0]
-        quantise_wd(wd_first, 0, "wd_grouped")
-        wd_second = [load_wd(g, 1) for g in range(PASSES)]
+        j_a, j_b, j_c, j_d = range(0, J, CHUNK)
 
-        h_a = hidden(words_a, scales_a, 0, 0)
-        for c in (1, 2):
-            page = placed.tile([P, T], F32, name=f"page{c}", offset=8192 * (c - 1))
-            clear(page)
-        message(0, 0, [h_a])
-        page3 = keep.tile([P, T], F32, name="page3", tag="biased0_0")
-        clear(page3)
-        message(1, 0, [h_a])
-        quantise_wd(wd_second, 1, f"rows{P}")
-        message(2, 0, [h_a])
-        h_b = hidden(words_b, scales_b, 0, CHUNK)
-        held((3,), 0, h_a)
-        for c in range(3):
-            message(c, CHUNK, [h_b])
-        h_c = hidden(words_cd, scales_cd, 0, HALF)
-        held((3,), CHUNK, h_b)
-        message(0, HALF, [h_c])
-        message(1, HALF, [h_c])
-        h_d = hidden(words_cd, scales_cd, CHUNK, HALF + CHUNK)
-        held((2,), HALF, h_c)
-        for c in range(3):
-            message(c, HALF + CHUNK, [h_d])
+        planes_a = pick_scales(j_a, CHUNK, nc.scalar, PICKED_A)
+        words_a = pick_words(j_a, CHUNK, PAIRS_A)
+        wd_first = load_wd(0)
+        planes_b = pick_scales(j_b, CHUNK, nc.scalar, PICKED_B)
+        words_b = pick_words(j_b, CHUNK, PAIRS_B)
+        planes_cd = pick_scales(j_c, 2 * CHUNK, nc.sync, PICKED_CD)
+        weight = sbuf([P, J], F32, "weight", PICKED_A)
+        nc.sync.dma_start(out=weight[:], in_=wgo)
+        bias = sbuf([P, PAGES], F32, "bias", BIAS)
+        with nc.allow_non_contiguous_dma(reason="one bias value a partition and page"):
+            nc.sync.dma_start(out=bias[:], in_=b.rearrange("(c p) -> p c", p=P))
+        words_cd = pick_words(j_c, 2 * CHUNK, PAIRS_CD)
+        clear_page(None)
+        clear_page(PAGE_1)
+        quantise_wd(wd_first, 0, WD_GROUPED_0)
+        clear_page(WD_GROUPED_0)
+        wd_second = load_wd(1)
+
+        h_a = hidden(words_a, planes_a, 0, j_a, H_GROUPED_A, H_ROWS_A1)
+        clear_page(H_GROUPED_A)
+        message(0, j_a, [h_a])
+        message(1, j_a, [h_a])
+        quantise_wd(wd_second, 1, H_ROWS_A1)
+        message(2, j_a, [h_a])
+        h_b = hidden(words_b, planes_b, 0, j_b)
+        message(3, j_a, [h_a], held=True)
+        h_c = hidden(words_cd, planes_cd, 0, j_c)
+        for c in range(PAGES - 1):
+            message(c, j_b, [h_b])
+        message(3, j_b, [h_b], held=True)
+        h_d = hidden(words_cd, planes_cd, CHUNK, j_d)
+        message(0, j_c, [h_c])
+        message(1, j_c, [h_c])
+        message(2, j_c, [h_c], held=True)
+        for c in range(PAGES - 1):
+            message(c, j_d, [h_d])
             store(c)
-        message(3, HALF, [h_c, h_d])
+        message(3, j_c, [h_c, h_d])
         store(3)

@@ -39,8 +39,7 @@ PAIRS_B = PICKED_B + LISTS * CHUNK
 PICKED_CD = PAIRS_B
 BIAS = PICKED_CD + LISTS * 2 * CHUNK
 PAIRS_CD = BIAS + 64
-PAGE_1 = PAIRS_CD + LISTS * 2 * CHUNK * 4 - OVERLAP
-PICKED_A = PAGE_1 + 4 * T
+PICKED_A = PAIRS_CD + LISTS * 2 * CHUNK * 4
 WD_GROUPED_0 = PICKED_A + 4 * J
 H_GROUPED_A = WD_GROUPED_0 + 4 * T
 H_ROWS_A1 = H_GROUPED_A + 4 * T
@@ -100,7 +99,9 @@ def tile_list_msg_relu_bias_kernel(
         load_w_scales(1, wt_scales, range(QUADRANTS - 1, QUADRANTS))
         load_wt(1)
 
-        make_identity(nc, ident[:])
+        narrow = keep.tile([P, P], BF16, name="narrow")
+        make_identity(nc, narrow[:])
+        nc.scalar.activation(out=ident[:], in_=narrow[:], func=ACT.Identity)
 
         def entries(l, j0, width):
             return lists[l][:, j0 // PER_COLUMN : (j0 + width) // PER_COLUMN]
@@ -150,7 +151,7 @@ def tile_list_msg_relu_bias_kernel(
 
         def first_product(parted, planes, col, j0, offset):
             banks = [double.tile([P, BANK], F32, name=f"a{g}") for g in range(PASSES)]
-            terms = [(l, a) for a in range(PASSES) for l in range(LISTS)]
+            terms = [(l, a) for l in range(LISTS) for a in range(PASSES)]
             for i, (l, a) in enumerate(terms):
                 for g in range(PASSES):
                     if l == 0:
@@ -236,6 +237,9 @@ def tile_list_msg_relu_bias_kernel(
 
         j_a, j_b, j_c, j_d = range(0, J, CHUNK)
 
+        clear_page(None)
+        clear_page(None)
+
         planes_a = pick_scales(j_a, CHUNK, nc.scalar, PICKED_A)
         words_a = pick_words(j_a, CHUNK, PAIRS_A)
         wd_first = load_wd(0)
@@ -248,8 +252,6 @@ def tile_list_msg_relu_bias_kernel(
         with nc.allow_non_contiguous_dma(reason="one bias value a partition and page"):
             nc.sync.dma_start(out=bias[:], in_=b.rearrange("(c p) -> p c", p=P))
         words_cd = pick_words(j_c, 2 * CHUNK, PAIRS_CD)
-        clear_page(None)
-        clear_page(PAGE_1)
         quantise_wd(wd_first, 0, WD_GROUPED_0)
         clear_page(WD_GROUPED_0)
         wd_second = load_wd(1)

@@ -27,22 +27,29 @@ BANK = 512
 CHUNK = 256
 WD_COLS = 256
 PAGES = N // P
+BLOCKS = CHUNK // P
 
-SCALE_ROW = 24
+BY_BLOCK = [(block, l, a) for block in range(BLOCKS) for l in range(LISTS) for a in range(PASSES)]
+PASS_0_FIRST = [(block, l, 0) for l in range(LISTS) for block in range(BLOCKS)] + [
+    (block, l, 1) for block in range(BLOCKS) for l in range(LISTS)
+]
+
 MOVED_ROWS = 100
 
-OVERLAP = 512
-WD_RAW = 0
-PAIRS_A = WD_RAW + PASSES * 4 * WD_COLS * 4 - OVERLAP
-PICKED_B = PAIRS_A + OVERLAP
-PAIRS_B = PICKED_B + LISTS * CHUNK
-PICKED_CD = PAIRS_B
-BIAS = PICKED_CD + LISTS * 2 * CHUNK
-PAIRS_CD = BIAS + 64
-PICKED_A = PAIRS_CD + LISTS * 2 * CHUNK * 4
-WD_GROUPED_0 = PICKED_A + 4 * J
-H_GROUPED_A = WD_GROUPED_0 + 4 * T
-H_ROWS_A1 = H_GROUPED_A + 4 * T
+OVERLAP = 64
+PAIRS = 4 * CHUNK
+RAW = PASSES * 4 * WD_COLS * 4
+PICKED_CD = 0
+PAIRS_AB0 = PICKED_CD + PAIRS - OVERLAP
+PAIRS_CD0 = PAIRS_AB0 + PAIRS - OVERLAP
+WD_RAW_1 = PAIRS_CD0 + 2 * PAIRS
+PAIRS_A1 = WD_RAW_1 + RAW - OVERLAP
+PAIRS_B1 = PAIRS_A1 + OVERLAP
+BIAS = PAIRS_B1 + OVERLAP
+PAIRS_CD1 = PAIRS_B1 + PAIRS - OVERLAP
+WD_RAW_0 = PAIRS_CD1 + 2 * PAIRS
+H_GROUPED_A = WD_RAW_0 + RAW
+H_ROWS_A1 = H_GROUPED_A + 4 * PAIRS
 
 
 def tile_list_msg_relu_bias_kernel(
@@ -70,8 +77,7 @@ def tile_list_msg_relu_bias_kernel(
         wd_scales = [sbuf([P, PASSES, WD_COLS], U8, f"wd_scales{half}") for half in range(N // WD_COLS)]
         ident = keep.tile([P, P], F32, name="ident")
 
-        for q in range(QUADRANTS):
-            nc.vector.memset(tab_s[32 * q : 32 * q + SCALE_ROW, :].bitcast(I32), 0)
+        nc.vector.memset(tab_s[:].bitcast(I32), 0)
 
         def load_w_scales(l, scales, quadrants):
             for q in quadrants:
@@ -83,21 +89,25 @@ def tile_list_msg_relu_bias_kernel(
         def load_wt(a):
             nc.sync.dma_start(out=wt_w[a][:].bitcast(I32), in_=wt_words[a].rearrange("p r i -> p (r i)").bitcast(I32))
 
-        for q in range(QUADRANTS):
-            nc.sync.dma_start(
-                out=tab_s[32 * q + SCALE_ROW : 32 * (q + 1), :].bitcast(I32),
-                in_=tab_scales[:, 4 * q : 4 * q + 4, :].bitcast(I32),
-            )
+        def load_wd(raw, half, g):
+            rows = wd[PASS_ROWS * g : PASS_ROWS * (g + 1), WD_COLS * half : WD_COLS * (half + 1)]
+            nc.sync.dma_start(out=raw[:, g], in_=rows.rearrange("(p t) n -> p t n", t=4))
+
         nc.sync.dma_start(lists[0][:], offs)
         nc.sync.dma_start(lists[1][:], offs2)
-        load_w_scales(0, ws_scales, range(1))
         nc.sync.dma_start(out=tab_w[:].bitcast(I32), in_=tab_words[0].rearrange("p t b -> p (t b)").bitcast(I32))
-        load_w_scales(0, ws_scales, range(1, QUADRANTS))
+        for q in range(QUADRANTS):
+            nc.sync.dma_start(
+                out=tab_s[32 * q : 32 * q + 4 * PASSES, :].bitcast(I32),
+                in_=tab_scales[:, 4 * q : 4 * q + 4, :].bitcast(I32),
+            )
         nc.sync.dma_start(out=ws_w[:].bitcast(I32), in_=ws_words.rearrange("a p c -> p a c").bitcast(I32))
-        load_w_scales(1, wt_scales, range(QUADRANTS - 1))
-        load_wt(0)
-        load_w_scales(1, wt_scales, range(QUADRANTS - 1, QUADRANTS))
-        load_wt(1)
+        load_w_scales(0, ws_scales, range(QUADRANTS))
+        load_w_scales(1, wt_scales, range(QUADRANTS))
+        wd_first = sbuf([P, PASSES, 4, WD_COLS], F32, "wd_first", WD_RAW_0)
+        for a in range(PASSES):
+            load_wt(a)
+            load_wd(wd_first, 0, a)
 
         narrow = keep.tile([P, P], BF16, name="narrow")
         make_identity(nc, narrow[:])
@@ -106,72 +116,80 @@ def tile_list_msg_relu_bias_kernel(
         def entries(l, j0, width):
             return lists[l][:, j0 // PER_COLUMN : (j0 + width) // PER_COLUMN]
 
-        def pick_scales(j0, width, queue, offset):
-            picked = sbuf([P, LISTS, width], U8, f"picked{j0}", offset)
-            for l in range(LISTS):
-                nc.vector.tensor_copy(picked[:, l, :], tab_s[:].indirect(entries(l, j0, width)))
-            planes = []
-            for a in range(PASSES):
-                plane = sbuf([P, LISTS, width], U8, f"plane{a}_{j0}")
-                first = SCALE_ROW + 4 * a
-                queue.dma_start(
-                    out=plane[0:MOVED_ROWS].rearrange("p l j -> p (l j)").bitcast(I32),
-                    in_=picked[first : first + MOVED_ROWS].rearrange("p l j -> p (l j)").bitcast(I32),
-                )
-                planes.append(plane)
-            return planes
+        def pick_words(l, j0, width, offset):
+            pairs = sbuf([P, width], U32, f"pairs{l}_{j0}", offset)
+            nc.vector.tensor_copy(pairs[:], tab_w[:].indirect(entries(l, j0, width)))
+            return pairs
 
-        def pick_words(j0, width, offset):
-            pairs = sbuf([P, LISTS, width], U32, f"pairs{j0}", offset)
-            for l in range(LISTS):
-                nc.vector.tensor_copy(pairs[:, l, :], tab_w[:].indirect(entries(l, j0, width)))
-            parted = sbuf([P, LISTS, PASSES, 2 * width], U8, f"parted{j0}")
+        def part(pairs, l, j0, offset=None):
+            words = sbuf([P, PASSES, 2 * pairs.shape[1]], U8, f"words{l}_{j0}", offset)
             nc.vector.tensor_copy(
-                out=parted[:].bitcast(U16),
-                in_=pairs[:].bitcast(U16).rearrange("p l (j a) -> p l a j", a=PASSES),
+                out=words[:].bitcast(U16), in_=pairs[:].bitcast(U16).rearrange("p (j a) -> p a j", a=PASSES)
             )
-            return parted
+            return words
 
-        def load_wd(half):
-            raw = sbuf([P, PASSES, 4, WD_COLS], F32, f"wd_raw{half}", WD_RAW)
-            for g in range(PASSES):
-                rows = wd[PASS_ROWS * g : PASS_ROWS * (g + 1), WD_COLS * half : WD_COLS * (half + 1)]
-                nc.sync.dma_start(out=raw[:, g], in_=rows.rearrange("(p t) n -> p t n", t=4))
-            return raw
+        def pick_scales(picked, l, j0):
+            nc.vector.tensor_copy(picked[:, l, :], tab_s[:].indirect(entries(l, j0, picked.shape[2])))
+
+        def scale_planes(picked, j0, queue):
+            moved = sbuf(list(picked.shape), U8, f"moved{j0}")
+            queue.dma_start(
+                out=moved[0:MOVED_ROWS].rearrange("p l j -> p (l j)").bitcast(I32),
+                in_=picked[4 : 4 + MOVED_ROWS].rearrange("p l j -> p (l j)").bitcast(I32),
+            )
+            return [picked, moved]
+
+        def look_up(j0, queue, pairs_offsets):
+            pairs = [pick_words(l, j0, CHUNK, pairs_offsets[l]) for l in range(LISTS)]
+            picked = sbuf([P, LISTS, CHUNK], U8, f"picked{j0}")
+            words = []
+            for l in range(LISTS):
+                pick_scales(picked, l, j0)
+                words.append(part(pairs[l], l, j0))
+            return words, scale_planes(picked, j0, queue)
 
         def quantise_wd(raw, half, offset):
             grouped = sbuf([P, PASSES, WD_COLS, 4], BF16, f"wd_grouped{half}", offset)
             for g in range(PASSES):
-                nc.scalar.copy(out=grouped[:, g], in_=raw[:, g].rearrange("p t n -> p n t"))
+                nc.scalar.copy(
+                    out=grouped[:, g].rearrange("p (c i) t -> p c t i", i=4),
+                    in_=raw[:, g].rearrange("p t (c i) -> p c t i", i=4),
+                )
             nc.vector.quantize_mx(
                 out=wd_codes[half][:].rearrange("p g n -> p (g n)").bitcast(FP8X4),
                 scales=wd_scales[half][:].rearrange("p g n -> p (g n)"),
                 in_=grouped[:].rearrange("p g n t -> p (g n t)"),
             )
 
-        def first_product(parted, planes, col, j0, offset):
-            banks = [double.tile([P, BANK], F32, name=f"a{g}") for g in range(PASSES)]
-            terms = [(l, a) for l in range(LISTS) for a in range(PASSES)]
-            for i, (l, a) in enumerate(terms):
+        def first_product(looked_up, col, j0, order, offsets):
+            words, planes = looked_up
+            banks = [[double.tile([P, BANK], F32, name=f"a{g}") for g in range(PASSES)] for block in range(BLOCKS)]
+            rows = []
+            for block, l, a in order:
+                c0 = col + P * block
                 for g in range(PASSES):
                     if l == 0:
                         w_words = ws_w[:, a, 2 * BANK * g : 2 * BANK * (g + 1)].bitcast(FP4X4)
                     else:
                         w_words = wt_w[a][:, 4 * BANK * g : 4 * BANK * (g + 1)].bitcast(FP8X4)
                     nc.tensor.matmul_mx(
-                        out=banks[g][:],
-                        lhsT=parted[:, l, a, 2 * col : 2 * (col + P)].bitcast(FP4X4),
-                        lhsT_scale=planes[a][:, l, col : col + P],
+                        out=banks[block][g][:],
+                        lhsT=words[l][:, a, 2 * c0 : 2 * (c0 + P)].bitcast(FP4X4),
+                        lhsT_scale=planes[a][:, l, c0 : c0 + P],
                         rhs=w_words,
                         rhs_scale=w_s[:, l, a, BANK * g : BANK * (g + 1)],
-                        start=(i == 0),
-                        stop=(i == len(terms) - 1),
+                        start=(l, a) == (0, 0),
+                        stop=(l, a) == (LISTS - 1, PASSES - 1),
                     )
-            rows = sbuf([P, PASSES, 2, P, 2], BF16, f"h_rows{j0}", offset)
-            for g in range(PASSES):
-                nc.scalar.activation(
-                    out=rows[:, g], in_=banks[g][:].rearrange("p (m u e) -> p u m e", u=2, e=2), func=ACT.Relu
-                )
+                if (l, a) == (LISTS - 1, PASSES - 1):
+                    done = sbuf([P, PASSES, 2, P, 2], BF16, f"h_rows{j0}_{block}", offsets[block])
+                    for g in range(PASSES):
+                        nc.scalar.activation(
+                            out=done[:, g],
+                            in_=banks[block][g][:].rearrange("p (m u e) -> p u m e", u=2, e=2),
+                            func=ACT.Relu,
+                        )
+                    rows.append(done)
             return rows
 
         def turn(rows, grouped, col, bank_name):
@@ -186,10 +204,9 @@ def tile_list_msg_relu_bias_kernel(
                 in_=turned[:].rearrange("p g u j -> p g j u"),
             )
 
-        def hidden(parted, planes, col, j0, grouped_offset=None, last_rows_offset=None):
+        def hidden(looked_up, col, j0, order, grouped_offset=None, last_rows_offset=None):
             grouped = sbuf([P, PASSES, CHUNK, 4], BF16, f"h_grouped{j0}", grouped_offset)
-            first_rows = first_product(parted, planes, col, j0, None)
-            last_rows = first_product(parted, planes, col + P, j0 + P, last_rows_offset)
+            first_rows, last_rows = first_product(looked_up, col, j0, order, [None, last_rows_offset])
             turn(first_rows, grouped, 0, "early")
             turn(last_rows, grouped, P, "late")
             codes = sbuf([P, PASSES, CHUNK], U32, f"h_codes{j0}")
@@ -227,8 +244,8 @@ def tile_list_msg_relu_bias_kernel(
 
         pages = []
 
-        def clear_page(offset):
-            page = sbuf([P, T], F32, f"page{len(pages)}", offset)
+        def clear_page():
+            page = sbuf([P, T], F32, f"page{len(pages)}")
             nc.vector.memset(page[:].bitcast(I32), 0)
             pages.append(page)
 
@@ -237,38 +254,40 @@ def tile_list_msg_relu_bias_kernel(
 
         j_a, j_b, j_c, j_d = range(0, J, CHUNK)
 
-        clear_page(None)
-        clear_page(None)
+        for c in range(PAGES):
+            clear_page()
 
-        planes_a = pick_scales(j_a, CHUNK, nc.scalar, PICKED_A)
-        words_a = pick_words(j_a, CHUNK, PAIRS_A)
-        wd_first = load_wd(0)
-        planes_b = pick_scales(j_b, CHUNK, nc.scalar, PICKED_B)
-        words_b = pick_words(j_b, CHUNK, PAIRS_B)
-        planes_cd = pick_scales(j_c, 2 * CHUNK, nc.sync, PICKED_CD)
-        weight = sbuf([P, J], F32, "weight", PICKED_A)
-        nc.sync.dma_start(out=weight[:], in_=wgo)
+        looked_a = look_up(j_a, nc.scalar, [PAIRS_AB0, PAIRS_A1])
+        wd_second = sbuf([P, PASSES, 4, WD_COLS], F32, "wd_second", WD_RAW_1)
+        for g in range(PASSES):
+            load_wd(wd_second, 1, g)
+        looked_b = look_up(j_b, nc.sync, [PAIRS_AB0, PAIRS_B1])
         bias = sbuf([P, PAGES], F32, "bias", BIAS)
         with nc.allow_non_contiguous_dma(reason="one bias value a partition and page"):
             nc.sync.dma_start(out=bias[:], in_=b.rearrange("(c p) -> p c", p=P))
-        words_cd = pick_words(j_c, 2 * CHUNK, PAIRS_CD)
-        quantise_wd(wd_first, 0, WD_GROUPED_0)
-        clear_page(WD_GROUPED_0)
-        wd_second = load_wd(1)
+        picked_cd = sbuf([P, LISTS, 2 * CHUNK], U8, "picked_cd", PICKED_CD)
+        for l in range(LISTS):
+            pick_scales(picked_cd, l, j_c)
+        planes_cd = scale_planes(picked_cd, j_c, nc.sync)
+        pairs_cd = [pick_words(l, j_c, 2 * CHUNK, offset) for l, offset in enumerate([PAIRS_CD0, PAIRS_CD1])]
+        quantise_wd(wd_first, 0, None)
+        weight = sbuf([P, J], F32, "weight", WD_RAW_0)
+        nc.sync.dma_start(out=weight[:], in_=wgo)
 
-        h_a = hidden(words_a, planes_a, 0, j_a, H_GROUPED_A, H_ROWS_A1)
-        clear_page(H_GROUPED_A)
+        h_a = hidden(looked_a, 0, j_a, PASS_0_FIRST, H_GROUPED_A, H_ROWS_A1)
+        words_cd = [part(pairs_cd[l], l, j_c, H_GROUPED_A + 2 * PAIRS * l) for l in range(LISTS)]
+        looked_cd = words_cd, planes_cd
         message(0, j_a, [h_a])
         message(1, j_a, [h_a])
         quantise_wd(wd_second, 1, H_ROWS_A1)
         message(2, j_a, [h_a])
-        h_b = hidden(words_b, planes_b, 0, j_b)
+        h_b = hidden(looked_b, 0, j_b, BY_BLOCK)
         message(3, j_a, [h_a], held=True)
-        h_c = hidden(words_cd, planes_cd, 0, j_c)
+        h_c = hidden(looked_cd, 0, j_c, BY_BLOCK)
         for c in range(PAGES - 1):
             message(c, j_b, [h_b])
         message(3, j_b, [h_b], held=True)
-        h_d = hidden(words_cd, planes_cd, CHUNK, j_d)
+        h_d = hidden(looked_cd, CHUNK, j_d, BY_BLOCK)
         message(0, j_c, [h_c])
         message(1, j_c, [h_c])
         message(2, j_c, [h_c], held=True)

@@ -39,9 +39,11 @@ MOVED_ROWS = 100
 OVERLAP = 64
 PAIRS = 4 * CHUNK
 RAW = PASSES * 4 * WD_COLS * 4
-PICKED_CD = 0
-PAIRS_AB0 = PICKED_CD + PAIRS - OVERLAP
-PAIRS_CD0 = PAIRS_AB0 + PAIRS - OVERLAP
+PICKED_B = 0
+PAIRS_A0 = PICKED_B + LISTS * CHUNK - OVERLAP
+PICKED_CD = PAIRS_A0 + OVERLAP
+PAIRS_B0 = PAIRS_A0 + PAIRS - OVERLAP
+PAIRS_CD0 = PAIRS_B0 + PAIRS - OVERLAP
 WD_RAW_1 = PAIRS_CD0 + 2 * PAIRS
 PAIRS_A1 = WD_RAW_1 + RAW - OVERLAP
 PAIRS_B1 = PAIRS_A1 + OVERLAP
@@ -86,6 +88,11 @@ def tile_list_msg_relu_bias_kernel(
                     in_=scales[:, 4 * q : 4 * q + 4, :].rearrange("a s r -> s a r").bitcast(I32),
                 )
 
+        def load_tab_words(half):
+            columns = slice(half * T // 2, (half + 1) * T // 2)
+            words = tab_words[0, :, columns, :].rearrange("p t b -> p (t b)")
+            nc.sync.dma_start(out=tab_w[:, columns].bitcast(I32), in_=words.bitcast(I32))
+
         def load_wt(a):
             nc.sync.dma_start(out=wt_w[a][:].bitcast(I32), in_=wt_words[a].rearrange("p r i -> p (r i)").bitcast(I32))
 
@@ -95,19 +102,18 @@ def tile_list_msg_relu_bias_kernel(
 
         nc.sync.dma_start(lists[0][:], offs)
         nc.sync.dma_start(lists[1][:], offs2)
-        nc.sync.dma_start(out=tab_w[:].bitcast(I32), in_=tab_words[0].rearrange("p t b -> p (t b)").bitcast(I32))
+        load_tab_words(0)
         for q in range(QUADRANTS):
             nc.sync.dma_start(
                 out=tab_s[32 * q : 32 * q + 4 * PASSES, :].bitcast(I32),
                 in_=tab_scales[:, 4 * q : 4 * q + 4, :].bitcast(I32),
             )
+        load_tab_words(1)
         nc.sync.dma_start(out=ws_w[:].bitcast(I32), in_=ws_words.rearrange("a p c -> p a c").bitcast(I32))
         load_w_scales(0, ws_scales, range(QUADRANTS))
-        load_w_scales(1, wt_scales, range(QUADRANTS))
         wd_first = sbuf([P, PASSES, 4, WD_COLS], F32, "wd_first", WD_RAW_0)
-        for a in range(PASSES):
-            load_wt(a)
-            load_wd(wd_first, 0, a)
+        load_wt(0)
+        load_wd(wd_first, 0, 0)
 
         narrow = keep.tile([P, P], BF16, name="narrow")
         make_identity(nc, narrow[:])
@@ -131,22 +137,21 @@ def tile_list_msg_relu_bias_kernel(
         def pick_scales(picked, l, j0):
             nc.vector.tensor_copy(picked[:, l, :], tab_s[:].indirect(entries(l, j0, picked.shape[2])))
 
-        def scale_planes(picked, j0, queue):
+        def scale_planes(picked, j0):
             moved = sbuf(list(picked.shape), U8, f"moved{j0}")
-            queue.dma_start(
+            nc.sync.dma_start(
                 out=moved[0:MOVED_ROWS].rearrange("p l j -> p (l j)").bitcast(I32),
                 in_=picked[4 : 4 + MOVED_ROWS].rearrange("p l j -> p (l j)").bitcast(I32),
             )
             return [picked, moved]
 
-        def look_up(j0, queue, pairs_offsets):
-            pairs = [pick_words(l, j0, CHUNK, pairs_offsets[l]) for l in range(LISTS)]
-            picked = sbuf([P, LISTS, CHUNK], U8, f"picked{j0}")
-            words = []
+        def look_up(j0, picked_offset, pairs_offsets):
+            picked = sbuf([P, LISTS, CHUNK], U8, f"picked{j0}", picked_offset)
             for l in range(LISTS):
                 pick_scales(picked, l, j0)
-                words.append(part(pairs[l], l, j0))
-            return words, scale_planes(picked, j0, queue)
+            planes = scale_planes(picked, j0)
+            pairs = [pick_words(l, j0, CHUNK, pairs_offsets[l]) for l in range(LISTS)]
+            return [part(pairs[l], l, j0) for l in range(LISTS)], planes
 
         def quantise_wd(raw, half, offset):
             grouped = sbuf([P, PASSES, WD_COLS, 4], BF16, f"wd_grouped{half}", offset)
@@ -244,9 +249,10 @@ def tile_list_msg_relu_bias_kernel(
 
         pages = []
 
-        def clear_page():
+        def clear_page(engine, cuts):
             page = sbuf([P, T], F32, f"page{len(pages)}")
-            nc.vector.memset(page[:].bitcast(I32), 0)
+            for first, last in zip(cuts, cuts[1:]):
+                engine.memset(page[:, first:last].bitcast(I32), 0)
             pages.append(page)
 
         def store(c):
@@ -254,21 +260,26 @@ def tile_list_msg_relu_bias_kernel(
 
         j_a, j_b, j_c, j_d = range(0, J, CHUNK)
 
-        for c in range(PAGES):
-            clear_page()
+        for c in range(PAGES // 2):
+            clear_page(nc.vector, [0, T // 2 - 1, T])
+        for c in range(PAGES // 2):
+            clear_page(nc.gpsimd, [0, T])
 
-        looked_a = look_up(j_a, nc.scalar, [PAIRS_AB0, PAIRS_A1])
+        looked_a = look_up(j_a, None, [PAIRS_A0, PAIRS_A1])
+        load_w_scales(1, wt_scales, range(QUADRANTS))
+        load_wt(1)
+        load_wd(wd_first, 0, 1)
         wd_second = sbuf([P, PASSES, 4, WD_COLS], F32, "wd_second", WD_RAW_1)
         for g in range(PASSES):
             load_wd(wd_second, 1, g)
-        looked_b = look_up(j_b, nc.sync, [PAIRS_AB0, PAIRS_B1])
+        looked_b = look_up(j_b, PICKED_B, [PAIRS_B0, PAIRS_B1])
         bias = sbuf([P, PAGES], F32, "bias", BIAS)
         with nc.allow_non_contiguous_dma(reason="one bias value a partition and page"):
             nc.sync.dma_start(out=bias[:], in_=b.rearrange("(c p) -> p c", p=P))
         picked_cd = sbuf([P, LISTS, 2 * CHUNK], U8, "picked_cd", PICKED_CD)
         for l in range(LISTS):
             pick_scales(picked_cd, l, j_c)
-        planes_cd = scale_planes(picked_cd, j_c, nc.sync)
+        planes_cd = scale_planes(picked_cd, j_c)
         pairs_cd = [pick_words(l, j_c, 2 * CHUNK, offset) for l, offset in enumerate([PAIRS_CD0, PAIRS_CD1])]
         quantise_wd(wd_first, 0, None)
         weight = sbuf([P, J], F32, "weight", WD_RAW_0)

@@ -29,7 +29,7 @@ WD_COLS = 256
 PAGES = N // P
 BLOCKS = CHUNK // P
 
-BY_BLOCK = [(block, l, a) for block in range(BLOCKS) for l in range(LISTS) for a in range(PASSES)]
+BY_BLOCK = [(block, l, a) for block in range(BLOCKS) for a in range(PASSES) for l in range(LISTS)]
 PASS_0_FIRST = [(block, l, 0) for l in range(LISTS) for block in range(BLOCKS)] + [
     (block, l, 1) for block in range(BLOCKS) for l in range(LISTS)
 ]
@@ -39,19 +39,20 @@ MOVED_ROWS = 100
 OVERLAP = 64
 PAIRS = 4 * CHUNK
 RAW = PASSES * 4 * WD_COLS * 4
-PICKED_B = 0
-PAIRS_A0 = PICKED_B + LISTS * CHUNK - OVERLAP
-PICKED_CD = PAIRS_A0 + OVERLAP
-PAIRS_B0 = PAIRS_A0 + PAIRS - OVERLAP
-PAIRS_CD0 = PAIRS_B0 + PAIRS - OVERLAP
-WD_RAW_1 = PAIRS_CD0 + 2 * PAIRS
-PAIRS_A1 = WD_RAW_1 + RAW - OVERLAP
-PAIRS_B1 = PAIRS_A1 + OVERLAP
-BIAS = PAIRS_B1 + OVERLAP
-PAIRS_CD1 = PAIRS_B1 + PAIRS - OVERLAP
-WD_RAW_0 = PAIRS_CD1 + 2 * PAIRS
-H_GROUPED_A = WD_RAW_0 + RAW
+LATE_LOADS = 0
+PAIRS_B = LATE_LOADS + RAW + 4 * J - OVERLAP
+BIAS = PAIRS_B + OVERLAP
+PAIRS_A1 = BIAS + OVERLAP
+PAIRS_CD = PAIRS_B + 2 * PAIRS - OVERLAP
+PICKED_B = PAIRS_CD + 4 * PAIRS
+PAIRS_A0 = PICKED_B
+PICKED_CD = PICKED_B + LISTS * CHUNK
+H_GROUPED_A = PICKED_CD + PAIRS
 H_ROWS_A1 = H_GROUPED_A + 4 * PAIRS
+H_ROWS_B1 = H_ROWS_A1 + 2 * R
+PAGE_3 = H_ROWS_B1 + 2 * R
+H_GROUPED_B = PAGE_3 + 4 * T - OVERLAP
+WD_CODES_1 = H_GROUPED_B + OVERLAP
 
 
 def tile_list_msg_relu_bias_kernel(
@@ -75,8 +76,6 @@ def tile_list_msg_relu_bias_kernel(
         w_s = sbuf([P, LISTS, PASSES, R], U8, "w_s")
         ws_w = sbuf([P, PASSES, 2 * R], U8, "ws_w")
         wt_w = [sbuf([P, 4 * R], U8, f"wt_w{a}") for a in range(PASSES)]
-        wd_codes = [sbuf([P, PASSES, WD_COLS], U32, f"wd_codes{half}") for half in range(N // WD_COLS)]
-        wd_scales = [sbuf([P, PASSES, WD_COLS], U8, f"wd_scales{half}") for half in range(N // WD_COLS)]
         ident = keep.tile([P, P], F32, name="ident")
 
         nc.vector.memset(tab_s[:].bitcast(I32), 0)
@@ -111,7 +110,7 @@ def tile_list_msg_relu_bias_kernel(
         load_tab_words(1)
         nc.sync.dma_start(out=ws_w[:].bitcast(I32), in_=ws_words.rearrange("a p c -> p a c").bitcast(I32))
         load_w_scales(0, ws_scales, range(QUADRANTS))
-        wd_first = sbuf([P, PASSES, 4, WD_COLS], F32, "wd_first", WD_RAW_0)
+        wd_first = sbuf([P, PASSES, 4, WD_COLS], F32, "wd_first")
         load_wt(0)
         load_wd(wd_first, 0, 0)
 
@@ -122,17 +121,16 @@ def tile_list_msg_relu_bias_kernel(
         def entries(l, j0, width):
             return lists[l][:, j0 // PER_COLUMN : (j0 + width) // PER_COLUMN]
 
-        def pick_words(l, j0, width, offset):
-            pairs = sbuf([P, width], U32, f"pairs{l}_{j0}", offset)
-            nc.vector.tensor_copy(pairs[:], tab_w[:].indirect(entries(l, j0, width)))
-            return pairs
+        def pick_words(pairs, l, j0):
+            nc.vector.tensor_copy(pairs, tab_w[:].indirect(entries(l, j0, pairs.shape[1])))
 
-        def part(pairs, l, j0, offset=None):
-            words = sbuf([P, PASSES, 2 * pairs.shape[1]], U8, f"words{l}_{j0}", offset)
+        def part(pairs, name, offset=None):
+            count, width = pairs.shape[1:]
+            words = sbuf([P, count, PASSES, 2 * width], U8, name, offset)
             nc.vector.tensor_copy(
-                out=words[:].bitcast(U16), in_=pairs[:].bitcast(U16).rearrange("p (j a) -> p a j", a=PASSES)
+                out=words[:].bitcast(U16), in_=pairs[:].bitcast(U16).rearrange("p l (j a) -> p l a j", a=PASSES)
             )
-            return words
+            return [words[:, l] for l in range(count)]
 
         def pick_scales(picked, l, j0):
             nc.vector.tensor_copy(picked[:, l, :], tab_s[:].indirect(entries(l, j0, picked.shape[2])))
@@ -145,28 +143,20 @@ def tile_list_msg_relu_bias_kernel(
             )
             return [picked, moved]
 
-        def look_up(j0, picked_offset, pairs_offsets):
-            picked = sbuf([P, LISTS, CHUNK], U8, f"picked{j0}", picked_offset)
-            for l in range(LISTS):
-                pick_scales(picked, l, j0)
-            planes = scale_planes(picked, j0)
-            pairs = [pick_words(l, j0, CHUNK, pairs_offsets[l]) for l in range(LISTS)]
-            return [part(pairs[l], l, j0) for l in range(LISTS)], planes
+        def round_wd(copy, raw, grouped):
+            copy(out=grouped.rearrange("p (c i) t -> p c t i", i=4), in_=raw.rearrange("p t (c i) -> p c t i", i=4))
 
-        def quantise_wd(raw, half, offset):
-            grouped = sbuf([P, PASSES, WD_COLS, 4], BF16, f"wd_grouped{half}", offset)
-            for g in range(PASSES):
-                nc.scalar.copy(
-                    out=grouped[:, g].rearrange("p (c i) t -> p c t i", i=4),
-                    in_=raw[:, g].rearrange("p t (c i) -> p c t i", i=4),
-                )
-            nc.vector.quantize_mx(
-                out=wd_codes[half][:].rearrange("p g n -> p (g n)").bitcast(FP8X4),
-                scales=wd_scales[half][:].rearrange("p g n -> p (g n)"),
-                in_=grouped[:].rearrange("p g n t -> p (g n t)"),
-            )
+        def quantise(codes, scales, grouped):
+            nc.vector.quantize_mx(out=codes.bitcast(FP8X4), scales=scales, in_=grouped)
 
-        def first_product(looked_up, col, j0, order, offsets):
+        wd_codes, wd_scales = [], []
+
+        def wd_tiles(offset=None):
+            wd_codes.append(sbuf([P, PASSES, WD_COLS], U32, f"wd_codes{len(wd_codes)}", offset))
+            wd_scales.append(sbuf([P, PASSES, WD_COLS], U8, f"wd_scales{len(wd_scales)}"))
+            return wd_codes[-1], wd_scales[-1]
+
+        def first_product(looked_up, col, j0, order, offsets, between):
             words, planes = looked_up
             banks = [[double.tile([P, BANK], F32, name=f"a{g}") for g in range(PASSES)] for block in range(BLOCKS)]
             rows = []
@@ -195,6 +185,8 @@ def tile_list_msg_relu_bias_kernel(
                             func=ACT.Relu,
                         )
                     rows.append(done)
+                if (block, l, a) in between:
+                    between[block, l, a]()
             return rows
 
         def turn(rows, grouped, col, bank_name):
@@ -209,21 +201,21 @@ def tile_list_msg_relu_bias_kernel(
                 in_=turned[:].rearrange("p g u j -> p g j u"),
             )
 
-        def hidden(looked_up, col, j0, order, grouped_offset=None, last_rows_offset=None):
+        def hidden(looked_up, col, j0, order, between, grouped_offset=None, last_rows_offset=None):
             grouped = sbuf([P, PASSES, CHUNK, 4], BF16, f"h_grouped{j0}", grouped_offset)
-            first_rows, last_rows = first_product(looked_up, col, j0, order, [None, last_rows_offset])
+            first_rows, last_rows = first_product(looked_up, col, j0, order, [None, last_rows_offset], between)
             turn(first_rows, grouped, 0, "early")
             turn(last_rows, grouped, P, "late")
             codes = sbuf([P, PASSES, CHUNK], U32, f"h_codes{j0}")
             scales = sbuf([P, PASSES, CHUNK], U8, f"h_scales{j0}")
-            nc.vector.quantize_mx(
-                out=codes[:].rearrange("p g j -> p (g j)").bitcast(FP8X4),
-                scales=scales[:].rearrange("p g j -> p (g j)"),
-                in_=grouped[:].rearrange("p g j t -> p (g j t)"),
+            quantise(
+                codes[:].rearrange("p g j -> p (g j)"),
+                scales[:].rearrange("p g j -> p (g j)"),
+                grouped[:].rearrange("p g j t -> p (g j t)"),
             )
             return codes, scales
 
-        def message(c, j0, chunks, held=False):
+        def message(c, chunks, biased, held=False):
             width = CHUNK * len(chunks)
             if held:
                 bank = single.tile([P, width], F32, name="late")
@@ -241,69 +233,104 @@ def tile_list_msg_relu_bias_kernel(
                         start=(g == 0),
                         stop=(g == PASSES - 1),
                     )
-            biased = keep.tile([P, width], F32, name=f"biased{c}_{j0}")
-            nc.scalar.activation(out=biased[:], in_=bank[:], func=ACT.Identity, bias=bias[:, c : c + 1], scale=1.0)
+            nc.scalar.activation(out=biased, in_=bank[:], func=ACT.Identity, bias=bias[:, c : c + 1], scale=1.0)
+
+        def scatter(c, j0, biased):
+            width = biased.shape[1]
             nc.vector.tensor_tensor(
-                pages[c][:].indirect(entries(1, j0, width)), biased[:], weight[:, j0 : j0 + width], MULT
+                pages[c][:].indirect(entries(1, j0, width)), biased, weight[:, j0 : j0 + width], MULT
             )
 
-        pages = []
-
-        def clear_page(engine, cuts):
-            page = sbuf([P, T], F32, f"page{len(pages)}")
-            for first, last in zip(cuts, cuts[1:]):
-                engine.memset(page[:, first:last].bitcast(I32), 0)
-            pages.append(page)
+        def send(c, j0, chunks, held=False):
+            biased = keep.tile([P, CHUNK * len(chunks)], F32, name=f"biased{c}_{j0}")
+            message(c, chunks, biased[:], held)
+            scatter(c, j0, biased[:])
 
         def store(c):
             nc.sync.dma_start(out=out[c * P : (c + 1) * P, :], in_=pages[c][:])
 
+        def first_pages(j0, h):
+            for c in range(2):
+                send(c, j0, [h])
+
         j_a, j_b, j_c, j_d = range(0, J, CHUNK)
 
-        for c in range(PAGES // 2):
-            clear_page(nc.vector, [0, T // 2 - 1, T])
-        for c in range(PAGES // 2):
-            clear_page(nc.gpsimd, [0, T])
+        def clear_page(offset=None):
+            page = sbuf([P, T], F32, f"page{len(pages)}", offset)
+            nc.vector.memset(page[:].bitcast(I32), 0)
+            pages.append(page)
 
-        looked_a = look_up(j_a, None, [PAIRS_A0, PAIRS_A1])
+        pages = []
+        for c in range(PAGES - 1):
+            clear_page()
+
+        picked_a = sbuf([P, LISTS, CHUNK], U8, "picked_a")
+        for l in range(LISTS):
+            pick_scales(picked_a, l, j_a)
+        planes_a = scale_planes(picked_a, j_a)
+        pairs_a = [sbuf([P, 1, CHUNK], U32, f"pairs_a{l}", offset) for l, offset in enumerate([PAIRS_A0, PAIRS_A1])]
+        for l in range(LISTS):
+            pick_words(pairs_a[l][:, 0, :], l, j_a)
+        words_a = part(pairs_a[0], "words_a0") + part(pairs_a[1], "words_a1")
         load_w_scales(1, wt_scales, range(QUADRANTS))
         load_wt(1)
+
+        picked_b = sbuf([P, LISTS, CHUNK], U8, "picked_b", PICKED_B)
+        for l in range(LISTS):
+            pick_scales(picked_b, l, j_b)
+        planes_b = scale_planes(picked_b, j_b)
         load_wd(wd_first, 0, 1)
-        wd_second = sbuf([P, PASSES, 4, WD_COLS], F32, "wd_second", WD_RAW_1)
-        for g in range(PASSES):
-            load_wd(wd_second, 1, g)
-        looked_b = look_up(j_b, PICKED_B, [PAIRS_B0, PAIRS_B1])
+        pairs_b = sbuf([P, LISTS, CHUNK], U32, "pairs_b", PAIRS_B)
+        for l in range(LISTS):
+            pick_words(pairs_b[:, l, :], l, j_b)
+        picked_cd = sbuf([P, LISTS, 2 * CHUNK], U8, "picked_cd", PICKED_CD)
+        pick_scales(picked_cd, 0, j_c)
+        words_b = part(pairs_b, "words_b")
+        pick_scales(picked_cd, 1, j_c)
+
+        late = sbuf([P, (RAW + 4 * J) // 4], F32, "late_loads", LATE_LOADS)
+        wd_second = late[:, : RAW // 4].rearrange("p (g t n) -> p g t n", g=PASSES, t=4)
+        weight = late[:, RAW // 4 :]
+        load_wd(wd_second, 1, 0)
         bias = sbuf([P, PAGES], F32, "bias", BIAS)
         with nc.allow_non_contiguous_dma(reason="one bias value a partition and page"):
             nc.sync.dma_start(out=bias[:], in_=b.rearrange("(c p) -> p c", p=P))
-        picked_cd = sbuf([P, LISTS, 2 * CHUNK], U8, "picked_cd", PICKED_CD)
-        for l in range(LISTS):
-            pick_scales(picked_cd, l, j_c)
+        nc.sync.dma_start(out=weight, in_=wgo)
+        load_wd(wd_second, 1, 1)
         planes_cd = scale_planes(picked_cd, j_c)
-        pairs_cd = [pick_words(l, j_c, 2 * CHUNK, offset) for l, offset in enumerate([PAIRS_CD0, PAIRS_CD1])]
-        quantise_wd(wd_first, 0, None)
-        weight = sbuf([P, J], F32, "weight", WD_RAW_0)
-        nc.sync.dma_start(out=weight[:], in_=wgo)
+        pairs_cd = sbuf([P, LISTS, 2 * CHUNK], U32, "pairs_cd", PAIRS_CD)
+        for l in range(LISTS):
+            pick_words(pairs_cd[:, l, :], l, j_c)
+        grouped = sbuf([P, PASSES, WD_COLS, 4], BF16, "wd_grouped")
+        round_wd(nc.scalar.copy, wd_first[:, 0], grouped[:, 0])
+        round_wd(nc.vector.tensor_copy, wd_first[:, 1], grouped[:, 1])
+        codes, scales = wd_tiles()
+        quantise(
+            codes[:].rearrange("p g n -> p (g n)"),
+            scales[:].rearrange("p g n -> p (g n)"),
+            grouped[:].rearrange("p g n t -> p (g n t)"),
+        )
 
-        h_a = hidden(looked_a, 0, j_a, PASS_0_FIRST, H_GROUPED_A, H_ROWS_A1)
-        words_cd = [part(pairs_cd[l], l, j_c, H_GROUPED_A + 2 * PAIRS * l) for l in range(LISTS)]
-        looked_cd = words_cd, planes_cd
-        message(0, j_a, [h_a])
-        message(1, j_a, [h_a])
-        quantise_wd(wd_second, 1, H_ROWS_A1)
-        message(2, j_a, [h_a])
-        h_b = hidden(looked_b, 0, j_b, BY_BLOCK)
-        message(3, j_a, [h_a], held=True)
-        h_c = hidden(looked_cd, 0, j_c, BY_BLOCK)
+        h_a = hidden((words_a, planes_a), 0, j_a, PASS_0_FIRST, {}, H_GROUPED_A, H_ROWS_A1)
+        words_cd = part(pairs_cd, "words_cd", H_GROUPED_A)
+        second_grouped = [sbuf([P, WD_COLS, 4], BF16, "wd_second_grouped0", H_ROWS_A1)]
+        round_wd(nc.scalar.copy, wd_second[:, 0], second_grouped[0][:])
+        sends = {(1, 1, 0): lambda: first_pages(j_a, h_a)}
+        h_b = hidden((words_b, planes_b), 0, j_b, BY_BLOCK, sends, H_GROUPED_B, H_ROWS_B1)
+        clear_page(PAGE_3)
+        second_grouped.append(sbuf([P, WD_COLS, 4], BF16, "wd_second_grouped1", H_ROWS_B1))
+        round_wd(nc.scalar.copy, wd_second[:, 1], second_grouped[1][:])
+        codes, scales = wd_tiles(WD_CODES_1)
+        for g in range(PASSES):
+            quantise(codes[:, g, :], scales[:, g, :], second_grouped[g][:].rearrange("p n t -> p (n t)"))
+
+        sends = {(1, 0, 0): lambda: first_pages(j_b, h_b), (1, 1, 1): lambda: send(2, j_a, [h_a, h_b])}
+        h_c = hidden((words_cd, planes_cd), 0, j_c, BY_BLOCK, sends)
+        send(3, j_a, [h_a, h_b], held=True)
+        h_d = hidden((words_cd, planes_cd), CHUNK, j_d, BY_BLOCK, {(1, 1, 1): lambda: first_pages(j_c, h_c)})
+        send(2, j_c, [h_c], held=True)
         for c in range(PAGES - 1):
-            message(c, j_b, [h_b])
-        message(3, j_b, [h_b], held=True)
-        h_d = hidden(looked_cd, CHUNK, j_d, BY_BLOCK)
-        message(0, j_c, [h_c])
-        message(1, j_c, [h_c])
-        message(2, j_c, [h_c], held=True)
-        for c in range(PAGES - 1):
-            message(c, j_d, [h_d])
+            send(c, j_d, [h_d])
             store(c)
-        message(3, j_c, [h_c, h_d])
+        send(3, j_c, [h_c, h_d])
         store(3)

@@ -29,11 +29,14 @@ WD_COLS = 256
 PAGES = N // P
 BLOCKS = CHUNK // P
 
-BY_BLOCK = [(block, l, a) for block in range(BLOCKS) for a in range(PASSES) for l in range(LISTS)]
-PASS_0_FIRST = [(block, l, 0) for l in range(LISTS) for block in range(BLOCKS)] + [
-    (block, l, 1) for block in range(BLOCKS) for l in range(LISTS)
+BANKS = [(block, g) for block in range(BLOCKS) for g in range(PASSES)]
+BY_BANK = [(block, g, l, a) for block, g in BANKS for a in range(PASSES) for l in range(LISTS)]
+PASS_0_FIRST = [(block, g, l, 0) for l in range(LISTS) for block, g in BANKS] + [
+    (block, g, l, 1) for block, g in BANKS for l in range(LISTS)
 ]
 
+TAB_FIRST = T // 4
+PORT_ORDER = [0, 2, 1, 3]
 MOVED_ROWS = 100
 
 OVERLAP = 64
@@ -44,15 +47,16 @@ PAIRS_B = LATE_LOADS + RAW + 4 * J - OVERLAP
 BIAS = PAIRS_B + OVERLAP
 PAIRS_A1 = BIAS + OVERLAP
 PAIRS_CD = PAIRS_B + 2 * PAIRS - OVERLAP
-PICKED_B = PAIRS_CD + 4 * PAIRS
-PAIRS_A0 = PICKED_B
-PICKED_CD = PICKED_B + LISTS * CHUNK
+PAIRS_A0 = PAIRS_CD + 4 * PAIRS
+PICKED_B = PAIRS_A0
+PICKED_CD = PICKED_B + CHUNK
 H_GROUPED_A = PICKED_CD + PAIRS
 H_ROWS_A1 = H_GROUPED_A + 4 * PAIRS
-H_ROWS_B1 = H_ROWS_A1 + 2 * R
-PAGE_3 = H_ROWS_B1 + 2 * R
-H_GROUPED_B = PAGE_3 + 4 * T - OVERLAP
-WD_CODES_1 = H_GROUPED_B + OVERLAP
+PAGE_3 = H_ROWS_A1 + 2 * R
+FIRST_MESSAGE = PAGE_3
+SECOND_GROUPED_1 = PAGE_3 + 4 * T
+H_GROUPED_B = SECOND_GROUPED_1
+WD_CODES_1 = H_GROUPED_B + 2 * R
 
 
 def tile_list_msg_relu_bias_kernel(
@@ -80,15 +84,15 @@ def tile_list_msg_relu_bias_kernel(
 
         nc.vector.memset(tab_s[:].bitcast(I32), 0)
 
-        def load_w_scales(l, scales, quadrants):
-            for q in quadrants:
+        def load_w_scales(l, scales):
+            for q in PORT_ORDER:
                 nc.sync.dma_start(
                     out=w_s[32 * q : 32 * q + 4, l, :, :].bitcast(I32),
                     in_=scales[:, 4 * q : 4 * q + 4, :].rearrange("a s r -> s a r").bitcast(I32),
                 )
 
-        def load_tab_words(half):
-            columns = slice(half * T // 2, (half + 1) * T // 2)
+        def load_tab_words(first, last):
+            columns = slice(first, last)
             words = tab_words[0, :, columns, :].rearrange("p t b -> p (t b)")
             nc.sync.dma_start(out=tab_w[:, columns].bitcast(I32), in_=words.bitcast(I32))
 
@@ -99,17 +103,17 @@ def tile_list_msg_relu_bias_kernel(
             rows = wd[PASS_ROWS * g : PASS_ROWS * (g + 1), WD_COLS * half : WD_COLS * (half + 1)]
             nc.sync.dma_start(out=raw[:, g], in_=rows.rearrange("(p t) n -> p t n", t=4))
 
+        load_tab_words(0, TAB_FIRST)
         nc.sync.dma_start(lists[0][:], offs)
         nc.sync.dma_start(lists[1][:], offs2)
-        load_tab_words(0)
-        for q in range(QUADRANTS):
+        for q in PORT_ORDER:
             nc.sync.dma_start(
                 out=tab_s[32 * q : 32 * q + 4 * PASSES, :].bitcast(I32),
                 in_=tab_scales[:, 4 * q : 4 * q + 4, :].bitcast(I32),
             )
-        load_tab_words(1)
+        load_tab_words(TAB_FIRST, T)
         nc.sync.dma_start(out=ws_w[:].bitcast(I32), in_=ws_words.rearrange("a p c -> p a c").bitcast(I32))
-        load_w_scales(0, ws_scales, range(QUADRANTS))
+        load_w_scales(0, ws_scales)
         wd_first = sbuf([P, PASSES, 4, WD_COLS], F32, "wd_first")
         load_wt(0)
         load_wd(wd_first, 0, 0)
@@ -133,15 +137,15 @@ def tile_list_msg_relu_bias_kernel(
             return [words[:, l] for l in range(count)]
 
         def pick_scales(picked, l, j0):
-            nc.vector.tensor_copy(picked[:, l, :], tab_s[:].indirect(entries(l, j0, picked.shape[2])))
+            nc.vector.tensor_copy(picked, tab_s[:].indirect(entries(l, j0, picked.shape[1])))
 
-        def scale_planes(picked, j0):
-            moved = sbuf(list(picked.shape), U8, f"moved{j0}")
-            nc.sync.dma_start(
-                out=moved[0:MOVED_ROWS].rearrange("p l j -> p (l j)").bitcast(I32),
-                in_=picked[4 : 4 + MOVED_ROWS].rearrange("p l j -> p (l j)").bitcast(I32),
-            )
-            return [picked, moved]
+        def scale_planes(picked, name):
+            moved = sbuf(list(picked.shape), U8, name)
+            nc.sync.dma_start(out=moved[0:MOVED_ROWS].bitcast(I32), in_=picked[4 : 4 + MOVED_ROWS].bitcast(I32))
+            return [picked[:], moved[:]]
+
+        def columns(planes, first, width):
+            return [plane[:, first : first + width] for plane in planes]
 
         def round_wd(copy, raw, grouped):
             copy(out=grouped.rearrange("p (c i) t -> p c t i", i=4), in_=raw.rearrange("p t (c i) -> p c t i", i=4))
@@ -159,34 +163,31 @@ def tile_list_msg_relu_bias_kernel(
         def first_product(looked_up, col, j0, order, offsets, between):
             words, planes = looked_up
             banks = [[double.tile([P, BANK], F32, name=f"a{g}") for g in range(PASSES)] for block in range(BLOCKS)]
-            rows = []
-            for block, l, a in order:
+            rows = [sbuf([P, PASSES, 2, P, 2], BF16, f"h_rows{j0}_{block}", offsets[block]) for block in range(BLOCKS)]
+            for block, g, l, a in order:
                 c0 = col + P * block
-                for g in range(PASSES):
-                    if l == 0:
-                        w_words = ws_w[:, a, 2 * BANK * g : 2 * BANK * (g + 1)].bitcast(FP4X4)
-                    else:
-                        w_words = wt_w[a][:, 4 * BANK * g : 4 * BANK * (g + 1)].bitcast(FP8X4)
-                    nc.tensor.matmul_mx(
-                        out=banks[block][g][:],
-                        lhsT=words[l][:, a, 2 * c0 : 2 * (c0 + P)].bitcast(FP4X4),
-                        lhsT_scale=planes[a][:, l, c0 : c0 + P],
-                        rhs=w_words,
-                        rhs_scale=w_s[:, l, a, BANK * g : BANK * (g + 1)],
-                        start=(l, a) == (0, 0),
-                        stop=(l, a) == (LISTS - 1, PASSES - 1),
+                if l == 0:
+                    w_words = ws_w[:, a, 2 * BANK * g : 2 * BANK * (g + 1)].bitcast(FP4X4)
+                else:
+                    w_words = wt_w[a][:, 4 * BANK * g : 4 * BANK * (g + 1)].bitcast(FP8X4)
+                last = (l, a) == (LISTS - 1, PASSES - 1)
+                nc.tensor.matmul_mx(
+                    out=banks[block][g][:],
+                    lhsT=words[l][:, a, 2 * c0 : 2 * (c0 + P)].bitcast(FP4X4),
+                    lhsT_scale=planes[l][a][:, c0 : c0 + P],
+                    rhs=w_words,
+                    rhs_scale=w_s[:, l, a, BANK * g : BANK * (g + 1)],
+                    start=(l, a) == (0, 0),
+                    stop=last,
+                )
+                if last:
+                    nc.scalar.activation(
+                        out=rows[block][:, g],
+                        in_=banks[block][g][:].rearrange("p (m u e) -> p u m e", u=2, e=2),
+                        func=ACT.Relu,
                     )
-                if (l, a) == (LISTS - 1, PASSES - 1):
-                    done = sbuf([P, PASSES, 2, P, 2], BF16, f"h_rows{j0}_{block}", offsets[block])
-                    for g in range(PASSES):
-                        nc.scalar.activation(
-                            out=done[:, g],
-                            in_=banks[block][g][:].rearrange("p (m u e) -> p u m e", u=2, e=2),
-                            func=ACT.Relu,
-                        )
-                    rows.append(done)
-                if (block, l, a) in between:
-                    between[block, l, a]()
+                    if (block, g) in between:
+                        between[block, g]()
             return rows
 
         def turn(rows, grouped, col, bank_name):
@@ -241,17 +242,17 @@ def tile_list_msg_relu_bias_kernel(
                 pages[c][:].indirect(entries(1, j0, width)), biased, weight[:, j0 : j0 + width], MULT
             )
 
-        def send(c, j0, chunks, held=False):
-            biased = keep.tile([P, CHUNK * len(chunks)], F32, name=f"biased{c}_{j0}")
+        def send(c, j0, chunks, held=False, offset=None):
+            biased = sbuf([P, CHUNK * len(chunks)], F32, f"biased{c}_{j0}", offset)
             message(c, chunks, biased[:], held)
             scatter(c, j0, biased[:])
 
         def store(c):
             nc.sync.dma_start(out=out[c * P : (c + 1) * P, :], in_=pages[c][:])
 
-        def first_pages(j0, h):
-            for c in range(2):
-                send(c, j0, [h])
+        def first_pages(j0, h, offset=None):
+            send(0, j0, [h], offset=offset)
+            send(1, j0, [h])
 
         j_a, j_b, j_c, j_d = range(0, J, CHUNK)
 
@@ -264,29 +265,30 @@ def tile_list_msg_relu_bias_kernel(
         for c in range(PAGES - 1):
             clear_page()
 
-        picked_a = sbuf([P, LISTS, CHUNK], U8, "picked_a")
-        for l in range(LISTS):
-            pick_scales(picked_a, l, j_a)
-        planes_a = scale_planes(picked_a, j_a)
+        picked_ab = sbuf([P, 2 * CHUNK], U8, "picked_ab")
+        pick_scales(picked_ab[:], 0, j_a)
+        planes_ab = scale_planes(picked_ab, "moved_ab")
+        picked_a = sbuf([P, CHUNK], U8, "picked_a")
+        pick_scales(picked_a[:], 1, j_a)
+        planes_a = [columns(planes_ab, 0, CHUNK), scale_planes(picked_a, "moved_a")]
         pairs_a = [sbuf([P, 1, CHUNK], U32, f"pairs_a{l}", offset) for l, offset in enumerate([PAIRS_A0, PAIRS_A1])]
         for l in range(LISTS):
             pick_words(pairs_a[l][:, 0, :], l, j_a)
         words_a = part(pairs_a[0], "words_a0") + part(pairs_a[1], "words_a1")
-        load_w_scales(1, wt_scales, range(QUADRANTS))
+        load_w_scales(1, wt_scales)
         load_wt(1)
 
-        picked_b = sbuf([P, LISTS, CHUNK], U8, "picked_b", PICKED_B)
-        for l in range(LISTS):
-            pick_scales(picked_b, l, j_b)
-        planes_b = scale_planes(picked_b, j_b)
+        picked_b = sbuf([P, CHUNK], U8, "picked_b", PICKED_B)
+        pick_scales(picked_b[:], 1, j_b)
+        planes_b = [columns(planes_ab, CHUNK, CHUNK), scale_planes(picked_b, "moved_b")]
         load_wd(wd_first, 0, 1)
         pairs_b = sbuf([P, LISTS, CHUNK], U32, "pairs_b", PAIRS_B)
         for l in range(LISTS):
             pick_words(pairs_b[:, l, :], l, j_b)
-        picked_cd = sbuf([P, LISTS, 2 * CHUNK], U8, "picked_cd", PICKED_CD)
-        pick_scales(picked_cd, 0, j_c)
+        picked_cd = sbuf([P, LISTS * 2 * CHUNK], U8, "picked_cd", PICKED_CD)
+        pick_scales(picked_cd[:, : 2 * CHUNK], 0, j_c)
         words_b = part(pairs_b, "words_b")
-        pick_scales(picked_cd, 1, j_c)
+        pick_scales(picked_cd[:, 2 * CHUNK :], 1, j_c)
 
         late = sbuf([P, (RAW + 4 * J) // 4], F32, "late_loads", LATE_LOADS)
         wd_second = late[:, : RAW // 4].rearrange("p (g t n) -> p g t n", g=PASSES, t=4)
@@ -297,7 +299,8 @@ def tile_list_msg_relu_bias_kernel(
             nc.sync.dma_start(out=bias[:], in_=b.rearrange("(c p) -> p c", p=P))
         nc.sync.dma_start(out=weight, in_=wgo)
         load_wd(wd_second, 1, 1)
-        planes_cd = scale_planes(picked_cd, j_c)
+        both = scale_planes(picked_cd, "moved_cd")
+        planes_cd = [columns(both, 2 * CHUNK * l, 2 * CHUNK) for l in range(LISTS)]
         pairs_cd = sbuf([P, LISTS, 2 * CHUNK], U32, "pairs_cd", PAIRS_CD)
         for l in range(LISTS):
             pick_words(pairs_cd[:, l, :], l, j_c)
@@ -315,22 +318,22 @@ def tile_list_msg_relu_bias_kernel(
         words_cd = part(pairs_cd, "words_cd", H_GROUPED_A)
         second_grouped = [sbuf([P, WD_COLS, 4], BF16, "wd_second_grouped0", H_ROWS_A1)]
         round_wd(nc.scalar.copy, wd_second[:, 0], second_grouped[0][:])
-        sends = {(1, 1, 0): lambda: first_pages(j_a, h_a)}
-        h_b = hidden((words_b, planes_b), 0, j_b, BY_BLOCK, sends, H_GROUPED_B, H_ROWS_B1)
-        clear_page(PAGE_3)
-        second_grouped.append(sbuf([P, WD_COLS, 4], BF16, "wd_second_grouped1", H_ROWS_B1))
-        round_wd(nc.scalar.copy, wd_second[:, 1], second_grouped[1][:])
+        sends = {(0, 1): lambda: [first_pages(j_a, h_a, FIRST_MESSAGE), clear_page(PAGE_3)]}
+        h_b = hidden((words_b, planes_b), 0, j_b, BY_BANK, sends, H_GROUPED_B)
+        second_grouped.append(sbuf([P, WD_COLS, 4], BF16, "wd_second_grouped1", SECOND_GROUPED_1))
+        round_wd(nc.vector.tensor_copy, wd_second[:, 1], second_grouped[1][:])
         codes, scales = wd_tiles(WD_CODES_1)
         for g in range(PASSES):
             quantise(codes[:, g, :], scales[:, g, :], second_grouped[g][:].rearrange("p n t -> p (n t)"))
 
-        sends = {(1, 0, 0): lambda: first_pages(j_b, h_b), (1, 1, 1): lambda: send(2, j_a, [h_a, h_b])}
-        h_c = hidden((words_cd, planes_cd), 0, j_c, BY_BLOCK, sends)
+        sends = {(0, 1): lambda: first_pages(j_b, h_b), (1, 1): lambda: send(2, j_a, [h_a, h_b])}
+        h_c = hidden((words_cd, planes_cd), 0, j_c, BY_BANK, sends)
         send(3, j_a, [h_a, h_b], held=True)
-        h_d = hidden((words_cd, planes_cd), CHUNK, j_d, BY_BLOCK, {(1, 1, 1): lambda: first_pages(j_c, h_c)})
-        send(2, j_c, [h_c], held=True)
-        for c in range(PAGES - 1):
+        h_d = hidden((words_cd, planes_cd), CHUNK, j_d, BY_BANK, {(1, 1): lambda: send(0, j_c, [h_c])})
+        send(1, j_c, [h_c], held=True)
+        for c in range(2):
             send(c, j_d, [h_d])
             store(c)
-        send(3, j_c, [h_c, h_d])
-        store(3)
+        for c in range(2, PAGES):
+            send(c, j_c, [h_c, h_d])
+            store(c)

@@ -52,9 +52,9 @@ PICKED_B = PAIRS_A0
 PICKED_CD = PICKED_B + CHUNK
 H_GROUPED_A = PICKED_CD + PAIRS
 H_ROWS_A1 = H_GROUPED_A + 4 * PAIRS
-PAGE_3 = H_ROWS_A1 + 2 * R
-FIRST_MESSAGE = PAGE_3
-SECOND_GROUPED_1 = PAGE_3 + 4 * T
+PAGE_3 = H_ROWS_A1
+H_ROWS_B0 = PAGE_3 + 4 * T
+SECOND_GROUPED_1 = H_ROWS_B0 + 2 * R
 H_GROUPED_B = SECOND_GROUPED_1
 WD_CODES_1 = H_GROUPED_B + 2 * R
 
@@ -116,7 +116,7 @@ def tile_list_msg_relu_bias_kernel(
         load_w_scales(0, ws_scales)
         wd_first = sbuf([P, PASSES, 4, WD_COLS], F32, "wd_first")
         load_wt(0)
-        load_wd(wd_first, 0, 0)
+        load_w_scales(1, wt_scales)
 
         narrow = keep.tile([P, P], BF16, name="narrow")
         make_identity(nc, narrow[:])
@@ -202,9 +202,9 @@ def tile_list_msg_relu_bias_kernel(
                 in_=turned[:].rearrange("p g u j -> p g j u"),
             )
 
-        def hidden(looked_up, col, j0, order, between, grouped_offset=None, last_rows_offset=None):
+        def hidden(looked_up, col, j0, order, between, grouped_offset=None, rows_offsets=(None, None)):
             grouped = sbuf([P, PASSES, CHUNK, 4], BF16, f"h_grouped{j0}", grouped_offset)
-            first_rows, last_rows = first_product(looked_up, col, j0, order, [None, last_rows_offset], between)
+            first_rows, last_rows = first_product(looked_up, col, j0, order, rows_offsets, between)
             turn(first_rows, grouped, 0, "early")
             turn(last_rows, grouped, P, "late")
             codes = sbuf([P, PASSES, CHUNK], U32, f"h_codes{j0}")
@@ -242,17 +242,17 @@ def tile_list_msg_relu_bias_kernel(
                 pages[c][:].indirect(entries(1, j0, width)), biased, weight[:, j0 : j0 + width], MULT
             )
 
-        def send(c, j0, chunks, held=False, offset=None):
-            biased = sbuf([P, CHUNK * len(chunks)], F32, f"biased{c}_{j0}", offset)
+        def send(c, j0, chunks, held=False):
+            biased = sbuf([P, CHUNK * len(chunks)], F32, f"biased{c}_{j0}")
             message(c, chunks, biased[:], held)
             scatter(c, j0, biased[:])
 
         def store(c):
             nc.sync.dma_start(out=out[c * P : (c + 1) * P, :], in_=pages[c][:])
 
-        def first_pages(j0, h, offset=None):
-            send(0, j0, [h], offset=offset)
-            send(1, j0, [h])
+        def first_pages(j0, h):
+            for c in range(2):
+                send(c, j0, [h])
 
         j_a, j_b, j_c, j_d = range(0, J, CHUNK)
 
@@ -265,18 +265,17 @@ def tile_list_msg_relu_bias_kernel(
         for c in range(PAGES - 1):
             clear_page()
 
-        picked_ab = sbuf([P, 2 * CHUNK], U8, "picked_ab")
-        pick_scales(picked_ab[:], 0, j_a)
+        picked_ab = sbuf([P, 3 * CHUNK], U8, "picked_ab")
+        pick_scales(picked_ab[:, : 2 * CHUNK], 0, j_a)
+        pick_scales(picked_ab[:, 2 * CHUNK :], 1, j_a)
         planes_ab = scale_planes(picked_ab, "moved_ab")
-        picked_a = sbuf([P, CHUNK], U8, "picked_a")
-        pick_scales(picked_a[:], 1, j_a)
-        planes_a = [columns(planes_ab, 0, CHUNK), scale_planes(picked_a, "moved_a")]
+        planes_a = [columns(planes_ab, 0, CHUNK), columns(planes_ab, 2 * CHUNK, CHUNK)]
         pairs_a = [sbuf([P, 1, CHUNK], U32, f"pairs_a{l}", offset) for l, offset in enumerate([PAIRS_A0, PAIRS_A1])]
         for l in range(LISTS):
             pick_words(pairs_a[l][:, 0, :], l, j_a)
         words_a = part(pairs_a[0], "words_a0") + part(pairs_a[1], "words_a1")
-        load_w_scales(1, wt_scales)
         load_wt(1)
+        load_wd(wd_first, 0, 0)
 
         picked_b = sbuf([P, CHUNK], U8, "picked_b", PICKED_B)
         pick_scales(picked_b[:], 1, j_b)
@@ -304,7 +303,10 @@ def tile_list_msg_relu_bias_kernel(
         pairs_cd = sbuf([P, LISTS, 2 * CHUNK], U32, "pairs_cd", PAIRS_CD)
         for l in range(LISTS):
             pick_words(pairs_cd[:, l, :], l, j_c)
-        grouped = sbuf([P, PASSES, WD_COLS, 4], BF16, "wd_grouped")
+
+        h_a = hidden((words_a, planes_a), 0, j_a, PASS_0_FIRST, {}, H_GROUPED_A, (None, H_ROWS_A1))
+        words_cd = part(pairs_cd, "words_cd", H_GROUPED_A)
+        grouped = sbuf([P, PASSES, WD_COLS, 4], BF16, "wd_grouped", H_ROWS_A1)
         round_wd(nc.scalar.copy, wd_first[:, 0], grouped[:, 0])
         round_wd(nc.vector.tensor_copy, wd_first[:, 1], grouped[:, 1])
         codes, scales = wd_tiles()
@@ -313,13 +315,11 @@ def tile_list_msg_relu_bias_kernel(
             scales[:].rearrange("p g n -> p (g n)"),
             grouped[:].rearrange("p g n t -> p (g n t)"),
         )
-
-        h_a = hidden((words_a, planes_a), 0, j_a, PASS_0_FIRST, {}, H_GROUPED_A, H_ROWS_A1)
-        words_cd = part(pairs_cd, "words_cd", H_GROUPED_A)
-        second_grouped = [sbuf([P, WD_COLS, 4], BF16, "wd_second_grouped0", H_ROWS_A1)]
+        clear_page(PAGE_3)
+        sends = {(1, 0): lambda: first_pages(j_a, h_a)}
+        h_b = hidden((words_b, planes_b), 0, j_b, BY_BANK, sends, H_GROUPED_B, (H_ROWS_B0, None))
+        second_grouped = [sbuf([P, WD_COLS, 4], BF16, "wd_second_grouped0", H_ROWS_B0)]
         round_wd(nc.scalar.copy, wd_second[:, 0], second_grouped[0][:])
-        sends = {(0, 1): lambda: [first_pages(j_a, h_a, FIRST_MESSAGE), clear_page(PAGE_3)]}
-        h_b = hidden((words_b, planes_b), 0, j_b, BY_BANK, sends, H_GROUPED_B)
         second_grouped.append(sbuf([P, WD_COLS, 4], BF16, "wd_second_grouped1", SECOND_GROUPED_1))
         round_wd(nc.vector.tensor_copy, wd_second[:, 1], second_grouped[1][:])
         codes, scales = wd_tiles(WD_CODES_1)

@@ -18,7 +18,6 @@ ACT = mybir.ActivationFunctionType
 MULT = mybir.AluOpType.mult
 
 P = 128
-QUADRANTS = 4
 PASS_ROWS = 512
 PASSES = 2
 LISTS = 2
@@ -35,13 +34,14 @@ PASS_0_FIRST = [(block, g, l, 0) for l in range(LISTS) for block, g in BANKS] + 
     (block, g, l, 1) for block, g in BANKS for l in range(LISTS)
 ]
 
+MOVED_ROWS = 100
 TAB_FIRST = T // 4
 PORT_ORDER = [0, 2, 1, 3]
-MOVED_ROWS = 100
 
 OVERLAP = 64
 PAIRS = 4 * CHUNK
 RAW = PASSES * 4 * WD_COLS * 4
+ROWS = 2 * R
 LATE_LOADS = 0
 PAIRS_B = LATE_LOADS + RAW + 4 * J - OVERLAP
 BIAS = PAIRS_B + OVERLAP
@@ -50,13 +50,11 @@ PAIRS_CD = PAIRS_B + 2 * PAIRS - OVERLAP
 PAIRS_A0 = PAIRS_CD + 4 * PAIRS
 PICKED_B = PAIRS_A0
 PICKED_CD = PICKED_B + CHUNK
-H_GROUPED_A = PICKED_CD + PAIRS
-H_ROWS_A1 = H_GROUPED_A + 4 * PAIRS
+H_ROWS_A1 = PICKED_CD + PAIRS
 PAGE_3 = H_ROWS_A1
 H_ROWS_B0 = PAGE_3 + 4 * T
-SECOND_GROUPED_1 = H_ROWS_B0 + 2 * R
-H_GROUPED_B = SECOND_GROUPED_1
-WD_CODES_1 = H_GROUPED_B + 2 * R
+H_GROUPED_B = H_ROWS_B0 + ROWS
+WD_CODES_1 = H_GROUPED_B + ROWS
 
 
 def tile_list_msg_relu_bias_kernel(
@@ -92,16 +90,15 @@ def tile_list_msg_relu_bias_kernel(
                 )
 
         def load_tab_words(first, last):
-            columns = slice(first, last)
-            words = tab_words[0, :, columns, :].rearrange("p t b -> p (t b)")
-            nc.sync.dma_start(out=tab_w[:, columns].bitcast(I32), in_=words.bitcast(I32))
+            source = tab_words[0, :, first:last, :].rearrange("p t b -> p (t b)")
+            nc.sync.dma_start(out=tab_w[:, first:last].bitcast(I32), in_=source.bitcast(I32))
 
         def load_wt(a):
             nc.sync.dma_start(out=wt_w[a][:].bitcast(I32), in_=wt_words[a].rearrange("p r i -> p (r i)").bitcast(I32))
 
         def load_wd(raw, half, g):
-            rows = wd[PASS_ROWS * g : PASS_ROWS * (g + 1), WD_COLS * half : WD_COLS * (half + 1)]
-            nc.sync.dma_start(out=raw[:, g], in_=rows.rearrange("(p t) n -> p t n", t=4))
+            source = wd[PASS_ROWS * g : PASS_ROWS * (g + 1), WD_COLS * half : WD_COLS * (half + 1)]
+            nc.sync.dma_start(out=raw[:, g], in_=source.rearrange("(p t) n -> p t n", t=4))
 
         load_tab_words(0, TAB_FIRST)
         nc.sync.dma_start(lists[0][:], offs)
@@ -128,9 +125,9 @@ def tile_list_msg_relu_bias_kernel(
         def pick_words(pairs, l, j0):
             nc.vector.tensor_copy(pairs, tab_w[:].indirect(entries(l, j0, pairs.shape[1])))
 
-        def part(pairs, name, offset=None):
+        def part(pairs, name):
             count, width = pairs.shape[1:]
-            words = sbuf([P, count, PASSES, 2 * width], U8, name, offset)
+            words = sbuf([P, count, PASSES, 2 * width], U8, name)
             nc.vector.tensor_copy(
                 out=words[:].bitcast(U16), in_=pairs[:].bitcast(U16).rearrange("p l (j a) -> p l a j", a=PASSES)
             )
@@ -191,12 +188,12 @@ def tile_list_msg_relu_bias_kernel(
             return rows
 
         def turn(rows, grouped, col, bank_name):
-            words = rows[:].rearrange("p g u m e -> p (g u m e)").bitcast(F32)
+            h_pairs = rows[:].rearrange("p g u m e -> p (g u m e)").bitcast(F32)
             turned = single.tile([P, PASSES, 2, P], F32, name=bank_name)
             for g in range(PASSES):
                 for u in range(2):
                     w0 = (2 * g + u) * P
-                    nc.tensor.transpose(turned[:, g, u, :], words[:, w0 : w0 + P], ident[:])
+                    nc.tensor.transpose(turned[:, g, u, :], h_pairs[:, w0 : w0 + P], ident[:])
             nc.scalar.copy(
                 out=grouped[:].bitcast(F32)[:, :, col : col + P, :],
                 in_=turned[:].rearrange("p g u j -> p g j u"),
@@ -250,7 +247,7 @@ def tile_list_msg_relu_bias_kernel(
         def store(c):
             nc.sync.dma_start(out=out[c * P : (c + 1) * P, :], in_=pages[c][:])
 
-        def first_pages(j0, h):
+        def send_first_pages(j0, h):
             for c in range(2):
                 send(c, j0, [h])
 
@@ -289,47 +286,48 @@ def tile_list_msg_relu_bias_kernel(
         words_b = part(pairs_b, "words_b")
         pick_scales(picked_cd[:, 2 * CHUNK :], 1, j_c)
 
-        late = sbuf([P, (RAW + 4 * J) // 4], F32, "late_loads", LATE_LOADS)
-        wd_second = late[:, : RAW // 4].rearrange("p (g t n) -> p g t n", g=PASSES, t=4)
-        weight = late[:, RAW // 4 :]
+        late_loads = sbuf([P, (RAW + 4 * J) // 4], F32, "late_loads", LATE_LOADS)
+        wd_second = late_loads[:, : RAW // 4].rearrange("p (g t n) -> p g t n", g=PASSES, t=4)
+        weight = late_loads[:, RAW // 4 :]
         load_wd(wd_second, 1, 0)
         bias = sbuf([P, PAGES], F32, "bias", BIAS)
         with nc.allow_non_contiguous_dma(reason="one bias value a partition and page"):
             nc.sync.dma_start(out=bias[:], in_=b.rearrange("(c p) -> p c", p=P))
         nc.sync.dma_start(out=weight, in_=wgo)
         load_wd(wd_second, 1, 1)
-        both = scale_planes(picked_cd, "moved_cd")
-        planes_cd = [columns(both, 2 * CHUNK * l, 2 * CHUNK) for l in range(LISTS)]
+        both_lists = scale_planes(picked_cd, "moved_cd")
+        planes_cd = [columns(both_lists, 2 * CHUNK * l, 2 * CHUNK) for l in range(LISTS)]
         pairs_cd = sbuf([P, LISTS, 2 * CHUNK], U32, "pairs_cd", PAIRS_CD)
         for l in range(LISTS):
             pick_words(pairs_cd[:, l, :], l, j_c)
+        words_cd = part(pairs_cd, "words_cd")
 
-        h_a = hidden((words_a, planes_a), 0, j_a, PASS_0_FIRST, {}, H_GROUPED_A, (None, H_ROWS_A1))
-        words_cd = part(pairs_cd, "words_cd", H_GROUPED_A)
-        grouped = sbuf([P, PASSES, WD_COLS, 4], BF16, "wd_grouped", H_ROWS_A1)
-        round_wd(nc.scalar.copy, wd_first[:, 0], grouped[:, 0])
-        round_wd(nc.vector.tensor_copy, wd_first[:, 1], grouped[:, 1])
-        codes, scales = wd_tiles()
+        h_a = hidden((words_a, planes_a), 0, j_a, PASS_0_FIRST, {}, None, (None, H_ROWS_A1))
+        first_grouped = sbuf([P, PASSES, WD_COLS, 4], BF16, "wd_grouped", H_ROWS_A1)
+        round_wd(nc.scalar.copy, wd_first[:, 0], first_grouped[:, 0])
+        round_wd(nc.vector.tensor_copy, wd_first[:, 1], first_grouped[:, 1])
+        first_codes, first_scales = wd_tiles()
         quantise(
-            codes[:].rearrange("p g n -> p (g n)"),
-            scales[:].rearrange("p g n -> p (g n)"),
-            grouped[:].rearrange("p g n t -> p (g n t)"),
+            first_codes[:].rearrange("p g n -> p (g n)"),
+            first_scales[:].rearrange("p g n -> p (g n)"),
+            first_grouped[:].rearrange("p g n t -> p (g n t)"),
         )
         clear_page(PAGE_3)
-        sends = {(1, 0): lambda: first_pages(j_a, h_a)}
-        h_b = hidden((words_b, planes_b), 0, j_b, BY_BANK, sends, H_GROUPED_B, (H_ROWS_B0, None))
+        among_b = {(1, 0): lambda: send_first_pages(j_a, h_a)}
+        h_b = hidden((words_b, planes_b), 0, j_b, BY_BANK, among_b, H_GROUPED_B, (H_ROWS_B0, None))
         second_grouped = [sbuf([P, WD_COLS, 4], BF16, "wd_second_grouped0", H_ROWS_B0)]
         round_wd(nc.scalar.copy, wd_second[:, 0], second_grouped[0][:])
-        second_grouped.append(sbuf([P, WD_COLS, 4], BF16, "wd_second_grouped1", SECOND_GROUPED_1))
+        second_grouped.append(sbuf([P, WD_COLS, 4], BF16, "wd_second_grouped1", H_GROUPED_B))
         round_wd(nc.vector.tensor_copy, wd_second[:, 1], second_grouped[1][:])
-        codes, scales = wd_tiles(WD_CODES_1)
+        second_codes, second_scales = wd_tiles(WD_CODES_1)
         for g in range(PASSES):
-            quantise(codes[:, g, :], scales[:, g, :], second_grouped[g][:].rearrange("p n t -> p (n t)"))
+            quantise(second_codes[:, g, :], second_scales[:, g, :], second_grouped[g][:].rearrange("p n t -> p (n t)"))
 
-        sends = {(0, 1): lambda: first_pages(j_b, h_b), (1, 1): lambda: send(2, j_a, [h_a, h_b])}
-        h_c = hidden((words_cd, planes_cd), 0, j_c, BY_BANK, sends)
+        among_c = {(0, 1): lambda: send_first_pages(j_b, h_b), (1, 1): lambda: send(2, j_a, [h_a, h_b])}
+        h_c = hidden((words_cd, planes_cd), 0, j_c, BY_BANK, among_c)
         send(3, j_a, [h_a, h_b], held=True)
-        h_d = hidden((words_cd, planes_cd), CHUNK, j_d, BY_BANK, {(1, 1): lambda: send(0, j_c, [h_c])})
+        among_d = {(1, 1): lambda: send(0, j_c, [h_c])}
+        h_d = hidden((words_cd, planes_cd), CHUNK, j_d, BY_BANK, among_d)
         send(1, j_c, [h_c], held=True)
         for c in range(2):
             send(c, j_d, [h_d])

@@ -33,7 +33,9 @@ BY_BANK = [(block, g, l, a) for block, g in BANKS for a in range(PASSES) for l i
 PASS_0_FIRST = [(block, g, l, 0) for l in range(LISTS) for block, g in BANKS] + [
     (block, g, l, 1) for block, g in BANKS for l in range(LISTS)
 ]
+LATE_PLANE = [(0, g, l, a) for a in range(PASSES) for g in range(PASSES) for l in range(LISTS)] + BY_BANK[8:]
 
+PASS_1_ROW = 16
 MOVED_ROWS = 100
 TAB_FIRST = T // 4
 PORT_ORDER = [0, 2, 1, 3]
@@ -48,9 +50,8 @@ BIAS = PAIRS_B + OVERLAP
 PAIRS_A1 = BIAS + OVERLAP
 PAIRS_CD = PAIRS_B + 2 * PAIRS - OVERLAP
 PAIRS_A0 = PAIRS_CD + 4 * PAIRS
-PICKED_B = PAIRS_A0
-PICKED_CD = PICKED_B + CHUNK
-H_ROWS_A1 = PICKED_CD + PAIRS
+PICKED_REST = PAIRS_A0
+H_ROWS_A1 = PICKED_REST + 2 * PAIRS
 PAGE_3 = H_ROWS_A1
 H_ROWS_B0 = PAGE_3 + 4 * T
 H_GROUPED_B = H_ROWS_B0 + ROWS
@@ -103,10 +104,10 @@ def tile_list_msg_relu_bias_kernel(
         load_tab_words(0, TAB_FIRST)
         nc.sync.dma_start(lists[0][:], offs)
         nc.sync.dma_start(lists[1][:], offs2)
-        for q in PORT_ORDER:
+        for s in range(4):
             nc.sync.dma_start(
-                out=tab_s[32 * q : 32 * q + 4 * PASSES, :].bitcast(I32),
-                in_=tab_scales[:, 4 * q : 4 * q + 4, :].bitcast(I32),
+                out=tab_s[s:P:PASS_1_ROW, :].bitcast(I32),
+                in_=tab_scales[:, s:16:4, :].rearrange("a q t -> q a t").bitcast(I32),
             )
         load_tab_words(TAB_FIRST, T)
         nc.sync.dma_start(out=ws_w[:].bitcast(I32), in_=ws_words.rearrange("a p c -> p a c").bitcast(I32))
@@ -138,7 +139,7 @@ def tile_list_msg_relu_bias_kernel(
 
         def scale_planes(picked, name):
             moved = sbuf(list(picked.shape), U8, name)
-            nc.sync.dma_start(out=moved[0:MOVED_ROWS].bitcast(I32), in_=picked[4 : 4 + MOVED_ROWS].bitcast(I32))
+            nc.sync.dma_start(out=moved[0:MOVED_ROWS].bitcast(I32), in_=picked[PASS_1_ROW : PASS_1_ROW + MOVED_ROWS].bitcast(I32))
             return [picked[:], moved[:]]
 
         def columns(planes, first, width):
@@ -262,29 +263,29 @@ def tile_list_msg_relu_bias_kernel(
         for c in range(PAGES - 1):
             clear_page()
 
-        picked_ab = sbuf([P, 3 * CHUNK], U8, "picked_ab")
-        pick_scales(picked_ab[:, : 2 * CHUNK], 0, j_a)
-        pick_scales(picked_ab[:, 2 * CHUNK :], 1, j_a)
-        planes_ab = scale_planes(picked_ab, "moved_ab")
-        planes_a = [columns(planes_ab, 0, CHUNK), columns(planes_ab, 2 * CHUNK, CHUNK)]
+        def look_up_scales(j0, width, name, offset=None):
+            picked = sbuf([P, LISTS * width], U8, f"picked_{name}", offset)
+            for l in range(LISTS):
+                pick_scales(picked[:, width * l : width * (l + 1)], l, j0)
+            both = scale_planes(picked, f"moved_{name}")
+            return [columns(both, width * l, width) for l in range(LISTS)]
+
+        planes_a = look_up_scales(j_a, CHUNK, "a")
         pairs_a = [sbuf([P, 1, CHUNK], U32, f"pairs_a{l}", offset) for l, offset in enumerate([PAIRS_A0, PAIRS_A1])]
         for l in range(LISTS):
             pick_words(pairs_a[l][:, 0, :], l, j_a)
         words_a = part(pairs_a[0], "words_a0") + part(pairs_a[1], "words_a1")
         load_wt(1)
-        load_wd(wd_first, 0, 0)
+        for g in range(PASSES):
+            load_wd(wd_first, 0, g)
 
-        picked_b = sbuf([P, CHUNK], U8, "picked_b", PICKED_B)
-        pick_scales(picked_b[:], 1, j_b)
-        planes_b = [columns(planes_ab, CHUNK, CHUNK), scale_planes(picked_b, "moved_b")]
-        load_wd(wd_first, 0, 1)
         pairs_b = sbuf([P, LISTS, CHUNK], U32, "pairs_b", PAIRS_B)
         for l in range(LISTS):
             pick_words(pairs_b[:, l, :], l, j_b)
-        picked_cd = sbuf([P, LISTS * 2 * CHUNK], U8, "picked_cd", PICKED_CD)
-        pick_scales(picked_cd[:, : 2 * CHUNK], 0, j_c)
+        planes_rest = look_up_scales(j_b, J - CHUNK, "rest", PICKED_REST)
         words_b = part(pairs_b, "words_b")
-        pick_scales(picked_cd[:, 2 * CHUNK :], 1, j_c)
+        planes_b = [[plane[:, :CHUNK] for plane in planes] for planes in planes_rest]
+        planes_cd = [[plane[:, CHUNK:] for plane in planes] for planes in planes_rest]
 
         late_loads = sbuf([P, (RAW + 4 * J) // 4], F32, "late_loads", LATE_LOADS)
         wd_second = late_loads[:, : RAW // 4].rearrange("p (g t n) -> p g t n", g=PASSES, t=4)
@@ -295,8 +296,6 @@ def tile_list_msg_relu_bias_kernel(
             nc.sync.dma_start(out=bias[:], in_=b.rearrange("(c p) -> p c", p=P))
         nc.sync.dma_start(out=weight, in_=wgo)
         load_wd(wd_second, 1, 1)
-        both_lists = scale_planes(picked_cd, "moved_cd")
-        planes_cd = [columns(both_lists, 2 * CHUNK * l, 2 * CHUNK) for l in range(LISTS)]
         pairs_cd = sbuf([P, LISTS, 2 * CHUNK], U32, "pairs_cd", PAIRS_CD)
         for l in range(LISTS):
             pick_words(pairs_cd[:, l, :], l, j_c)
@@ -314,7 +313,7 @@ def tile_list_msg_relu_bias_kernel(
         )
         clear_page(PAGE_3)
         among_b = {(1, 0): lambda: send_first_pages(j_a, h_a)}
-        h_b = hidden((words_b, planes_b), 0, j_b, BY_BANK, among_b, H_GROUPED_B, (H_ROWS_B0, None))
+        h_b = hidden((words_b, planes_b), 0, j_b, LATE_PLANE, among_b, H_GROUPED_B, (H_ROWS_B0, None))
         second_grouped = [sbuf([P, WD_COLS, 4], BF16, "wd_second_grouped0", H_ROWS_B0)]
         round_wd(nc.scalar.copy, wd_second[:, 0], second_grouped[0][:])
         second_grouped.append(sbuf([P, WD_COLS, 4], BF16, "wd_second_grouped1", H_GROUPED_B))

@@ -47,11 +47,11 @@ ROWS = 2 * R
 LATE_LOADS = 0
 PAIRS_B = LATE_LOADS + RAW + 4 * J - OVERLAP
 BIAS = PAIRS_B + OVERLAP
-PAIRS_A1 = BIAS + OVERLAP
-PAIRS_CD = PAIRS_B + 2 * PAIRS - OVERLAP
-PAIRS_A0 = PAIRS_CD + 4 * PAIRS
-PICKED_REST = PAIRS_A0
-H_ROWS_A1 = PICKED_REST + 2 * PAIRS
+PAIRS_A0 = PAIRS_B + 2 * PAIRS - OVERLAP
+PICKED_REST = PAIRS_A0 + OVERLAP
+PAIRS_A1 = PICKED_REST + 2 * PAIRS
+PAIRS_CD = PAIRS_A1
+H_ROWS_A1 = PAIRS_A1 + 4 * PAIRS
 PAGE_3 = H_ROWS_A1
 H_ROWS_B0 = PAGE_3 + 4 * T
 H_GROUPED_B = H_ROWS_B0 + ROWS
@@ -130,7 +130,7 @@ def tile_list_msg_relu_bias_kernel(
             count, width = pairs.shape[1:]
             words = sbuf([P, count, PASSES, 2 * width], U8, name)
             nc.vector.tensor_copy(
-                out=words[:].bitcast(U16), in_=pairs[:].bitcast(U16).rearrange("p l (j a) -> p l a j", a=PASSES)
+                out=words[:].bitcast(U16), in_=pairs.bitcast(U16).rearrange("p l (j a) -> p l a j", a=PASSES)
             )
             return [words[:, l] for l in range(count)]
 
@@ -274,7 +274,7 @@ def tile_list_msg_relu_bias_kernel(
         pairs_a = [sbuf([P, 1, CHUNK], U32, f"pairs_a{l}", offset) for l, offset in enumerate([PAIRS_A0, PAIRS_A1])]
         for l in range(LISTS):
             pick_words(pairs_a[l][:, 0, :], l, j_a)
-        words_a = part(pairs_a[0], "words_a0") + part(pairs_a[1], "words_a1")
+        words_a = part(pairs_a[0][:], "words_a0") + part(pairs_a[1][:], "words_a1")
         load_wt(1)
         for g in range(PASSES):
             load_wd(wd_first, 0, g)
@@ -283,7 +283,7 @@ def tile_list_msg_relu_bias_kernel(
         for l in range(LISTS):
             pick_words(pairs_b[:, l, :], l, j_b)
         planes_rest = look_up_scales(j_b, J - CHUNK, "rest", PICKED_REST)
-        words_b = part(pairs_b, "words_b")
+        words_b = part(pairs_b[:], "words_b")
         planes_b = [[plane[:, :CHUNK] for plane in planes] for planes in planes_rest]
         planes_cd = [[plane[:, CHUNK:] for plane in planes] for planes in planes_rest]
 
@@ -299,7 +299,7 @@ def tile_list_msg_relu_bias_kernel(
         pairs_cd = sbuf([P, LISTS, 2 * CHUNK], U32, "pairs_cd", PAIRS_CD)
         for l in range(LISTS):
             pick_words(pairs_cd[:, l, :], l, j_c)
-        words_cd = part(pairs_cd, "words_cd")
+        words_cd = part(pairs_cd[:, 0:1], "words_cd0") + part(pairs_cd[:, 1:2], "words_cd1")
 
         h_a = hidden((words_a, planes_a), 0, j_a, PASS_0_FIRST, {}, None, (None, H_ROWS_A1))
         first_grouped = sbuf([P, PASSES, WD_COLS, 4], BF16, "wd_grouped", H_ROWS_A1)

@@ -1,7 +1,6 @@
 from contextlib import ExitStack
 
 import concourse.mybir as mybir
-from concourse.masks import make_identity
 
 K, R, N, T, J = 1024, 1024, 512, 2048, 1024
 FLOPS = 2 * 2 * K * R * J + 2 * R * N * J
@@ -42,20 +41,22 @@ PORT_ORDER = [0, 2, 1, 3]
 
 OVERLAP = 64
 PAIRS = 4 * CHUNK
-RAW = PASSES * 4 * WD_COLS * 4
+RAW = 4 * WD_COLS * 4
 ROWS = 2 * R
 LATE_LOADS = 0
 PAIRS_B = LATE_LOADS + RAW + 4 * J - OVERLAP
 BIAS = PAIRS_B + OVERLAP
-PAIRS_A0 = PAIRS_B + 2 * PAIRS - OVERLAP
-PICKED_REST = PAIRS_A0 + OVERLAP
-PAIRS_A1 = PICKED_REST + 2 * PAIRS
-PAIRS_CD = PAIRS_A1
-H_ROWS_A1 = PAIRS_A1 + 4 * PAIRS
-PAGE_3 = H_ROWS_A1
-H_ROWS_B0 = PAGE_3 + 4 * T
-H_GROUPED_B = H_ROWS_B0 + ROWS
-WD_CODES_1 = H_GROUPED_B + ROWS
+PAIRS_A0 = BIAS + OVERLAP
+SECOND_RAW_0 = PAIRS_B + 2 * PAIRS - OVERLAP
+SECOND_GROUPED_1 = SECOND_RAW_0
+SECOND_CODES = SECOND_RAW_0 + ROWS
+PICKED_REST = SECOND_RAW_0 + RAW
+PAIRS_A1 = PICKED_REST + LISTS * (J - CHUNK) - OVERLAP
+PAIRS_CD = PAIRS_A1 + PAIRS - OVERLAP
+H_ROWS_A1 = PAIRS_CD + 4 * PAIRS
+FIRST_RAW_0 = H_ROWS_A1 + 2 * ROWS
+PAGE_3 = FIRST_RAW_0
+H_ROWS_B = [PAGE_3 + 4 * T, PAGE_3 + 4 * T + ROWS]
 
 
 def tile_list_msg_relu_bias_kernel(
@@ -99,7 +100,7 @@ def tile_list_msg_relu_bias_kernel(
 
         def load_wd(raw, half, g):
             source = wd[PASS_ROWS * g : PASS_ROWS * (g + 1), WD_COLS * half : WD_COLS * (half + 1)]
-            nc.sync.dma_start(out=raw[:, g], in_=source.rearrange("(p t) n -> p t n", t=4))
+            nc.sync.dma_start(out=raw, in_=source.rearrange("(p t) n -> p t n", t=4))
 
         load_tab_words(0, TAB_FIRST)
         nc.sync.dma_start(lists[0][:], offs)
@@ -112,13 +113,17 @@ def tile_list_msg_relu_bias_kernel(
         load_tab_words(TAB_FIRST, T)
         nc.sync.dma_start(out=ws_w[:].bitcast(I32), in_=ws_words.rearrange("a p c -> p a c").bitcast(I32))
         load_w_scales(0, ws_scales)
-        wd_first = sbuf([P, PASSES, 4, WD_COLS], F32, "wd_first")
+        wd_first = [sbuf([P, 4, WD_COLS], F32, f"wd_first{g}", offset) for g, offset in enumerate([FIRST_RAW_0, None])]
         load_wt(0)
         load_w_scales(1, wt_scales)
 
-        narrow = keep.tile([P, P], BF16, name="narrow")
-        make_identity(nc, narrow[:])
-        nc.scalar.activation(out=ident[:], in_=narrow[:], func=ACT.Identity)
+        distance = keep.tile([P, P], F32, name="distance")
+        squared = keep.tile([P, P], F32, name="squared")
+        nc.gpsimd.iota(
+            distance[:], pattern=[[1, P]], base=0, channel_multiplier=-1, allow_small_or_imprecise_dtypes=True
+        )
+        nc.scalar.activation(out=squared[:], in_=distance[:], func=ACT.Square)
+        nc.scalar.activation(out=ident[:], in_=squared[:], func=ACT.Relu, scale=-1.0, bias=1.0)
 
         def entries(l, j0, width):
             return lists[l][:, j0 // PER_COLUMN : (j0 + width) // PER_COLUMN]
@@ -200,8 +205,8 @@ def tile_list_msg_relu_bias_kernel(
                 in_=turned[:].rearrange("p g u j -> p g j u"),
             )
 
-        def hidden(looked_up, col, j0, order, between, grouped_offset=None, rows_offsets=(None, None)):
-            grouped = sbuf([P, PASSES, CHUNK, 4], BF16, f"h_grouped{j0}", grouped_offset)
+        def hidden(looked_up, col, j0, order, between, rows_offsets=(None, None)):
+            grouped = sbuf([P, PASSES, CHUNK, 4], BF16, f"h_grouped{j0}")
             first_rows, last_rows = first_product(looked_up, col, j0, order, rows_offsets, between)
             turn(first_rows, grouped, 0, "early")
             turn(last_rows, grouped, P, "late")
@@ -277,7 +282,7 @@ def tile_list_msg_relu_bias_kernel(
         words_a = part(pairs_a[0][:], "words_a0") + part(pairs_a[1][:], "words_a1")
         load_wt(1)
         for g in range(PASSES):
-            load_wd(wd_first, 0, g)
+            load_wd(wd_first[g][:], 0, g)
 
         pairs_b = sbuf([P, LISTS, CHUNK], U32, "pairs_b", PAIRS_B)
         for l in range(LISTS):
@@ -288,23 +293,24 @@ def tile_list_msg_relu_bias_kernel(
         planes_cd = [[plane[:, CHUNK:] for plane in planes] for planes in planes_rest]
 
         late_loads = sbuf([P, (RAW + 4 * J) // 4], F32, "late_loads", LATE_LOADS)
-        wd_second = late_loads[:, : RAW // 4].rearrange("p (g t n) -> p g t n", g=PASSES, t=4)
+        second_raw_0 = sbuf([P, 4, WD_COLS], F32, "second_raw_0", SECOND_RAW_0)
+        second_raw_1 = late_loads[:, : RAW // 4].rearrange("p (t n) -> p t n", t=4)
         weight = late_loads[:, RAW // 4 :]
-        load_wd(wd_second, 1, 0)
+        load_wd(second_raw_0[:], 1, 0)
         bias = sbuf([P, PAGES], F32, "bias", BIAS)
         with nc.allow_non_contiguous_dma(reason="one bias value a partition and page"):
             nc.sync.dma_start(out=bias[:], in_=b.rearrange("(c p) -> p c", p=P))
         nc.sync.dma_start(out=weight, in_=wgo)
-        load_wd(wd_second, 1, 1)
+        load_wd(second_raw_1, 1, 1)
         pairs_cd = sbuf([P, LISTS, 2 * CHUNK], U32, "pairs_cd", PAIRS_CD)
         for l in range(LISTS):
             pick_words(pairs_cd[:, l, :], l, j_c)
         words_cd = part(pairs_cd[:, 0:1], "words_cd0") + part(pairs_cd[:, 1:2], "words_cd1")
 
-        h_a = hidden((words_a, planes_a), 0, j_a, PASS_0_FIRST, {}, None, (None, H_ROWS_A1))
+        h_a = hidden((words_a, planes_a), 0, j_a, PASS_0_FIRST, {}, (None, H_ROWS_A1))
         first_grouped = sbuf([P, PASSES, WD_COLS, 4], BF16, "wd_grouped", H_ROWS_A1)
-        round_wd(nc.scalar.copy, wd_first[:, 0], first_grouped[:, 0])
-        round_wd(nc.vector.tensor_copy, wd_first[:, 1], first_grouped[:, 1])
+        round_wd(nc.scalar.copy, wd_first[0][:], first_grouped[:, 0])
+        round_wd(nc.vector.tensor_copy, wd_first[1][:], first_grouped[:, 1])
         first_codes, first_scales = wd_tiles()
         quantise(
             first_codes[:].rearrange("p g n -> p (g n)"),
@@ -313,14 +319,19 @@ def tile_list_msg_relu_bias_kernel(
         )
         clear_page(PAGE_3)
         among_b = {(1, 0): lambda: send_first_pages(j_a, h_a)}
-        h_b = hidden((words_b, planes_b), 0, j_b, LATE_PLANE, among_b, H_GROUPED_B, (H_ROWS_B0, None))
-        second_grouped = [sbuf([P, WD_COLS, 4], BF16, "wd_second_grouped0", H_ROWS_B0)]
-        round_wd(nc.scalar.copy, wd_second[:, 0], second_grouped[0][:])
-        second_grouped.append(sbuf([P, WD_COLS, 4], BF16, "wd_second_grouped1", H_GROUPED_B))
-        round_wd(nc.vector.tensor_copy, wd_second[:, 1], second_grouped[1][:])
-        second_codes, second_scales = wd_tiles(WD_CODES_1)
-        for g in range(PASSES):
-            quantise(second_codes[:, g, :], second_scales[:, g, :], second_grouped[g][:].rearrange("p n t -> p (n t)"))
+        h_b = hidden((words_b, planes_b), 0, j_b, LATE_PLANE, among_b, H_ROWS_B)
+        pieces = []
+        for block in range(BLOCKS):
+            grouped = sbuf([P, P, 4], BF16, f"second_grouped_0{block}", H_ROWS_B[block])
+            round_wd(nc.scalar.copy, second_raw_0[:, :, P * block : P * (block + 1)], grouped[:])
+            pieces.append((grouped, 0, P * block))
+        grouped = sbuf([P, WD_COLS, 4], BF16, "second_grouped_1", SECOND_GROUPED_1)
+        round_wd(nc.vector.tensor_copy, second_raw_1, grouped[:])
+        pieces.append((grouped, 1, 0))
+        second_codes, second_scales = wd_tiles(SECOND_CODES)
+        for grouped, g, first in pieces:
+            cols = slice(first, first + grouped.shape[1])
+            quantise(second_codes[:, g, cols], second_scales[:, g, cols], grouped[:].rearrange("p n t -> p (n t)"))
 
         among_c = {(0, 1): lambda: send_first_pages(j_b, h_b), (1, 1): lambda: send(2, j_a, [h_a, h_b])}
         h_c = hidden((words_cd, planes_cd), 0, j_c, BY_BANK, among_c)

@@ -54,8 +54,9 @@ PICKED_REST = SECOND_RAW_0 + RAW
 PAIRS_A1 = PICKED_REST + LISTS * (J - CHUNK) - OVERLAP
 PAIRS_CD = PAIRS_A1 + PAIRS - OVERLAP
 H_ROWS_A1 = PAIRS_CD + 4 * PAIRS
-FIRST_RAW_0 = H_ROWS_A1 + 2 * ROWS
-PAGE_3 = FIRST_RAW_0
+WORDS_CD1 = H_ROWS_A1 + 2 * ROWS
+FIRST_RAW_0 = WORDS_CD1 + ROWS - OVERLAP
+PAGE_3 = FIRST_RAW_0 + OVERLAP
 H_ROWS_B = [PAGE_3 + 4 * T, PAGE_3 + 4 * T + ROWS]
 
 
@@ -116,6 +117,7 @@ def tile_list_msg_relu_bias_kernel(
         wd_first = [sbuf([P, 4, WD_COLS], F32, f"wd_first{g}", offset) for g, offset in enumerate([FIRST_RAW_0, None])]
         load_wt(0)
         load_w_scales(1, wt_scales)
+        load_wt(1)
 
         distance = keep.tile([P, P], F32, name="distance")
         squared = keep.tile([P, P], F32, name="squared")
@@ -131,9 +133,9 @@ def tile_list_msg_relu_bias_kernel(
         def pick_words(pairs, l, j0):
             nc.vector.tensor_copy(pairs, tab_w[:].indirect(entries(l, j0, pairs.shape[1])))
 
-        def part(pairs, name):
+        def part(pairs, name, offset=None):
             count, width = pairs.shape[1:]
-            words = sbuf([P, count, PASSES, 2 * width], U8, name)
+            words = sbuf([P, count, PASSES, 2 * width], U8, name, offset)
             nc.vector.tensor_copy(
                 out=words[:].bitcast(U16), in_=pairs.bitcast(U16).rearrange("p l (j a) -> p l a j", a=PASSES)
             )
@@ -280,7 +282,6 @@ def tile_list_msg_relu_bias_kernel(
         for l in range(LISTS):
             pick_words(pairs_a[l][:, 0, :], l, j_a)
         words_a = part(pairs_a[0][:], "words_a0") + part(pairs_a[1][:], "words_a1")
-        load_wt(1)
         for g in range(PASSES):
             load_wd(wd_first[g][:], 0, g)
 
@@ -305,7 +306,7 @@ def tile_list_msg_relu_bias_kernel(
         pairs_cd = sbuf([P, LISTS, 2 * CHUNK], U32, "pairs_cd", PAIRS_CD)
         for l in range(LISTS):
             pick_words(pairs_cd[:, l, :], l, j_c)
-        words_cd = part(pairs_cd[:, 0:1], "words_cd0") + part(pairs_cd[:, 1:2], "words_cd1")
+        words_cd = part(pairs_cd[:, 0:1], "words_cd0")
 
         h_a = hidden((words_a, planes_a), 0, j_a, PASS_0_FIRST, {}, (None, H_ROWS_A1))
         first_grouped = sbuf([P, PASSES, WD_COLS, 4], BF16, "wd_grouped", H_ROWS_A1)
@@ -318,6 +319,7 @@ def tile_list_msg_relu_bias_kernel(
             first_grouped[:].rearrange("p g n t -> p (g n t)"),
         )
         clear_page(PAGE_3)
+        words_cd = words_cd + part(pairs_cd[:, 1:2], "words_cd1", WORDS_CD1)
         among_b = {(1, 0): lambda: send_first_pages(j_a, h_a)}
         h_b = hidden((words_b, planes_b), 0, j_b, LATE_PLANE, among_b, H_ROWS_B)
         pieces = []

@@ -37,7 +37,6 @@ LATE_PLANE = [(0, g, l, a) for a in range(PASSES) for g in range(PASSES) for l i
 PASS_1_ROW = 16
 MOVED_ROWS = 100
 TAB_FIRST = T // 4
-PORT_ORDER = [0, 2, 1, 3]
 
 OVERLAP = 64
 PAIRS = 4 * CHUNK
@@ -78,23 +77,26 @@ def tile_list_msg_relu_bias_kernel(
         lists = [keep.tile([P, J // PER_COLUMN], U16, name=f"list{l}") for l in range(LISTS)]
         tab_s = sbuf([P, T], U8, "tab_s")
         tab_w = sbuf([P, T], U32, "tab_w")
-        w_s = sbuf([P, LISTS, PASSES, R], U8, "w_s")
-        ws_w = sbuf([P, PASSES, 2 * R], U8, "ws_w")
+        w_s = [sbuf([P, PASSES, R], U8, f"w_s{l}") for l in range(LISTS)]
+        ws_w = [sbuf([P, 2 * R], U8, f"ws_w{a}") for a in range(PASSES)]
         wt_w = [sbuf([P, 4 * R], U8, f"wt_w{a}") for a in range(PASSES)]
         ident = keep.tile([P, P], F32, name="ident")
 
         nc.vector.memset(tab_s[:].bitcast(I32), 0)
 
         def load_w_scales(l, scales):
-            for q in PORT_ORDER:
+            for s in range(4):
                 nc.sync.dma_start(
-                    out=w_s[32 * q : 32 * q + 4, l, :, :].bitcast(I32),
-                    in_=scales[:, 4 * q : 4 * q + 4, :].rearrange("a s r -> s a r").bitcast(I32),
+                    out=w_s[l][s:P:32].bitcast(I32),
+                    in_=scales[:, s:16:4, :].rearrange("a q r -> q a r").bitcast(I32),
                 )
 
         def load_tab_words(first, last):
             source = tab_words[0, :, first:last, :].rearrange("p t b -> p (t b)")
             nc.sync.dma_start(out=tab_w[:, first:last].bitcast(I32), in_=source.bitcast(I32))
+
+        def load_ws(a):
+            nc.sync.dma_start(out=ws_w[a][:].bitcast(I32), in_=ws_words[a].bitcast(I32))
 
         def load_wt(a):
             nc.sync.dma_start(out=wt_w[a][:].bitcast(I32), in_=wt_words[a].rearrange("p r i -> p (r i)").bitcast(I32))
@@ -112,11 +114,12 @@ def tile_list_msg_relu_bias_kernel(
                 in_=tab_scales[:, s:16:4, :].rearrange("a q t -> q a t").bitcast(I32),
             )
         load_tab_words(TAB_FIRST, T)
-        nc.sync.dma_start(out=ws_w[:].bitcast(I32), in_=ws_words.rearrange("a p c -> p a c").bitcast(I32))
+        load_ws(0)
         load_w_scales(0, ws_scales)
         wd_first = [sbuf([P, 4, WD_COLS], F32, f"wd_first{g}", offset) for g, offset in enumerate([FIRST_RAW_0, None])]
         load_wt(0)
         load_w_scales(1, wt_scales)
+        load_ws(1)
         load_wt(1)
 
         distance = keep.tile([P, P], F32, name="distance")
@@ -172,7 +175,7 @@ def tile_list_msg_relu_bias_kernel(
             for block, g, l, a in order:
                 c0 = col + P * block
                 if l == 0:
-                    w_words = ws_w[:, a, 2 * BANK * g : 2 * BANK * (g + 1)].bitcast(FP4X4)
+                    w_words = ws_w[a][:, 2 * BANK * g : 2 * BANK * (g + 1)].bitcast(FP4X4)
                 else:
                     w_words = wt_w[a][:, 4 * BANK * g : 4 * BANK * (g + 1)].bitcast(FP8X4)
                 last = (l, a) == (LISTS - 1, PASSES - 1)
@@ -181,7 +184,7 @@ def tile_list_msg_relu_bias_kernel(
                     lhsT=words[l][:, a, 2 * c0 : 2 * (c0 + P)].bitcast(FP4X4),
                     lhsT_scale=planes[l][a][:, c0 : c0 + P],
                     rhs=w_words,
-                    rhs_scale=w_s[:, l, a, BANK * g : BANK * (g + 1)],
+                    rhs_scale=w_s[l][:, a, BANK * g : BANK * (g + 1)],
                     start=(l, a) == (0, 0),
                     stop=last,
                 )

@@ -49,14 +49,14 @@ PAIRS_A0 = BIAS + OVERLAP
 SECOND_RAW_0 = PAIRS_B + 2 * PAIRS - OVERLAP
 SECOND_GROUPED_1 = SECOND_RAW_0
 SECOND_CODES = SECOND_RAW_0 + ROWS
-PICKED_REST = SECOND_RAW_0 + RAW
-PAIRS_A1 = PICKED_REST + LISTS * (J - CHUNK) - OVERLAP
-PAIRS_CD = PAIRS_A1 + PAIRS - OVERLAP
+PAGE_3 = SECOND_RAW_0 + RAW
+PAIRS_A1 = PAGE_3 + 4 * T - OVERLAP
+PICKED_REST = PAIRS_A1 + OVERLAP
+PAIRS_CD = PAIRS_A1 + 2 * PAIRS - OVERLAP
 H_ROWS_A1 = PAIRS_CD + 4 * PAIRS
 WORDS_CD1 = H_ROWS_A1 + 2 * ROWS
 FIRST_RAW_0 = WORDS_CD1 + ROWS - OVERLAP
-PAGE_3 = FIRST_RAW_0 + OVERLAP
-H_ROWS_B = [PAGE_3 + 4 * T, PAGE_3 + 4 * T + ROWS]
+H_ROWS_B = [FIRST_RAW_0 + RAW, FIRST_RAW_0 + RAW + ROWS]
 
 
 def tile_list_msg_relu_bias_kernel(
@@ -264,14 +264,14 @@ def tile_list_msg_relu_bias_kernel(
 
         j_a, j_b, j_c, j_d = range(0, J, CHUNK)
 
-        def clear_page(offset=None):
+        def clear_page(engine, offset=None):
             page = sbuf([P, T], F32, f"page{len(pages)}", offset)
-            nc.vector.memset(page[:].bitcast(I32), 0)
+            engine.memset(page[:].bitcast(I32), 0)
             pages.append(page)
 
         pages = []
         for c in range(PAGES - 1):
-            clear_page()
+            clear_page(nc.vector)
 
         def look_up_scales(j0, width, name, offset=None):
             picked = sbuf([P, LISTS * width], U8, f"picked_{name}", offset)
@@ -281,10 +281,11 @@ def tile_list_msg_relu_bias_kernel(
             return [columns(both, width * l, width) for l in range(LISTS)]
 
         planes_a = look_up_scales(j_a, CHUNK, "a")
-        pairs_a = [sbuf([P, 1, CHUNK], U32, f"pairs_a{l}", offset) for l, offset in enumerate([PAIRS_A0, PAIRS_A1])]
+        pairs_a = [sbuf([P, 1 + l, CHUNK], U32, f"pairs_a{l}", offset) for l, offset in enumerate([PAIRS_A0, PAIRS_A1])]
         for l in range(LISTS):
             pick_words(pairs_a[l][:, 0, :], l, j_a)
-        words_a = part(pairs_a[0][:], "words_a0") + part(pairs_a[1][:], "words_a1")
+        words_a = part(pairs_a[0][:], "words_a0") + part(pairs_a[1][:, 0:1], "words_a1")
+        clear_page(nc.gpsimd, PAGE_3)
         for g in range(PASSES):
             load_wd(wd_first[g][:], 0, g)
 
@@ -321,7 +322,6 @@ def tile_list_msg_relu_bias_kernel(
             first_scales[:].rearrange("p g n -> p (g n)"),
             first_grouped[:].rearrange("p g n t -> p (g n t)"),
         )
-        clear_page(PAGE_3)
         words_cd = words_cd + part(pairs_cd[:, 1:2], "words_cd1", WORDS_CD1)
         among_b = {(1, 0): lambda: send_first_pages(j_a, h_a)}
         h_b = hidden((words_b, planes_b), 0, j_b, LATE_PLANE, among_b, H_ROWS_B)

@@ -42,21 +42,24 @@ OVERLAP = 64
 PAIRS = 4 * CHUNK
 RAW = 4 * WD_COLS * 4
 ROWS = 2 * R
+PAGE = 4 * T
 LATE_LOADS = 0
-PAIRS_B = LATE_LOADS + RAW + 4 * J - OVERLAP
+PAIRS_B = LATE_LOADS + RAW + 2 * J - OVERLAP
 BIAS = PAIRS_B + OVERLAP
 PAIRS_A0 = BIAS + OVERLAP
-SECOND_RAW_0 = PAIRS_B + 2 * PAIRS - OVERLAP
-SECOND_GROUPED_1 = SECOND_RAW_0
-SECOND_CODES = SECOND_RAW_0 + ROWS
-PAGE_3 = SECOND_RAW_0 + RAW
-PAIRS_A1 = PAGE_3 + 4 * T - OVERLAP
+RAW_10 = PAIRS_B + 2 * PAIRS - OVERLAP
+PAIRS_D = RAW_10 + RAW // 2 - OVERLAP
+PAGE_2 = PAIRS_D + 2 * PAIRS
+PAIRS_A1 = PAGE_2 + PAGE - OVERLAP
 PICKED_REST = PAIRS_A1 + OVERLAP
-PAIRS_CD = PAIRS_A1 + 2 * PAIRS - OVERLAP
-H_ROWS_A1 = PAIRS_CD + 4 * PAIRS
-WORDS_CD1 = H_ROWS_A1 + 2 * ROWS
-FIRST_RAW_0 = WORDS_CD1 + ROWS - OVERLAP
-H_ROWS_B = [FIRST_RAW_0 + RAW, FIRST_RAW_0 + RAW + ROWS]
+PAIRS_C = PICKED_REST + 5 * CHUNK
+PAIRS_D0 = PAIRS_C + 2 * PAIRS
+PAGE_3 = PAIRS_D0 + PAIRS
+H_ROWS = [PAGE_3 + PAGE + ROWS * k for k in range(4)]
+GROUPED_11 = RAW_10 - OVERLAP
+GROUPED_A = H_ROWS[-1] + ROWS
+RAW_00 = GROUPED_A + RAW
+WORDS_A0 = RAW_00 + RAW
 
 
 def tile_list_msg_relu_bias_kernel(
@@ -66,8 +69,7 @@ def tile_list_msg_relu_bias_kernel(
     with ExitStack() as ctx:
         keep = ctx.enter_context(tc.tile_pool(name="keep", bufs=1))
         stage = ctx.enter_context(tc.tile_pool(name="stage", bufs=1))
-        single = ctx.enter_context(tc.psum_pool(name="single", bufs=1))
-        double = ctx.enter_context(tc.psum_pool(name="double", bufs=2))
+        psum = ctx.enter_context(tc.psum_pool(name="psum", bufs=1))
 
         def sbuf(shape, dtype, name, offset=None):
             if offset is None:
@@ -101,8 +103,8 @@ def tile_list_msg_relu_bias_kernel(
         def load_wt(a):
             nc.sync.dma_start(out=wt_w[a][:].bitcast(I32), in_=wt_words[a].rearrange("p r i -> p (r i)").bitcast(I32))
 
-        def load_wd(raw, half, g):
-            source = wd[PASS_ROWS * g : PASS_ROWS * (g + 1), WD_COLS * half : WD_COLS * (half + 1)]
+        def load_wd(raw, first, g):
+            source = wd[PASS_ROWS * g : PASS_ROWS * (g + 1), first : first + raw.shape[2]]
             nc.sync.dma_start(out=raw, in_=source.rearrange("(p t) n -> p t n", t=4))
 
         load_tab_words(0, TAB_FIRST)
@@ -116,14 +118,15 @@ def tile_list_msg_relu_bias_kernel(
         load_tab_words(TAB_FIRST, T)
         load_ws(0)
         load_w_scales(0, ws_scales)
-        wd_first = [sbuf([P, 4, WD_COLS], F32, f"wd_first{g}", offset) for g, offset in enumerate([FIRST_RAW_0, None])]
         load_wt(0)
         load_w_scales(1, wt_scales)
         load_ws(1)
+        raw_0 = [sbuf([P, 4, WD_COLS], F32, f"raw_0{g}", offset) for g, offset in enumerate([RAW_00, None])]
+        load_wd(raw_0[0][:], 0, 0)
         load_wt(1)
 
         distance = keep.tile([P, P], F32, name="distance")
-        squared = keep.tile([P, P], F32, name="squared")
+        squared = sbuf([P, P], F32, "squared")
         nc.gpsimd.iota(
             distance[:], pattern=[[1, P]], base=0, channel_multiplier=-1, allow_small_or_imprecise_dtypes=True
         )
@@ -161,46 +164,12 @@ def tile_list_msg_relu_bias_kernel(
         def quantise(codes, scales, grouped):
             nc.vector.quantize_mx(out=codes.bitcast(FP8X4), scales=scales, in_=grouped)
 
-        wd_codes, wd_scales = [], []
-
-        def wd_tiles(offset=None):
-            wd_codes.append(sbuf([P, PASSES, WD_COLS], U32, f"wd_codes{len(wd_codes)}", offset))
-            wd_scales.append(sbuf([P, PASSES, WD_COLS], U8, f"wd_scales{len(wd_scales)}"))
-            return wd_codes[-1], wd_scales[-1]
-
-        def first_product(looked_up, col, j0, order, offsets, between):
-            words, planes = looked_up
-            banks = [[double.tile([P, BANK], F32, name=f"a{g}") for g in range(PASSES)] for block in range(BLOCKS)]
-            rows = [sbuf([P, PASSES, 2, P, 2], BF16, f"h_rows{j0}_{block}", offsets[block]) for block in range(BLOCKS)]
-            for block, g, l, a in order:
-                c0 = col + P * block
-                if l == 0:
-                    w_words = ws_w[a][:, 2 * BANK * g : 2 * BANK * (g + 1)].bitcast(FP4X4)
-                else:
-                    w_words = wt_w[a][:, 4 * BANK * g : 4 * BANK * (g + 1)].bitcast(FP8X4)
-                last = (l, a) == (LISTS - 1, PASSES - 1)
-                nc.tensor.matmul_mx(
-                    out=banks[block][g][:],
-                    lhsT=words[l][:, a, 2 * c0 : 2 * (c0 + P)].bitcast(FP4X4),
-                    lhsT_scale=planes[l][a][:, c0 : c0 + P],
-                    rhs=w_words,
-                    rhs_scale=w_s[l][:, a, BANK * g : BANK * (g + 1)],
-                    start=(l, a) == (0, 0),
-                    stop=last,
-                )
-                if last:
-                    nc.scalar.activation(
-                        out=rows[block][:, g],
-                        in_=banks[block][g][:].rearrange("p (m u e) -> p u m e", u=2, e=2),
-                        func=ACT.Relu,
-                    )
-                    if (block, g) in between:
-                        between[block, g]()
-            return rows
+        wd_codes = [sbuf([P, PASSES, WD_COLS], U32, f"wd_codes{half}", offset) for half, offset in enumerate([RAW_00, None])]
+        wd_scales = [sbuf([P, PASSES, WD_COLS], U8, f"wd_scales{half}") for half in range(2)]
 
         def turn(rows, grouped, col, bank_name):
             h_pairs = rows[:].rearrange("p g u m e -> p (g u m e)").bitcast(F32)
-            turned = single.tile([P, PASSES, 2, P], F32, name=bank_name)
+            turned = psum.tile([P, PASSES, 2, P], F32, name=bank_name)
             for g in range(PASSES):
                 for u in range(2):
                     w0 = (2 * g + u) * P
@@ -210,13 +179,44 @@ def tile_list_msg_relu_bias_kernel(
                 in_=turned[:].rearrange("p g u j -> p g j u"),
             )
 
-        def hidden(looked_up, col, j0, order, between, rows_offsets=(None, None)):
-            grouped = sbuf([P, PASSES, CHUNK, 4], BF16, f"h_grouped{j0}")
-            first_rows, last_rows = first_product(looked_up, col, j0, order, rows_offsets, between)
-            turn(first_rows, grouped, 0, "early")
-            turn(last_rows, grouped, P, "late")
-            codes = sbuf([P, PASSES, CHUNK], U32, f"h_codes{j0}")
-            scales = sbuf([P, PASSES, CHUNK], U8, f"h_scales{j0}")
+        def hidden(name, words, planes, col, order, between, last_rows, offset=None, first_rows=None):
+            grouped = sbuf([P, PASSES, CHUNK, 4], BF16, f"h_grouped_{name}", offset)
+            banks = {bank: psum.tile([P, BANK], F32, name=f"acc{k}") for k, bank in enumerate(BANKS)}
+            rows = [
+                sbuf([P, PASSES, 2, P, 2], BF16, f"h_rows_{name}{block}", offset)
+                for block, offset in enumerate([first_rows, last_rows])
+            ]
+            for block, g, l, a in order:
+                c0 = P * block
+                if l == 0:
+                    w_words = ws_w[a][:, 2 * BANK * g : 2 * BANK * (g + 1)].bitcast(FP4X4)
+                else:
+                    w_words = wt_w[a][:, 4 * BANK * g : 4 * BANK * (g + 1)].bitcast(FP8X4)
+                last = (l, a) == (LISTS - 1, PASSES - 1)
+                nc.tensor.matmul_mx(
+                    out=banks[block, g][:],
+                    lhsT=words[l][:, a, 2 * c0 : 2 * (c0 + P)].bitcast(FP4X4),
+                    lhsT_scale=planes[l][a][:, col + c0 : col + c0 + P],
+                    rhs=w_words,
+                    rhs_scale=w_s[l][:, a, BANK * g : BANK * (g + 1)],
+                    start=(l, a) == (0, 0),
+                    stop=last,
+                )
+                if last:
+                    nc.scalar.activation(
+                        out=rows[block][:, g],
+                        in_=banks[block, g][:].rearrange("p (m u e) -> p u m e", u=2, e=2),
+                        func=ACT.Relu,
+                    )
+                    if (block, g) in between:
+                        between[block, g]()
+            for block in range(BLOCKS):
+                turn(rows[block], grouped, P * block, f"turned{block}")
+            return grouped
+
+        def quantise_h(name, grouped):
+            codes = sbuf([P, PASSES, CHUNK], U32, f"h_codes_{name}")
+            scales = sbuf([P, PASSES, CHUNK], U8, f"h_scales_{name}")
             quantise(
                 codes[:].rearrange("p g j -> p (g j)"),
                 scales[:].rearrange("p g j -> p (g j)"),
@@ -224,12 +224,15 @@ def tile_list_msg_relu_bias_kernel(
             )
             return codes, scales
 
-        def message(c, chunks, biased, held=False):
-            width = CHUNK * len(chunks)
-            if held:
-                bank = single.tile([P, width], F32, name="late")
-            else:
-                bank = double.tile([P, width], F32, name="y")
+        def quantise_wd(half, grouped):
+            quantise(
+                wd_codes[half][:].rearrange("p g n -> p (g n)"),
+                wd_scales[half][:].rearrange("p g n -> p (g n)"),
+                grouped[:].rearrange("p g n t -> p (g n t)"),
+            )
+
+        def product(c, chunks, bank_name):
+            bank = psum.tile([P, CHUNK * len(chunks)], F32, name=bank_name)
             half, n0 = divmod(c * P, WD_COLS)
             for s, (codes, scales) in enumerate(chunks):
                 for g in range(PASSES):
@@ -242,111 +245,126 @@ def tile_list_msg_relu_bias_kernel(
                         start=(g == 0),
                         stop=(g == PASSES - 1),
                     )
-            nc.scalar.activation(out=biased, in_=bank[:], func=ACT.Identity, bias=bias[:, c : c + 1], scale=1.0)
+            return bank
 
-        def scatter(c, j0, biased):
-            width = biased.shape[1]
+        def send(c, j0, chunks, bank_name, offset=None):
+            bank = product(c, chunks, bank_name)
+            width = bank.shape[1]
+            biased = sbuf([P, width], F32, f"biased{c}_{j0}", offset)
+            nc.scalar.activation(out=biased[:], in_=bank[:], func=ACT.Identity, bias=bias[:, c : c + 1], scale=1.0)
             nc.vector.tensor_tensor(
-                pages[c][:].indirect(entries(1, j0, width)), biased, weight[:, j0 : j0 + width], MULT
+                pages[c][:].indirect(entries(1, j0, width)), biased[:], weight(j0, width), MULT
             )
-
-        def send(c, j0, chunks, held=False):
-            biased = sbuf([P, CHUNK * len(chunks)], F32, f"biased{c}_{j0}")
-            message(c, chunks, biased[:], held)
-            scatter(c, j0, biased[:])
 
         def store(c):
             nc.sync.dma_start(out=out[c * P : (c + 1) * P, :], in_=pages[c][:])
 
-        def send_first_pages(j0, h):
-            for c in range(2):
-                send(c, j0, [h])
-
         j_a, j_b, j_c, j_d = range(0, J, CHUNK)
+        pages = []
 
         def clear_page(engine, offset=None):
             page = sbuf([P, T], F32, f"page{len(pages)}", offset)
             engine.memset(page[:].bitcast(I32), 0)
             pages.append(page)
 
-        pages = []
-        for c in range(PAGES - 1):
+        for c in range(2):
             clear_page(nc.vector)
 
-        def look_up_scales(j0, width, name, offset=None):
-            picked = sbuf([P, LISTS * width], U8, f"picked_{name}", offset)
-            for l in range(LISTS):
-                pick_scales(picked[:, width * l : width * (l + 1)], l, j0)
+        def look_up_scales(spans, name, offset=None):
+            picked = sbuf([P, sum(width for first, width in spans)], U8, f"picked_{name}", offset)
+            starts = [0, spans[0][1]]
+            for l, (first, width) in enumerate(spans):
+                pick_scales(picked[:, starts[l] : starts[l] + width], l, first)
             both = scale_planes(picked, f"moved_{name}")
-            return [columns(both, width * l, width) for l in range(LISTS)]
+            return [columns(both, starts[l], width) for l, (first, width) in enumerate(spans)]
 
-        planes_a = look_up_scales(j_a, CHUNK, "a")
-        pairs_a = [sbuf([P, 1 + l, CHUNK], U32, f"pairs_a{l}", offset) for l, offset in enumerate([PAIRS_A0, PAIRS_A1])]
+        def pick_both(name, j0, offset):
+            pairs = sbuf([P, LISTS, CHUNK], U32, name, offset)
+            for l in range(LISTS):
+                pick_words(pairs[:, l, :], l, j0)
+            return pairs
+
+        def part_each(pairs, name):
+            return [part(pairs[:, l : l + 1], f"{name}{l}")[0] for l in range(LISTS)]
+
+        early = look_up_scales([(j_a, 2 * CHUNK), (j_a, CHUNK)], "early")
+        pairs_a = [sbuf([P, 1 + 4 * l, CHUNK], U32, f"pairs_a{l}", offset) for l, offset in enumerate([PAIRS_A0, PAIRS_A1])]
         for l in range(LISTS):
             pick_words(pairs_a[l][:, 0, :], l, j_a)
-        words_a = part(pairs_a[0][:], "words_a0") + part(pairs_a[1][:, 0:1], "words_a1")
+        words_a = part(pairs_a[0][:], "words_a0", WORDS_A0) + part(pairs_a[1][:, 0:1], "words_a1")
+        clear_page(nc.gpsimd, PAGE_2)
         clear_page(nc.gpsimd, PAGE_3)
-        for g in range(PASSES):
-            load_wd(wd_first[g][:], 0, g)
+        load_wd(raw_0[1][:], 0, 1)
 
-        pairs_b = sbuf([P, LISTS, CHUNK], U32, "pairs_b", PAIRS_B)
-        for l in range(LISTS):
-            pick_words(pairs_b[:, l, :], l, j_b)
-        planes_rest = look_up_scales(j_b, J - CHUNK, "rest", PICKED_REST)
+        pairs_b = pick_both("pairs_b", j_b, PAIRS_B)
+        late = look_up_scales([(j_c, 2 * CHUNK), (j_b, 3 * CHUNK)], "late", PICKED_REST)
+        planes_a = [columns(early[l], 0, CHUNK) for l in range(LISTS)]
+        planes_b = [columns(early[0], CHUNK, CHUNK), columns(late[1], 0, CHUNK)]
+        planes_c = [columns(late[l], l * CHUNK, CHUNK) for l in range(LISTS)]
+        planes_d = [columns(late[l], (l + 1) * CHUNK, CHUNK) for l in range(LISTS)]
+        pairs_c = sbuf([P, LISTS, CHUNK], U32, "pairs_c", PAIRS_C)
+        pick_words(pairs_c[:, 0, :], 0, j_c)
         words_b = part(pairs_b[:], "words_b")
-        planes_b = [[plane[:, :CHUNK] for plane in planes] for planes in planes_rest]
-        planes_cd = [[plane[:, CHUNK:] for plane in planes] for planes in planes_rest]
 
-        late_loads = sbuf([P, (RAW + 4 * J) // 4], F32, "late_loads", LATE_LOADS)
-        second_raw_0 = sbuf([P, 4, WD_COLS], F32, "second_raw_0", SECOND_RAW_0)
-        second_raw_1 = late_loads[:, : RAW // 4].rearrange("p (t n) -> p t n", t=4)
-        weight = late_loads[:, RAW // 4 :]
-        load_wd(second_raw_0[:], 1, 0)
+        raw_10 = [sbuf([P, 4, P], F32, f"raw_10{k}", offset) for k, offset in enumerate([RAW_10, None])]
+        late_loads = sbuf([P, (RAW + 2 * J) // 4], F32, "late_loads", LATE_LOADS)
+        raw_11 = late_loads[:, : RAW // 4].rearrange("p (t n) -> p t n", t=4)
+        weights = [late_loads[:, RAW // 4 :], sbuf([P, J // 2], F32, "weight_cd")[:]]
+
+        def weight(j0, width):
+            half, first = divmod(j0, J // 2)
+            return weights[half][:, first : first + width]
+
+        load_wd(raw_10[0][:], WD_COLS, 0)
         bias = sbuf([P, PAGES], F32, "bias", BIAS)
         with nc.allow_non_contiguous_dma(reason="one bias value a partition and page"):
             nc.sync.dma_start(out=bias[:], in_=b.rearrange("(c p) -> p c", p=P))
-        nc.sync.dma_start(out=weight, in_=wgo)
-        load_wd(second_raw_1, 1, 1)
-        pairs_cd = sbuf([P, LISTS, 2 * CHUNK], U32, "pairs_cd", PAIRS_CD)
-        for l in range(LISTS):
-            pick_words(pairs_cd[:, l, :], l, j_c)
-        words_cd = part(pairs_cd[:, 0:1], "words_cd0")
+        nc.sync.dma_start(out=weights[0], in_=wgo[:, : J // 2])
+        load_wd(raw_11, WD_COLS, 1)
+        pick_words(pairs_c[:, 1, :], 1, j_c)
+        pairs_d = [sbuf([P, 1, CHUNK], U32, f"pairs_d{l}", offset) for l, offset in enumerate([PAIRS_D0, PAIRS_D])]
+        pick_words(pairs_d[0][:, 0, :], 0, j_d)
+        words_c = part(pairs_c[:], "words_c")
 
-        h_a = hidden((words_a, planes_a), 0, j_a, PASS_0_FIRST, {}, (None, H_ROWS_A1))
-        first_grouped = sbuf([P, PASSES, WD_COLS, 4], BF16, "wd_grouped", H_ROWS_A1)
-        round_wd(nc.scalar.copy, wd_first[0][:], first_grouped[:, 0])
-        round_wd(nc.vector.tensor_copy, wd_first[1][:], first_grouped[:, 1])
-        first_codes, first_scales = wd_tiles()
-        quantise(
-            first_codes[:].rearrange("p g n -> p (g n)"),
-            first_scales[:].rearrange("p g n -> p (g n)"),
-            first_grouped[:].rearrange("p g n t -> p (g n t)"),
-        )
-        words_cd = words_cd + part(pairs_cd[:, 1:2], "words_cd1", WORDS_CD1)
-        among_b = {(1, 0): lambda: send_first_pages(j_a, h_a)}
-        h_b = hidden((words_b, planes_b), 0, j_b, LATE_PLANE, among_b, H_ROWS_B)
-        pieces = []
-        for block in range(BLOCKS):
-            grouped = sbuf([P, P, 4], BF16, f"second_grouped_0{block}", H_ROWS_B[block])
-            round_wd(nc.scalar.copy, second_raw_0[:, :, P * block : P * (block + 1)], grouped[:])
-            pieces.append((grouped, 0, P * block))
-        grouped = sbuf([P, WD_COLS, 4], BF16, "second_grouped_1", SECOND_GROUPED_1)
-        round_wd(nc.vector.tensor_copy, second_raw_1, grouped[:])
-        pieces.append((grouped, 1, 0))
-        second_codes, second_scales = wd_tiles(SECOND_CODES)
-        for grouped, g, first in pieces:
-            cols = slice(first, first + grouped.shape[1])
-            quantise(second_codes[:, g, cols], second_scales[:, g, cols], grouped[:].rearrange("p n t -> p (n t)"))
+        first_grouped = sbuf([P, PASSES, WD_COLS, 4], BF16, "first_grouped")
+        round_wd(nc.scalar.copy, raw_0[0][:], first_grouped[:, 0])
+        round_wd(nc.vector.tensor_copy, raw_0[1][:], first_grouped[:, 1])
+        grouped_a = hidden("a", words_a, planes_a, 0, PASS_0_FIRST, {}, H_ROWS[0], GROUPED_A, RAW_00)
+        words_d = part(pairs_d[0][:], "words_d0", WORDS_A0)
+        quantise_wd(0, first_grouped)
+        h_a = quantise_h("a", grouped_a)
+        piece_0 = sbuf([P, P, 4], BF16, "piece_0", H_ROWS[0])
+        round_wd(nc.scalar.copy, raw_10[0][:], piece_0[:])
+        pick_words(pairs_d[1][:, 0, :], 1, j_d)
+        grouped_11 = sbuf([P, WD_COLS, 4], BF16, "grouped_11", GROUPED_11)
+        round_wd(nc.vector.tensor_copy, raw_11, grouped_11[:])
+        words_d = words_d + part(pairs_d[1][:], "words_d1")
+        load_wd(raw_10[1][:], WD_COLS + P, 0)
+        nc.sync.dma_start(out=weights[1], in_=wgo[:, J // 2 :])
 
-        among_c = {(0, 1): lambda: send_first_pages(j_b, h_b), (1, 1): lambda: send(2, j_a, [h_a, h_b])}
-        h_c = hidden((words_cd, planes_cd), 0, j_c, BY_BANK, among_c)
-        send(3, j_a, [h_a, h_b], held=True)
-        among_d = {(1, 1): lambda: send(0, j_c, [h_c])}
-        h_d = hidden((words_cd, planes_cd), CHUNK, j_d, BY_BANK, among_d)
-        send(1, j_c, [h_c], held=True)
-        for c in range(2):
-            send(c, j_d, [h_d])
+        def first_messages():
+            send(0, j_a, [h_a], "y0")
+            piece_1 = sbuf([P, P, 4], BF16, "piece_1", GROUPED_A)
+            round_wd(nc.scalar.copy, raw_10[1][:], piece_1[:])
+            for piece, g, first in [(piece_0, 0, 0), (piece_1, 0, P), (grouped_11, 1, 0)]:
+                cols = slice(first, first + piece.shape[1])
+                quantise(wd_codes[1][:, g, cols], wd_scales[1][:, g, cols], piece[:].rearrange("p n t -> p (n t)"))
+            send(1, j_a, [h_a], "y1")
+
+        def pair(first, j0, h, offset=None):
+            for k in range(2):
+                send(first + k, j0, [h], f"y{k}", None if offset is None else offset + k * PAIRS)
+
+        h_b = quantise_h("b", hidden("b", words_b, planes_b, 0, LATE_PLANE, {(0, 1): first_messages}, H_ROWS[1]))
+        pair(2, j_a, h_a, H_ROWS[1])
+        among_c = {(0, 1): lambda: pair(0, j_b, h_b)}
+        h_c = quantise_h("c", hidden("c", words_c, planes_c, 0, BY_BANK, among_c, H_ROWS[2]))
+        pair(2, j_b, h_b, H_ROWS[2])
+        among_d = {(0, 1): lambda: pair(0, j_c, h_c)}
+        h_d = quantise_h("d", hidden("d", words_d, planes_d, 0, BY_BANK, among_d, H_ROWS[3]))
+        send(2, j_c, [h_c], "y0", H_ROWS[3])
+        for c, bank_name in enumerate(["y1", "acc0", "acc1"]):
+            send(c, j_d, [h_d], bank_name)
             store(c)
-        for c in range(2, PAGES):
-            send(c, j_c, [h_c, h_d])
-            store(c)
+        send(3, j_c, [h_c, h_d], "acc2")
+        store(3)

@@ -43,23 +43,23 @@ PAIRS = 4 * CHUNK
 RAW = 4 * WD_COLS * 4
 ROWS = 2 * R
 PAGE = 4 * T
-LATE_LOADS = 0
-PAIRS_B = LATE_LOADS + RAW + 2 * J - OVERLAP
-BIAS = PAIRS_B + OVERLAP
-PAIRS_A0 = BIAS + OVERLAP
-RAW_10 = PAIRS_B + 2 * PAIRS - OVERLAP
+PAIRS_B = 0
+PAIRS_A0 = PAIRS_B
+GROUPED_11 = PAIRS_B + 2 * PAIRS
+RAW_10 = GROUPED_11 + OVERLAP
 PAIRS_D = RAW_10 + RAW // 2 - OVERLAP
-PAGE_2 = PAIRS_D + 2 * PAIRS
-PAIRS_A1 = PAGE_2 + PAGE - OVERLAP
+PAIRS_A1 = PAIRS_D + 2 * PAIRS
 PICKED_REST = PAIRS_A1 + OVERLAP
 PAIRS_C = PICKED_REST + 5 * CHUNK
 PAIRS_D0 = PAIRS_C + 2 * PAIRS
 PAGE_3 = PAIRS_D0 + PAIRS
-H_ROWS = [PAGE_3 + PAGE + ROWS * k for k in range(4)]
-GROUPED_11 = RAW_10 - OVERLAP
+PAGE_2 = PAGE_3 + PAGE
+DIAGONAL = PAGE_2 - 2 * P
+H_ROWS = [PAGE_2 + PAGE + ROWS * k for k in range(4)]
 GROUPED_A = H_ROWS[-1] + ROWS
 RAW_00 = GROUPED_A + RAW
 WORDS_A0 = RAW_00 + RAW
+FIRST_GROUPED = WORDS_A0 + PAIRS
 
 
 def tile_list_msg_relu_bias_kernel(
@@ -124,14 +124,6 @@ def tile_list_msg_relu_bias_kernel(
         raw_0 = [sbuf([P, 4, WD_COLS], F32, f"raw_0{g}", offset) for g, offset in enumerate([RAW_00, None])]
         load_wd(raw_0[0][:], 0, 0)
         load_wt(1)
-
-        distance = keep.tile([P, P], F32, name="distance")
-        squared = sbuf([P, P], F32, "squared")
-        nc.gpsimd.iota(
-            distance[:], pattern=[[1, P]], base=0, channel_multiplier=-1, allow_small_or_imprecise_dtypes=True
-        )
-        nc.scalar.activation(out=squared[:], in_=distance[:], func=ACT.Square)
-        nc.scalar.activation(out=ident[:], in_=squared[:], func=ACT.Relu, scale=-1.0, bias=1.0)
 
         def entries(l, j0, width):
             return lists[l][:, j0 // PER_COLUMN : (j0 + width) // PER_COLUMN]
@@ -269,6 +261,20 @@ def tile_list_msg_relu_bias_kernel(
 
         for c in range(2):
             clear_page(nc.vector)
+        blank = sbuf([P, P], F32, "blank", FIRST_GROUPED)
+        nc.vector.memset(blank[:], 0.0)
+        diagonal = sbuf([P, P], F32, "diagonal", DIAGONAL)
+        nc.gpsimd.affine_select(
+            out=diagonal[:],
+            in_=blank[:],
+            pattern=[[-1, P]],
+            compare_op=mybir.AluOpType.not_equal,
+            fill=1.0,
+            base=0,
+            channel_multiplier=1,
+        )
+        nc.scalar.activation(out=ident[:], in_=diagonal[:], func=ACT.Relu)
+        clear_page(nc.gpsimd, PAGE_2)
 
         def look_up_scales(spans, name, offset=None):
             picked = sbuf([P, sum(width for first, width in spans)], U8, f"picked_{name}", offset)
@@ -287,46 +293,44 @@ def tile_list_msg_relu_bias_kernel(
         def part_each(pairs, name):
             return [part(pairs[:, l : l + 1], f"{name}{l}")[0] for l in range(LISTS)]
 
-        early = look_up_scales([(j_a, 2 * CHUNK), (j_a, CHUNK)], "early")
+        early = look_up_scales([(j_a, 2 * CHUNK), (j_a, 2 * CHUNK)], "early")
         pairs_a = [sbuf([P, 1 + 4 * l, CHUNK], U32, f"pairs_a{l}", offset) for l, offset in enumerate([PAIRS_A0, PAIRS_A1])]
         for l in range(LISTS):
             pick_words(pairs_a[l][:, 0, :], l, j_a)
         words_a = part(pairs_a[0][:], "words_a0", WORDS_A0) + part(pairs_a[1][:, 0:1], "words_a1")
-        clear_page(nc.gpsimd, PAGE_2)
         clear_page(nc.gpsimd, PAGE_3)
         load_wd(raw_0[1][:], 0, 1)
 
-        pairs_b = pick_both("pairs_b", j_b, PAIRS_B)
-        late = look_up_scales([(j_c, 2 * CHUNK), (j_b, 3 * CHUNK)], "late", PICKED_REST)
-        planes_a = [columns(early[l], 0, CHUNK) for l in range(LISTS)]
-        planes_b = [columns(early[0], CHUNK, CHUNK), columns(late[1], 0, CHUNK)]
-        planes_c = [columns(late[l], l * CHUNK, CHUNK) for l in range(LISTS)]
-        planes_d = [columns(late[l], (l + 1) * CHUNK, CHUNK) for l in range(LISTS)]
-        pairs_c = sbuf([P, LISTS, CHUNK], U32, "pairs_c", PAIRS_C)
-        pick_words(pairs_c[:, 0, :], 0, j_c)
-        words_b = part(pairs_b[:], "words_b")
-
         raw_10 = [sbuf([P, 4, P], F32, f"raw_10{k}", offset) for k, offset in enumerate([RAW_10, None])]
-        late_loads = sbuf([P, (RAW + 2 * J) // 4], F32, "late_loads", LATE_LOADS)
-        raw_11 = late_loads[:, : RAW // 4].rearrange("p (t n) -> p t n", t=4)
-        weights = [late_loads[:, RAW // 4 :], sbuf([P, J // 2], F32, "weight_cd")[:]]
+        raw_11 = sbuf([P, 4, WD_COLS], F32, "raw_11")
+        weights = [sbuf([P, J // 2], F32, f"weight{half}") for half in range(2)]
 
         def weight(j0, width):
             half, first = divmod(j0, J // 2)
             return weights[half][:, first : first + width]
 
         load_wd(raw_10[0][:], WD_COLS, 0)
-        bias = sbuf([P, PAGES], F32, "bias", BIAS)
+        load_wd(raw_11[:], WD_COLS, 1)
+        bias = sbuf([P, PAGES], F32, "bias")
         with nc.allow_non_contiguous_dma(reason="one bias value a partition and page"):
             nc.sync.dma_start(out=bias[:], in_=b.rearrange("(c p) -> p c", p=P))
-        nc.sync.dma_start(out=weights[0], in_=wgo[:, : J // 2])
-        load_wd(raw_11, WD_COLS, 1)
-        pick_words(pairs_c[:, 1, :], 1, j_c)
+        nc.sync.dma_start(out=weights[0][:], in_=wgo[:, : J // 2])
+        load_wd(raw_10[1][:], WD_COLS + P, 0)
+        nc.sync.dma_start(out=weights[1][:], in_=wgo[:, J // 2 :])
+        pairs_b = pick_both("pairs_b", j_b, PAIRS_B)
+        late = look_up_scales([(j_c, 2 * CHUNK), (j_c, 2 * CHUNK)], "late", PICKED_REST)
+        planes_a = [columns(early[l], 0, CHUNK) for l in range(LISTS)]
+        planes_b = [columns(early[l], CHUNK, CHUNK) for l in range(LISTS)]
+        planes_c = [columns(late[l], 0, CHUNK) for l in range(LISTS)]
+        planes_d = [columns(late[l], CHUNK, CHUNK) for l in range(LISTS)]
+        words_b = part(pairs_b[:], "words_b")
+        pairs_c = pick_both("pairs_c", j_c, PAIRS_C)
+
         pairs_d = [sbuf([P, 1, CHUNK], U32, f"pairs_d{l}", offset) for l, offset in enumerate([PAIRS_D0, PAIRS_D])]
         pick_words(pairs_d[0][:, 0, :], 0, j_d)
         words_c = part(pairs_c[:], "words_c")
 
-        first_grouped = sbuf([P, PASSES, WD_COLS, 4], BF16, "first_grouped")
+        first_grouped = sbuf([P, PASSES, WD_COLS, 4], BF16, "first_grouped", FIRST_GROUPED)
         round_wd(nc.scalar.copy, raw_0[0][:], first_grouped[:, 0])
         round_wd(nc.vector.tensor_copy, raw_0[1][:], first_grouped[:, 1])
         grouped_a = hidden("a", words_a, planes_a, 0, PASS_0_FIRST, {}, H_ROWS[0], GROUPED_A, RAW_00)
@@ -337,10 +341,8 @@ def tile_list_msg_relu_bias_kernel(
         round_wd(nc.scalar.copy, raw_10[0][:], piece_0[:])
         pick_words(pairs_d[1][:, 0, :], 1, j_d)
         grouped_11 = sbuf([P, WD_COLS, 4], BF16, "grouped_11", GROUPED_11)
-        round_wd(nc.vector.tensor_copy, raw_11, grouped_11[:])
+        round_wd(nc.vector.tensor_copy, raw_11[:], grouped_11[:])
         words_d = words_d + part(pairs_d[1][:], "words_d1")
-        load_wd(raw_10[1][:], WD_COLS + P, 0)
-        nc.sync.dma_start(out=weights[1], in_=wgo[:, J // 2 :])
 
         def first_messages():
             send(0, j_a, [h_a], "y0")

@@ -43,23 +43,25 @@ PAIRS = 4 * CHUNK
 RAW = 4 * WD_COLS * 4
 ROWS = 2 * R
 PAGE = 4 * T
-PAIRS_B = 0
-PAIRS_A0 = PAIRS_B
-GROUPED_11 = PAIRS_B + 2 * PAIRS
+PAIRS_A0 = 0
+PICKED_B = PAIRS_A0
+PAGE_3 = PAIRS_A0 + PAIRS
+GROUPED_11 = PAGE_3 + PAGE - OVERLAP
 RAW_10 = GROUPED_11 + OVERLAP
-PAIRS_D = RAW_10 + RAW // 2 - OVERLAP
-PAIRS_A1 = PAIRS_D + 2 * PAIRS
-PICKED_REST = PAIRS_A1 + OVERLAP
-PAIRS_C = PICKED_REST + 5 * CHUNK
+PAIRS_D1 = RAW_10 + RAW // 2 - OVERLAP
+WORDS_C = PAIRS_D1 + PAIRS
+PAGE_2 = WORDS_C + 2 * PAIRS
+PAIRS_A1 = PAGE_2 + PAGE - OVERLAP
+PICKED_CD = PAIRS_A1 + OVERLAP
+PAIRS_C = PICKED_CD + PAIRS
 PAIRS_D0 = PAIRS_C + 2 * PAIRS
-PAGE_3 = PAIRS_D0 + PAIRS
-PAGE_2 = PAGE_3 + PAGE
-DIAGONAL = PAGE_2 - 2 * P
-H_ROWS = [PAGE_2 + PAGE + ROWS * k for k in range(4)]
+FIRST_GROUPED = PAIRS_D0 + PAIRS
+PAIRS_B = FIRST_GROUPED + PAIRS
+SPAN_A1 = 6
+H_ROWS = [FIRST_GROUPED + RAW + ROWS * k for k in range(4)]
 GROUPED_A = H_ROWS[-1] + ROWS
-RAW_00 = GROUPED_A + RAW
-WORDS_A0 = RAW_00 + RAW
-FIRST_GROUPED = WORDS_A0 + PAIRS
+FIRST_ROWS = GROUPED_A + RAW
+WORDS_A0 = FIRST_ROWS + ROWS
 
 
 def tile_list_msg_relu_bias_kernel(
@@ -121,9 +123,15 @@ def tile_list_msg_relu_bias_kernel(
         load_wt(0)
         load_w_scales(1, wt_scales)
         load_ws(1)
-        raw_0 = [sbuf([P, 4, WD_COLS], F32, f"raw_0{g}", offset) for g, offset in enumerate([RAW_00, None])]
-        load_wd(raw_0[0][:], 0, 0)
         load_wt(1)
+
+        distance = keep.tile([P, P], F32, name="distance")
+        squared = keep.tile([P, P], F32, name="squared")
+        nc.gpsimd.iota(
+            distance[:], pattern=[[1, P]], base=0, channel_multiplier=-1, allow_small_or_imprecise_dtypes=True
+        )
+        nc.scalar.activation(out=squared[:], in_=distance[:], func=ACT.Square)
+        nc.scalar.activation(out=ident[:], in_=squared[:], func=ACT.Relu, scale=-1.0, bias=1.0)
 
         def entries(l, j0, width):
             return lists[l][:, j0 // PER_COLUMN : (j0 + width) // PER_COLUMN]
@@ -156,7 +164,7 @@ def tile_list_msg_relu_bias_kernel(
         def quantise(codes, scales, grouped):
             nc.vector.quantize_mx(out=codes.bitcast(FP8X4), scales=scales, in_=grouped)
 
-        wd_codes = [sbuf([P, PASSES, WD_COLS], U32, f"wd_codes{half}", offset) for half, offset in enumerate([RAW_00, None])]
+        wd_codes = [sbuf([P, PASSES, WD_COLS], U32, f"wd_codes{half}") for half in range(2)]
         wd_scales = [sbuf([P, PASSES, WD_COLS], U8, f"wd_scales{half}") for half in range(2)]
 
         def turn(rows, grouped, col, bank_name):
@@ -261,28 +269,6 @@ def tile_list_msg_relu_bias_kernel(
 
         for c in range(2):
             clear_page(nc.vector)
-        blank = sbuf([P, P], F32, "blank", FIRST_GROUPED)
-        nc.vector.memset(blank[:], 0.0)
-        diagonal = sbuf([P, P], F32, "diagonal", DIAGONAL)
-        nc.gpsimd.affine_select(
-            out=diagonal[:],
-            in_=blank[:],
-            pattern=[[-1, P]],
-            compare_op=mybir.AluOpType.not_equal,
-            fill=1.0,
-            base=0,
-            channel_multiplier=1,
-        )
-        nc.scalar.activation(out=ident[:], in_=diagonal[:], func=ACT.Relu)
-        clear_page(nc.gpsimd, PAGE_2)
-
-        def look_up_scales(spans, name, offset=None):
-            picked = sbuf([P, sum(width for first, width in spans)], U8, f"picked_{name}", offset)
-            starts = [0, spans[0][1]]
-            for l, (first, width) in enumerate(spans):
-                pick_scales(picked[:, starts[l] : starts[l] + width], l, first)
-            both = scale_planes(picked, f"moved_{name}")
-            return [columns(both, starts[l], width) for l, (first, width) in enumerate(spans)]
 
         def pick_both(name, j0, offset):
             pairs = sbuf([P, LISTS, CHUNK], U32, name, offset)
@@ -290,17 +276,35 @@ def tile_list_msg_relu_bias_kernel(
                 pick_words(pairs[:, l, :], l, j0)
             return pairs
 
-        def part_each(pairs, name):
-            return [part(pairs[:, l : l + 1], f"{name}{l}")[0] for l in range(LISTS)]
+        def planes_of(picked, name):
+            width = picked.shape[1] // LISTS
+            both = scale_planes(picked, name)
+            return [columns(both, width * l, width) for l in range(LISTS)]
 
-        early = look_up_scales([(j_a, 2 * CHUNK), (j_a, 2 * CHUNK)], "early")
-        pairs_a = [sbuf([P, 1 + 4 * l, CHUNK], U32, f"pairs_a{l}", offset) for l, offset in enumerate([PAIRS_A0, PAIRS_A1])]
+        def pick_list(picked, l, j0):
+            width = picked.shape[1] // LISTS
+            pick_scales(picked[:, width * l : width * (l + 1)], l, j0)
+
+        picked_a = sbuf([P, LISTS * CHUNK], U8, "picked_a")
+        for l in range(LISTS):
+            pick_list(picked_a, l, j_a)
+        planes_a = planes_of(picked_a, "moved_a")
+        raw_0 = [sbuf([P, 4, WD_COLS], F32, f"raw_0{g}") for g in range(PASSES)]
+        for g in range(PASSES):
+            load_wd(raw_0[g][:], 0, g)
+        pairs_a = [
+            sbuf([P, span, CHUNK], U32, f"pairs_a{l}", offset)
+            for l, (span, offset) in enumerate([(1, PAIRS_A0), (SPAN_A1, PAIRS_A1)])
+        ]
         for l in range(LISTS):
             pick_words(pairs_a[l][:, 0, :], l, j_a)
         words_a = part(pairs_a[0][:], "words_a0", WORDS_A0) + part(pairs_a[1][:, 0:1], "words_a1")
-        clear_page(nc.gpsimd, PAGE_3)
-        load_wd(raw_0[1][:], 0, 1)
+        clear_page(nc.gpsimd, PAGE_2)
 
+        picked_b = sbuf([P, LISTS * CHUNK], U8, "picked_b", PICKED_B)
+        for l in range(LISTS):
+            pick_list(picked_b, l, j_b)
+        planes_b = planes_of(picked_b, "moved_b")
         raw_10 = [sbuf([P, 4, P], F32, f"raw_10{k}", offset) for k, offset in enumerate([RAW_10, None])]
         raw_11 = sbuf([P, 4, WD_COLS], F32, "raw_11")
         weights = [sbuf([P, J // 2], F32, f"weight{half}") for half in range(2)]
@@ -317,24 +321,27 @@ def tile_list_msg_relu_bias_kernel(
         nc.sync.dma_start(out=weights[0][:], in_=wgo[:, : J // 2])
         load_wd(raw_10[1][:], WD_COLS + P, 0)
         nc.sync.dma_start(out=weights[1][:], in_=wgo[:, J // 2 :])
+
         pairs_b = pick_both("pairs_b", j_b, PAIRS_B)
-        late = look_up_scales([(j_c, 2 * CHUNK), (j_c, 2 * CHUNK)], "late", PICKED_REST)
-        planes_a = [columns(early[l], 0, CHUNK) for l in range(LISTS)]
-        planes_b = [columns(early[l], CHUNK, CHUNK) for l in range(LISTS)]
-        planes_c = [columns(late[l], 0, CHUNK) for l in range(LISTS)]
-        planes_d = [columns(late[l], CHUNK, CHUNK) for l in range(LISTS)]
+        picked_cd = sbuf([P, LISTS * 2 * CHUNK], U8, "picked_cd", PICKED_CD)
+        pick_list(picked_cd, 0, j_c)
         words_b = part(pairs_b[:], "words_b")
-        pairs_c = pick_both("pairs_c", j_c, PAIRS_C)
-
-        pairs_d = [sbuf([P, 1, CHUNK], U32, f"pairs_d{l}", offset) for l, offset in enumerate([PAIRS_D0, PAIRS_D])]
-        pick_words(pairs_d[0][:, 0, :], 0, j_d)
-        words_c = part(pairs_c[:], "words_c")
-
         first_grouped = sbuf([P, PASSES, WD_COLS, 4], BF16, "first_grouped", FIRST_GROUPED)
-        round_wd(nc.scalar.copy, raw_0[0][:], first_grouped[:, 0])
-        round_wd(nc.vector.tensor_copy, raw_0[1][:], first_grouped[:, 1])
-        grouped_a = hidden("a", words_a, planes_a, 0, PASS_0_FIRST, {}, H_ROWS[0], GROUPED_A, RAW_00)
-        words_d = part(pairs_d[0][:], "words_d0", WORDS_A0)
+        for g in range(PASSES):
+            nc.gpsimd.tensor_scalar(
+                first_grouped[:, g], raw_0[g][:].rearrange("p t n -> p n t"), 1.0, 0.0, MULT, mybir.AluOpType.add
+            )
+        pick_list(picked_cd, 1, j_c)
+        planes_cd = planes_of(picked_cd, "moved_cd")
+        planes_c = [columns(planes, 0, CHUNK) for planes in planes_cd]
+        planes_d = [columns(planes, CHUNK, CHUNK) for planes in planes_cd]
+        pairs_c = pick_both("pairs_c", j_c, PAIRS_C)
+        pairs_d = [sbuf([P, 1, CHUNK], U32, f"pairs_d{l}", offset) for l, offset in enumerate([PAIRS_D0, PAIRS_D1])]
+        pick_words(pairs_d[0][:, 0, :], 0, j_d)
+
+        grouped_a = hidden("a", words_a, planes_a, 0, PASS_0_FIRST, {}, H_ROWS[0], GROUPED_A, FIRST_ROWS)
+        words_c = part(pairs_c[:], "words_c", WORDS_A0)
+        words_d = part(pairs_d[0][:], "words_d0", FIRST_ROWS)
         quantise_wd(0, first_grouped)
         h_a = quantise_h("a", grouped_a)
         piece_0 = sbuf([P, P, 4], BF16, "piece_0", H_ROWS[0])
@@ -344,13 +351,15 @@ def tile_list_msg_relu_bias_kernel(
         round_wd(nc.vector.tensor_copy, raw_11[:], grouped_11[:])
         words_d = words_d + part(pairs_d[1][:], "words_d1")
 
+        piece_1 = sbuf([P, P, 4], BF16, "piece_1", GROUPED_A)
+        round_wd(nc.scalar.copy, raw_10[1][:], piece_1[:])
+        for piece, g, first in [(piece_0, 0, 0), (piece_1, 0, P), (grouped_11, 1, 0)]:
+            cols = slice(first, first + piece.shape[1])
+            quantise(wd_codes[1][:, g, cols], wd_scales[1][:, g, cols], piece[:].rearrange("p n t -> p (n t)"))
+        clear_page(nc.gpsimd, PAGE_3)
+
         def first_messages():
             send(0, j_a, [h_a], "y0")
-            piece_1 = sbuf([P, P, 4], BF16, "piece_1", GROUPED_A)
-            round_wd(nc.scalar.copy, raw_10[1][:], piece_1[:])
-            for piece, g, first in [(piece_0, 0, 0), (piece_1, 0, P), (grouped_11, 1, 0)]:
-                cols = slice(first, first + piece.shape[1])
-                quantise(wd_codes[1][:, g, cols], wd_scales[1][:, g, cols], piece[:].rearrange("p n t -> p (n t)"))
             send(1, j_a, [h_a], "y1")
 
         def pair(first, j0, h, offset=None):

@@ -45,23 +45,20 @@ ROWS = 2 * R
 PAGE = 4 * T
 PAIRS_A0 = 0
 PICKED_B = PAIRS_A0
-PAGE_3 = PAIRS_A0 + PAIRS
-GROUPED_11 = PAGE_3 + PAGE - OVERLAP
+GROUPED_11 = PAIRS_A0 + PAIRS
 RAW_10 = GROUPED_11 + OVERLAP
 PAIRS_D1 = RAW_10 + RAW // 2 - OVERLAP
-WORDS_C = PAIRS_D1 + PAIRS
-PAGE_2 = WORDS_C + 2 * PAIRS
+PAGE_2 = PAIRS_D1 + PAIRS
 PAIRS_A1 = PAGE_2 + PAGE - OVERLAP
 PICKED_CD = PAIRS_A1 + OVERLAP
 PAIRS_C = PICKED_CD + PAIRS
 PAIRS_D0 = PAIRS_C + 2 * PAIRS
-FIRST_GROUPED = PAIRS_D0 + PAIRS
-PAIRS_B = FIRST_GROUPED + PAIRS
-SPAN_A1 = 6
-H_ROWS = [FIRST_GROUPED + RAW + ROWS * k for k in range(4)]
-GROUPED_A = H_ROWS[-1] + ROWS
-FIRST_ROWS = GROUPED_A + RAW
-WORDS_A0 = FIRST_ROWS + ROWS
+PAIRS_B = PAIRS_D0 + PAIRS
+SPAN_A1 = 5
+PAGE_3 = PAIRS_B + 2 * PAIRS - OVERLAP
+H_ROWS = [PAGE_3 + PAGE + ROWS * k for k in range(4)]
+FIRST_ROWS = H_ROWS[-1] + ROWS
+WORDS_A0 = FIRST_ROWS + RAW
 
 
 def tile_list_msg_relu_bias_kernel(
@@ -123,6 +120,8 @@ def tile_list_msg_relu_bias_kernel(
         load_wt(0)
         load_w_scales(1, wt_scales)
         load_ws(1)
+        raw_0 = [sbuf([P, 4, WD_COLS], F32, f"raw_0{g}", offset) for g, offset in enumerate([FIRST_ROWS, None])]
+        load_wd(raw_0[0][:], 0, 0)
         load_wt(1)
 
         distance = keep.tile([P, P], F32, name="distance")
@@ -164,7 +163,7 @@ def tile_list_msg_relu_bias_kernel(
         def quantise(codes, scales, grouped):
             nc.vector.quantize_mx(out=codes.bitcast(FP8X4), scales=scales, in_=grouped)
 
-        wd_codes = [sbuf([P, PASSES, WD_COLS], U32, f"wd_codes{half}") for half in range(2)]
+        wd_codes = {}
         wd_scales = [sbuf([P, PASSES, WD_COLS], U8, f"wd_scales{half}") for half in range(2)]
 
         def turn(rows, grouped, col, bank_name):
@@ -285,13 +284,12 @@ def tile_list_msg_relu_bias_kernel(
             width = picked.shape[1] // LISTS
             pick_scales(picked[:, width * l : width * (l + 1)], l, j0)
 
-        picked_a = sbuf([P, LISTS * CHUNK], U8, "picked_a")
-        for l in range(LISTS):
-            pick_list(picked_a, l, j_a)
-        planes_a = planes_of(picked_a, "moved_a")
-        raw_0 = [sbuf([P, 4, WD_COLS], F32, f"raw_0{g}") for g in range(PASSES)]
-        for g in range(PASSES):
-            load_wd(raw_0[g][:], 0, g)
+        picked_early = sbuf([P, 3 * CHUNK], U8, "picked_early")
+        pick_scales(picked_early[:, : 2 * CHUNK], 0, j_a)
+        pick_scales(picked_early[:, 2 * CHUNK :], 1, j_a)
+        early = scale_planes(picked_early, "moved_early")
+        planes_a = [columns(early, 0, CHUNK), columns(early, 2 * CHUNK, CHUNK)]
+        load_wd(raw_0[1][:], 0, 1)
         pairs_a = [
             sbuf([P, span, CHUNK], U32, f"pairs_a{l}", offset)
             for l, (span, offset) in enumerate([(1, PAIRS_A0), (SPAN_A1, PAIRS_A1)])
@@ -301,10 +299,9 @@ def tile_list_msg_relu_bias_kernel(
         words_a = part(pairs_a[0][:], "words_a0", WORDS_A0) + part(pairs_a[1][:, 0:1], "words_a1")
         clear_page(nc.gpsimd, PAGE_2)
 
-        picked_b = sbuf([P, LISTS * CHUNK], U8, "picked_b", PICKED_B)
-        for l in range(LISTS):
-            pick_list(picked_b, l, j_b)
-        planes_b = planes_of(picked_b, "moved_b")
+        picked_b = sbuf([P, CHUNK], U8, "picked_b", PICKED_B)
+        pick_scales(picked_b[:], 1, j_b)
+        planes_b = [columns(early, CHUNK, CHUNK), scale_planes(picked_b, "moved_b")]
         raw_10 = [sbuf([P, 4, P], F32, f"raw_10{k}", offset) for k, offset in enumerate([RAW_10, None])]
         raw_11 = sbuf([P, 4, WD_COLS], F32, "raw_11")
         weights = [sbuf([P, J // 2], F32, f"weight{half}") for half in range(2)]
@@ -326,11 +323,7 @@ def tile_list_msg_relu_bias_kernel(
         picked_cd = sbuf([P, LISTS * 2 * CHUNK], U8, "picked_cd", PICKED_CD)
         pick_list(picked_cd, 0, j_c)
         words_b = part(pairs_b[:], "words_b")
-        first_grouped = sbuf([P, PASSES, WD_COLS, 4], BF16, "first_grouped", FIRST_GROUPED)
-        for g in range(PASSES):
-            nc.gpsimd.tensor_scalar(
-                first_grouped[:, g], raw_0[g][:].rearrange("p t n -> p n t"), 1.0, 0.0, MULT, mybir.AluOpType.add
-            )
+        clear_page(nc.gpsimd, PAGE_3)
         pick_list(picked_cd, 1, j_c)
         planes_cd = planes_of(picked_cd, "moved_cd")
         planes_c = [columns(planes, 0, CHUNK) for planes in planes_cd]
@@ -339,24 +332,26 @@ def tile_list_msg_relu_bias_kernel(
         pairs_d = [sbuf([P, 1, CHUNK], U32, f"pairs_d{l}", offset) for l, offset in enumerate([PAIRS_D0, PAIRS_D1])]
         pick_words(pairs_d[0][:, 0, :], 0, j_d)
 
-        grouped_a = hidden("a", words_a, planes_a, 0, PASS_0_FIRST, {}, H_ROWS[0], GROUPED_A, FIRST_ROWS)
+        first_grouped = sbuf([P, PASSES, WD_COLS, 4], BF16, "first_grouped")
+        round_wd(nc.scalar.copy, raw_0[0][:], first_grouped[:, 0])
+        round_wd(nc.vector.tensor_copy, raw_0[1][:], first_grouped[:, 1])
+        grouped_a = hidden("a", words_a, planes_a, 0, PASS_0_FIRST, {}, H_ROWS[0], None, FIRST_ROWS)
         words_c = part(pairs_c[:], "words_c", WORDS_A0)
         words_d = part(pairs_d[0][:], "words_d0", FIRST_ROWS)
+        wd_codes[0] = sbuf([P, PASSES, WD_COLS], U32, "wd_codes0", FIRST_ROWS + PAIRS)
+        wd_codes[1] = sbuf([P, PASSES, WD_COLS], U32, "wd_codes1")
         quantise_wd(0, first_grouped)
         h_a = quantise_h("a", grouped_a)
-        piece_0 = sbuf([P, P, 4], BF16, "piece_0", H_ROWS[0])
-        round_wd(nc.scalar.copy, raw_10[0][:], piece_0[:])
+        grouped_10 = sbuf([P, WD_COLS, 4], BF16, "grouped_10", H_ROWS[0])
+        for k in range(2):
+            round_wd(nc.scalar.copy, raw_10[k][:], grouped_10[:, k * P : (k + 1) * P])
         pick_words(pairs_d[1][:, 0, :], 1, j_d)
         grouped_11 = sbuf([P, WD_COLS, 4], BF16, "grouped_11", GROUPED_11)
         round_wd(nc.vector.tensor_copy, raw_11[:], grouped_11[:])
         words_d = words_d + part(pairs_d[1][:], "words_d1")
 
-        piece_1 = sbuf([P, P, 4], BF16, "piece_1", GROUPED_A)
-        round_wd(nc.scalar.copy, raw_10[1][:], piece_1[:])
-        for piece, g, first in [(piece_0, 0, 0), (piece_1, 0, P), (grouped_11, 1, 0)]:
-            cols = slice(first, first + piece.shape[1])
-            quantise(wd_codes[1][:, g, cols], wd_scales[1][:, g, cols], piece[:].rearrange("p n t -> p (n t)"))
-        clear_page(nc.gpsimd, PAGE_3)
+        for g, grouped in enumerate([grouped_10, grouped_11]):
+            quantise(wd_codes[1][:, g, :], wd_scales[1][:, g, :], grouped[:].rearrange("p n t -> p (n t)"))
 
         def first_messages():
             send(0, j_a, [h_a], "y0")
@@ -366,12 +361,12 @@ def tile_list_msg_relu_bias_kernel(
             for k in range(2):
                 send(first + k, j0, [h], f"y{k}", None if offset is None else offset + k * PAIRS)
 
-        h_b = quantise_h("b", hidden("b", words_b, planes_b, 0, LATE_PLANE, {(0, 1): first_messages}, H_ROWS[1]))
+        h_b = quantise_h("b", hidden("b", words_b, planes_b, 0, LATE_PLANE, {(1, 0): first_messages}, H_ROWS[1]))
         pair(2, j_a, h_a, H_ROWS[1])
-        among_c = {(0, 1): lambda: pair(0, j_b, h_b)}
+        among_c = {(1, 0): lambda: pair(0, j_b, h_b)}
         h_c = quantise_h("c", hidden("c", words_c, planes_c, 0, BY_BANK, among_c, H_ROWS[2]))
         pair(2, j_b, h_b, H_ROWS[2])
-        among_d = {(0, 1): lambda: pair(0, j_c, h_c)}
+        among_d = {(1, 0): lambda: pair(0, j_c, h_c)}
         h_d = quantise_h("d", hidden("d", words_d, planes_d, 0, BY_BANK, among_d, H_ROWS[3]))
         send(2, j_c, [h_c], "y0", H_ROWS[3])
         for c, bank_name in enumerate(["y1", "acc0", "acc1"]):

@@ -47,14 +47,14 @@ PAIRS_A0 = 0
 PICKED_B = PAIRS_A0
 GROUPED_11 = PAIRS_A0 + PAIRS
 RAW_10 = GROUPED_11 + OVERLAP
-PAIRS_D1 = RAW_10 + RAW // 2 - OVERLAP
-PAGE_2 = PAIRS_D1 + PAIRS
+WORDS_D = RAW_10 + RAW // 2 - OVERLAP
+PAGE_2 = WORDS_D + 2 * PAIRS
 PAIRS_A1 = PAGE_2 + PAGE - OVERLAP
 PICKED_CD = PAIRS_A1 + OVERLAP
 PAIRS_C = PICKED_CD + PAIRS
-PAIRS_D0 = PAIRS_C + 2 * PAIRS
-PAIRS_B = PAIRS_D0 + PAIRS
-SPAN_A1 = 5
+PAIRS_D = PAIRS_C + 2 * PAIRS
+PAIRS_B = PAIRS_D + 2 * PAIRS
+SPAN_A1 = 6
 PAGE_3 = PAIRS_B + 2 * PAIRS - OVERLAP
 H_ROWS = [PAGE_3 + PAGE + ROWS * k for k in range(4)]
 FIRST_ROWS = H_ROWS[-1] + ROWS
@@ -329,26 +329,23 @@ def tile_list_msg_relu_bias_kernel(
         planes_c = [columns(planes, 0, CHUNK) for planes in planes_cd]
         planes_d = [columns(planes, CHUNK, CHUNK) for planes in planes_cd]
         pairs_c = pick_both("pairs_c", j_c, PAIRS_C)
-        pairs_d = [sbuf([P, 1, CHUNK], U32, f"pairs_d{l}", offset) for l, offset in enumerate([PAIRS_D0, PAIRS_D1])]
-        pick_words(pairs_d[0][:, 0, :], 0, j_d)
+        pairs_d = pick_both("pairs_d", j_d, PAIRS_D)
 
         first_grouped = sbuf([P, PASSES, WD_COLS, 4], BF16, "first_grouped")
         round_wd(nc.scalar.copy, raw_0[0][:], first_grouped[:, 0])
         round_wd(nc.vector.tensor_copy, raw_0[1][:], first_grouped[:, 1])
         grouped_a = hidden("a", words_a, planes_a, 0, PASS_0_FIRST, {}, H_ROWS[0], None, FIRST_ROWS)
         words_c = part(pairs_c[:], "words_c", WORDS_A0)
-        words_d = part(pairs_d[0][:], "words_d0", FIRST_ROWS)
-        wd_codes[0] = sbuf([P, PASSES, WD_COLS], U32, "wd_codes0", FIRST_ROWS + PAIRS)
+        wd_codes[0] = sbuf([P, PASSES, WD_COLS], U32, "wd_codes0", FIRST_ROWS)
         wd_codes[1] = sbuf([P, PASSES, WD_COLS], U32, "wd_codes1")
         quantise_wd(0, first_grouped)
         h_a = quantise_h("a", grouped_a)
         grouped_10 = sbuf([P, WD_COLS, 4], BF16, "grouped_10", H_ROWS[0])
         for k in range(2):
             round_wd(nc.scalar.copy, raw_10[k][:], grouped_10[:, k * P : (k + 1) * P])
-        pick_words(pairs_d[1][:, 0, :], 1, j_d)
         grouped_11 = sbuf([P, WD_COLS, 4], BF16, "grouped_11", GROUPED_11)
         round_wd(nc.vector.tensor_copy, raw_11[:], grouped_11[:])
-        words_d = words_d + part(pairs_d[1][:], "words_d1")
+        words_d = part(pairs_d[:], "words_d", WORDS_D)
 
         for g, grouped in enumerate([grouped_10, grouped_11]):
             quantise(wd_codes[1][:, g, :], wd_scales[1][:, g, :], grouped[:].rearrange("p n t -> p (n t)"))
@@ -361,7 +358,7 @@ def tile_list_msg_relu_bias_kernel(
             for k in range(2):
                 send(first + k, j0, [h], f"y{k}", None if offset is None else offset + k * PAIRS)
 
-        h_b = quantise_h("b", hidden("b", words_b, planes_b, 0, LATE_PLANE, {(1, 0): first_messages}, H_ROWS[1]))
+        h_b = quantise_h("b", hidden("b", words_b, planes_b, 0, LATE_PLANE, {(0, 1): first_messages}, H_ROWS[1]))
         pair(2, j_a, h_a, H_ROWS[1])
         among_c = {(1, 0): lambda: pair(0, j_b, h_b)}
         h_c = quantise_h("c", hidden("c", words_c, planes_c, 0, BY_BANK, among_c, H_ROWS[2]))

@@ -43,20 +43,19 @@ PAIRS = 4 * CHUNK
 RAW = 4 * WD_COLS * 4
 ROWS = 2 * R
 PAGE = 4 * T
-PAIRS_A0 = 0
-PICKED_B = PAIRS_A0
-GROUPED_11 = PAIRS_A0 + PAIRS
+PAGE_2 = 0
+PAIRS_A0 = PAGE_2 + PAGE - OVERLAP
+PICKED_B = PAIRS_A0 + OVERLAP
+PAIRS_D = PAIRS_A0 + PAIRS - OVERLAP
+PICKED_CD = PAIRS_D + 2 * PAIRS
+PAIRS_A1 = PICKED_CD + 2 * OVERLAP
+PAIRS_C = PICKED_CD + PAIRS
+PAIRS_B = PAIRS_C + OVERLAP
+PAGE_3 = PAIRS_C + 2 * PAIRS
+GROUPED_11 = PAGE_3 + PAGE
 RAW_10 = GROUPED_11 + OVERLAP
 WORDS_D = RAW_10 + RAW // 2 - OVERLAP
-PAGE_2 = WORDS_D + 2 * PAIRS
-PAIRS_A1 = PAGE_2 + PAGE - OVERLAP
-PICKED_CD = PAIRS_A1 + OVERLAP
-PAIRS_C = PICKED_CD + PAIRS
-PAIRS_D = PAIRS_C + 2 * PAIRS
-PAIRS_B = PAIRS_D + 2 * PAIRS
-SPAN_A1 = 6
-PAGE_3 = PAIRS_B + 2 * PAIRS - OVERLAP
-H_ROWS = [PAGE_3 + PAGE + ROWS * k for k in range(4)]
+H_ROWS = [WORDS_D + 2 * PAIRS + ROWS * k for k in range(4)]
 FIRST_ROWS = H_ROWS[-1] + ROWS
 WORDS_A0 = FIRST_ROWS + RAW
 
@@ -290,13 +289,10 @@ def tile_list_msg_relu_bias_kernel(
         early = scale_planes(picked_early, "moved_early")
         planes_a = [columns(early, 0, CHUNK), columns(early, 2 * CHUNK, CHUNK)]
         load_wd(raw_0[1][:], 0, 1)
-        pairs_a = [
-            sbuf([P, span, CHUNK], U32, f"pairs_a{l}", offset)
-            for l, (span, offset) in enumerate([(1, PAIRS_A0), (SPAN_A1, PAIRS_A1)])
-        ]
+        pairs_a = [sbuf([P, 1, CHUNK], U32, f"pairs_a{l}", offset) for l, offset in enumerate([PAIRS_A0, PAIRS_A1])]
         for l in range(LISTS):
             pick_words(pairs_a[l][:, 0, :], l, j_a)
-        words_a = part(pairs_a[0][:], "words_a0", WORDS_A0) + part(pairs_a[1][:, 0:1], "words_a1")
+        words_a = part(pairs_a[0][:], "words_a0", WORDS_A0) + part(pairs_a[1][:], "words_a1")
         clear_page(nc.gpsimd, PAGE_2)
 
         picked_b = sbuf([P, CHUNK], U8, "picked_b", PICKED_B)

from contextlib import ExitStack

import concourse.mybir as mybir

K, R, N, T, J = 1024, 1024, 512, 2048, 1024
FLOPS = 2 * 2 * K * R * J + 2 * R * N * J

F32 = mybir.dt.float32
BF16 = mybir.dt.bfloat16
I32 = mybir.dt.int32
U32 = mybir.dt.uint32
U16 = mybir.dt.uint16
U8 = mybir.dt.uint8
FP8X4 = mybir.dt.float8_e4m3fn_x4
FP4X4 = mybir.dt.float4_e2m1fn_x4
ACT = mybir.ActivationFunctionType
MULT = mybir.AluOpType.mult

P = 128
PASS_ROWS = 512
PASSES = 2
LISTS = 2
PER_COLUMN = 16
BANK = 512
CHUNK = 256
WD_COLS = 256
PAGES = N // P
BLOCKS = CHUNK // P

BANKS = [(block, g) for block in range(BLOCKS) for g in range(PASSES)]
BY_BANK = [(block, g, l, a) for block, g in BANKS for a in range(PASSES) for l in range(LISTS)]
PASS_0_FIRST = [(block, g, l, 0) for l in range(LISTS) for block, g in BANKS] + [
    (block, g, l, 1) for block, g in BANKS for l in range(LISTS)
]
LATE_PLANE = [(0, g, l, a) for a in range(PASSES) for g in range(PASSES) for l in range(LISTS)] + BY_BANK[8:]

PASS_1_ROW = 16
MOVED_ROWS = 100
TAB_FIRST = T // 4

OVERLAP = 64
PAIRS = 4 * CHUNK
RAW = 4 * WD_COLS * 4
ROWS = 2 * R
PAGE = 4 * T
PAGE_2 = 0
PAIRS_A0 = PAGE_2 + PAGE - OVERLAP
PICKED_B = PAIRS_A0 + OVERLAP
PAIRS_D = PAIRS_A0 + PAIRS - OVERLAP
PICKED_CD = PAIRS_D + 2 * PAIRS
PAIRS_A1 = PICKED_CD + 2 * OVERLAP
PAIRS_C = PICKED_CD + PAIRS
PAIRS_B = PAIRS_C + OVERLAP
PAGE_3 = PAIRS_C + 2 * PAIRS
GROUPED_11 = PAGE_3 + PAGE
RAW_10 = GROUPED_11 + OVERLAP
WORDS_D = RAW_10 + RAW // 2 - OVERLAP
H_ROWS = [WORDS_D + 2 * PAIRS + ROWS * k for k in range(4)]
FIRST_ROWS = H_ROWS[-1] + ROWS
WORDS_A0 = FIRST_ROWS + RAW


def tile_list_msg_relu_bias_kernel(
    tc, tab_words, tab_scales, ws_words, ws_scales, wt_words, wt_scales, wd, b, wgo, offs, offs2, out
):
    nc = tc.nc
    with ExitStack() as ctx:
        keep = ctx.enter_context(tc.tile_pool(name="keep", bufs=1))
        stage = ctx.enter_context(tc.tile_pool(name="stage", bufs=1))
        psum = ctx.enter_context(tc.psum_pool(name="psum", bufs=1))

        def sbuf(shape, dtype, name, offset=None):
            if offset is None:
                return keep.tile(shape, dtype, name=name, align_bytes=64)
            return stage.tile(shape, dtype, name=name, offset=offset, align_bytes=64)

        lists = [keep.tile([P, J // PER_COLUMN], U16, name=f"list{l}") for l in range(LISTS)]
        tab_s = sbuf([P, T], U8, "tab_s")
        tab_w = sbuf([P, T], U32, "tab_w")
        w_s = [sbuf([P, PASSES, R], U8, f"w_s{l}") for l in range(LISTS)]
        ws_w = [sbuf([P, 2 * R], U8, f"ws_w{a}") for a in range(PASSES)]
        wt_w = [sbuf([P, 4 * R], U8, f"wt_w{a}") for a in range(PASSES)]
        ident = keep.tile([P, P], F32, name="ident")

        nc.vector.memset(tab_s[:].bitcast(I32), 0)

        def load_w_scales(l, scales):
            for s in range(4):
                nc.sync.dma_start(
                    out=w_s[l][s:P:32].bitcast(I32),
                    in_=scales[:, s:16:4, :].rearrange("a q r -> q a r").bitcast(I32),
                )

        def load_tab_words(first, last):
            source = tab_words[0, :, first:last, :].rearrange("p t b -> p (t b)")
            nc.sync.dma_start(out=tab_w[:, first:last].bitcast(I32), in_=source.bitcast(I32))

        def load_ws(a):
            nc.sync.dma_start(out=ws_w[a][:].bitcast(I32), in_=ws_words[a].bitcast(I32))

        def load_wt(a):
            nc.sync.dma_start(out=wt_w[a][:].bitcast(I32), in_=wt_words[a].rearrange("p r i -> p (r i)").bitcast(I32))

        def load_wd(raw, first, g):
            source = wd[PASS_ROWS * g : PASS_ROWS * (g + 1), first : first + raw.shape[2]]
            nc.sync.dma_start(out=raw, in_=source.rearrange("(p t) n -> p t n", t=4))

        load_tab_words(0, TAB_FIRST)
        nc.sync.dma_start(lists[0][:], offs)
        nc.sync.dma_start(lists[1][:], offs2)
        for s in range(4):
            nc.sync.dma_start(
                out=tab_s[s:P:PASS_1_ROW, :].bitcast(I32),
                in_=tab_scales[:, s:16:4, :].rearrange("a q t -> q a t").bitcast(I32),
            )
        load_tab_words(TAB_FIRST, T)
        load_ws(0)
        load_w_scales(0, ws_scales)
        load_wt(0)
        load_w_scales(1, wt_scales)
        load_ws(1)
        raw_0 = [sbuf([P, 4, WD_COLS], F32, f"raw_0{g}", offset) for g, offset in enumerate([FIRST_ROWS, None])]
        load_wd(raw_0[0][:], 0, 0)
        load_wt(1)

        distance = keep.tile([P, P], F32, name="distance")
        squared = keep.tile([P, P], F32, name="squared")
        nc.gpsimd.iota(
            distance[:], pattern=[[1, P]], base=0, channel_multiplier=-1, allow_small_or_imprecise_dtypes=True
        )
        nc.scalar.activation(out=squared[:], in_=distance[:], func=ACT.Square)
        nc.scalar.activation(out=ident[:], in_=squared[:], func=ACT.Relu, scale=-1.0, bias=1.0)

        def entries(l, j0, width):
            return lists[l][:, j0 // PER_COLUMN : (j0 + width) // PER_COLUMN]

        def pick_words(pairs, l, j0):
            nc.vector.tensor_copy(pairs, tab_w[:].indirect(entries(l, j0, pairs.shape[1])))

        def part(pairs, name, offset=None):
            count, width = pairs.shape[1:]
            words = sbuf([P, count, PASSES, 2 * width], U8, name, offset)
            nc.vector.tensor_copy(
                out=words[:].bitcast(U16), in_=pairs.bitcast(U16).rearrange("p l (j a) -> p l a j", a=PASSES)
            )
            return [words[:, l] for l in range(count)]

        def pick_scales(picked, l, j0):
            nc.vector.tensor_copy(picked, tab_s[:].indirect(entries(l, j0, picked.shape[1])))

        def scale_planes(picked, name):
            moved = sbuf(list(picked.shape), U8, name)
            nc.sync.dma_start(out=moved[0:MOVED_ROWS].bitcast(I32), in_=picked[PASS_1_ROW : PASS_1_ROW + MOVED_ROWS].bitcast(I32))
            return [picked[:], moved[:]]

        def columns(planes, first, width):
            return [plane[:, first : first + width] for plane in planes]

        def round_wd(copy, raw, grouped):
            copy(out=grouped.rearrange("p (c i) t -> p c t i", i=4), in_=raw.rearrange("p t (c i) -> p c t i", i=4))

        def quantise(codes, scales, grouped):
            nc.vector.quantize_mx(out=codes.bitcast(FP8X4), scales=scales, in_=grouped)

        wd_codes = {}
        wd_scales = [sbuf([P, PASSES, WD_COLS], U8, f"wd_scales{half}") for half in range(2)]

        def turn(rows, grouped, col, bank_name):
            h_pairs = rows[:].rearrange("p g u m e -> p (g u m e)").bitcast(F32)
            turned = psum.tile([P, PASSES, 2, P], F32, name=bank_name)
            for g in range(PASSES):
                for u in range(2):
                    w0 = (2 * g + u) * P
                    nc.tensor.transpose(turned[:, g, u, :], h_pairs[:, w0 : w0 + P], ident[:])
            nc.scalar.copy(
                out=grouped[:].bitcast(F32)[:, :, col : col + P, :],
                in_=turned[:].rearrange("p g u j -> p g j u"),
            )

        def hidden(name, words, planes, col, order, between, last_rows, offset=None, first_rows=None):
            grouped = sbuf([P, PASSES, CHUNK, 4], BF16, f"h_grouped_{name}", offset)
            banks = {bank: psum.tile([P, BANK], F32, name=f"acc{k}") for k, bank in enumerate(BANKS)}
            rows = [
                sbuf([P, PASSES, 2, P, 2], BF16, f"h_rows_{name}{block}", offset)
                for block, offset in enumerate([first_rows, last_rows])
            ]
            for block, g, l, a in order:
                c0 = P * block
                if l == 0:
                    w_words = ws_w[a][:, 2 * BANK * g : 2 * BANK * (g + 1)].bitcast(FP4X4)
                else:
                    w_words = wt_w[a][:, 4 * BANK * g : 4 * BANK * (g + 1)].bitcast(FP8X4)
                last = (l, a) == (LISTS - 1, PASSES - 1)
                nc.tensor.matmul_mx(
                    out=banks[block, g][:],
                    lhsT=words[l][:, a, 2 * c0 : 2 * (c0 + P)].bitcast(FP4X4),
                    lhsT_scale=planes[l][a][:, col + c0 : col + c0 + P],
                    rhs=w_words,
                    rhs_scale=w_s[l][:, a, BANK * g : BANK * (g + 1)],
                    start=(l, a) == (0, 0),
                    stop=last,
                )
                if last:
                    nc.scalar.activation(
                        out=rows[block][:, g],
                        in_=banks[block, g][:].rearrange("p (m u e) -> p u m e", u=2, e=2),
                        func=ACT.Relu,
                    )
                    if (block, g) in between:
                        between[block, g]()
            for block in range(BLOCKS):
                turn(rows[block], grouped, P * block, f"turned{block}")
            return grouped

        def quantise_h(name, grouped):
            codes = sbuf([P, PASSES, CHUNK], U32, f"h_codes_{name}")
            scales = sbuf([P, PASSES, CHUNK], U8, f"h_scales_{name}")
            quantise(
                codes[:].rearrange("p g j -> p (g j)"),
                scales[:].rearrange("p g j -> p (g j)"),
                grouped[:].rearrange("p g j t -> p (g j t)"),
            )
            return codes, scales

        def quantise_wd(half, grouped):
            quantise(
                wd_codes[half][:].rearrange("p g n -> p (g n)"),
                wd_scales[half][:].rearrange("p g n -> p (g n)"),
                grouped[:].rearrange("p g n t -> p (g n t)"),
            )

        def product(c, chunks, bank_name):
            bank = psum.tile([P, CHUNK * len(chunks)], F32, name=bank_name)
            half, n0 = divmod(c * P, WD_COLS)
            for s, (codes, scales) in enumerate(chunks):
                for g in range(PASSES):
                    nc.tensor.matmul_mx(
                        out=bank[:, s * CHUNK : (s + 1) * CHUNK],
                        lhsT=wd_codes[half][:, g, n0 : n0 + P].bitcast(FP8X4),
                        lhsT_scale=wd_scales[half][:, g, n0 : n0 + P],
                        rhs=codes[:, g, :].bitcast(FP8X4),
                        rhs_scale=scales[:, g, :],
                        start=(g == 0),
                        stop=(g == PASSES - 1),
                    )
            return bank

        def send(c, j0, chunks, bank_name, offset=None):
            bank = product(c, chunks, bank_name)
            width = bank.shape[1]
            biased = sbuf([P, width], F32, f"biased{c}_{j0}", offset)
            nc.scalar.activation(out=biased[:], in_=bank[:], func=ACT.Identity, bias=bias[:, c : c + 1], scale=1.0)
            nc.vector.tensor_tensor(
                pages[c][:].indirect(entries(1, j0, width)), biased[:], weight(j0, width), MULT
            )

        def store(c):
            nc.sync.dma_start(out=out[c * P : (c + 1) * P, :], in_=pages[c][:])

        j_a, j_b, j_c, j_d = range(0, J, CHUNK)
        pages = []

        def clear_page(engine, offset=None):
            page = sbuf([P, T], F32, f"page{len(pages)}", offset)
            engine.memset(page[:].bitcast(I32), 0)
            pages.append(page)

        for c in range(2):
            clear_page(nc.vector)

        def pick_both(name, j0, offset):
            pairs = sbuf([P, LISTS, CHUNK], U32, name, offset)
            for l in range(LISTS):
                pick_words(pairs[:, l, :], l, j0)
            return pairs

        def planes_of(picked, name):
            width = picked.shape[1] // LISTS
            both = scale_planes(picked, name)
            return [columns(both, width * l, width) for l in range(LISTS)]

        def pick_list(picked, l, j0):
            width = picked.shape[1] // LISTS
            pick_scales(picked[:, width * l : width * (l + 1)], l, j0)

        picked_early = sbuf([P, 3 * CHUNK], U8, "picked_early")
        pick_scales(picked_early[:, : 2 * CHUNK], 0, j_a)
        pick_scales(picked_early[:, 2 * CHUNK :], 1, j_a)
        early = scale_planes(picked_early, "moved_early")
        planes_a = [columns(early, 0, CHUNK), columns(early, 2 * CHUNK, CHUNK)]
        load_wd(raw_0[1][:], 0, 1)
        pairs_a = [sbuf([P, 1, CHUNK], U32, f"pairs_a{l}", offset) for l, offset in enumerate([PAIRS_A0, PAIRS_A1])]
        for l in range(LISTS):
            pick_words(pairs_a[l][:, 0, :], l, j_a)
        words_a = part(pairs_a[0][:], "words_a0", WORDS_A0) + part(pairs_a[1][:], "words_a1")
        clear_page(nc.gpsimd, PAGE_2)

        picked_b = sbuf([P, CHUNK], U8, "picked_b", PICKED_B)
        pick_scales(picked_b[:], 1, j_b)
        planes_b = [columns(early, CHUNK, CHUNK), scale_planes(picked_b, "moved_b")]
        raw_10 = [sbuf([P, 4, P], F32, f"raw_10{k}", offset) for k, offset in enumerate([RAW_10, None])]
        raw_11 = sbuf([P, 4, WD_COLS], F32, "raw_11")
        weights = [sbuf([P, J // 2], F32, f"weight{half}") for half in range(2)]

        def weight(j0, width):
            half, first = divmod(j0, J // 2)
            return weights[half][:, first : first + width]

        load_wd(raw_10[0][:], WD_COLS, 0)
        load_wd(raw_11[:], WD_COLS, 1)
        bias = sbuf([P, PAGES], F32, "bias")
        with nc.allow_non_contiguous_dma(reason="one bias value a partition and page"):
            nc.sync.dma_start(out=bias[:], in_=b.rearrange("(c p) -> p c", p=P))
        nc.sync.dma_start(out=weights[0][:], in_=wgo[:, : J // 2])
        load_wd(raw_10[1][:], WD_COLS + P, 0)
        nc.sync.dma_start(out=weights[1][:], in_=wgo[:, J // 2 :])

        pairs_b = pick_both("pairs_b", j_b, PAIRS_B)
        picked_cd = sbuf([P, LISTS * 2 * CHUNK], U8, "picked_cd", PICKED_CD)
        pick_list(picked_cd, 0, j_c)
        words_b = part(pairs_b[:], "words_b")
        clear_page(nc.gpsimd, PAGE_3)
        pick_list(picked_cd, 1, j_c)
        planes_cd = planes_of(picked_cd, "moved_cd")
        planes_c = [columns(planes, 0, CHUNK) for planes in planes_cd]
        planes_d = [columns(planes, CHUNK, CHUNK) for planes in planes_cd]
        pairs_c = pick_both("pairs_c", j_c, PAIRS_C)
        pairs_d = pick_both("pairs_d", j_d, PAIRS_D)

        first_grouped = sbuf([P, PASSES, WD_COLS, 4], BF16, "first_grouped")
        round_wd(nc.scalar.copy, raw_0[0][:], first_grouped[:, 0])
        round_wd(nc.vector.tensor_copy, raw_0[1][:], first_grouped[:, 1])
        grouped_a = hidden("a", words_a, planes_a, 0, PASS_0_FIRST, {}, H_ROWS[0], None, FIRST_ROWS)
        words_c = part(pairs_c[:], "words_c", WORDS_A0)
        wd_codes[0] = sbuf([P, PASSES, WD_COLS], U32, "wd_codes0", FIRST_ROWS)
        wd_codes[1] = sbuf([P, PASSES, WD_COLS], U32, "wd_codes1")
        quantise_wd(0, first_grouped)
        h_a = quantise_h("a", grouped_a)
        grouped_10 = sbuf([P, WD_COLS, 4], BF16, "grouped_10", H_ROWS[0])
        for k in range(2):
            round_wd(nc.scalar.copy, raw_10[k][:], grouped_10[:, k * P : (k + 1) * P])
        grouped_11 = sbuf([P, WD_COLS, 4], BF16, "grouped_11", GROUPED_11)
        round_wd(nc.vector.tensor_copy, raw_11[:], grouped_11[:])
        words_d = part(pairs_d[:], "words_d", WORDS_D)

        for g, grouped in enumerate([grouped_10, grouped_11]):
            quantise(wd_codes[1][:, g, :], wd_scales[1][:, g, :], grouped[:].rearrange("p n t -> p (n t)"))

        def first_messages():
            send(0, j_a, [h_a], "y0")
            send(1, j_a, [h_a], "y1")

        def pair(first, j0, h, offset=None):
            for k in range(2):
                send(first + k, j0, [h], f"y{k}", None if offset is None else offset + k * PAIRS)

        h_b = quantise_h("b", hidden("b", words_b, planes_b, 0, LATE_PLANE, {(0, 1): first_messages}, H_ROWS[1]))
        pair(2, j_a, h_a, H_ROWS[1])
        among_c = {(1, 0): lambda: pair(0, j_b, h_b)}
        h_c = quantise_h("c", hidden("c", words_c, planes_c, 0, BY_BANK, among_c, H_ROWS[2]))
        pair(2, j_b, h_b, H_ROWS[2])
        among_d = {(1, 0): lambda: pair(0, j_c, h_c)}
        h_d = quantise_h("d", hidden("d", words_d, planes_d, 0, BY_BANK, among_d, H_ROWS[3]))
        send(2, j_c, [h_c], "y0", H_ROWS[3])
        for c, bank_name in enumerate(["y1", "acc0", "acc1"]):
            send(c, j_d, [h_d], bank_name)
            store(c)
        send(3, j_c, [h_c, h_d], "acc2")
        store(3)
